import numpy as np
import ml_dtypes


def mxq(x, axis, fmt="e4m3"):
    dtype, down = {"e4m3": (ml_dtypes.float8_e4m3fn, 7), "e5m2": (ml_dtypes.float8_e5m2, 14)}[fmt]
    v = np.moveaxis(np.asarray(x, np.float32).astype(ml_dtypes.bfloat16).astype(np.float64), axis, -1)
    blocks = v.reshape(v.shape[:-1] + (-1, 32))
    amax = np.abs(blocks).max(-1, keepdims=True)
    byte = np.maximum(np.where(amax > 0, np.frexp(amax)[1] - 1 + 127, 0) - down, 1)
    scale = np.exp2(byte - 127.0)
    codes = (blocks / scale).astype(np.float32).astype(dtype).astype(np.float64)
    return np.moveaxis((codes * scale).reshape(v.shape), -1, axis)


WIDE = False


def mx_kscale(k):
    if not WIDE:
        return np.ones(k)
    levels = np.array([10, -10, 5, -5, 0])
    if k % 512:
        return np.exp2(np.random.permutation(np.resize(levels, k // 32))).repeat(32)
    a = np.empty((k // 512, 16))
    for p in range(k // 512):
        a[p, :8] = np.random.permutation(np.resize(levels, 8))
        for g in range(8):
            far = levels[np.abs(levels - a[p, g]) >= 10]
            a[p, g + 8] = far[np.random.randint(len(far))]
    return np.exp2(a.ravel()).repeat(32)


def f64(x):
    return np.asarray(x).astype(np.float64)


def striped(idx):
    return np.tile(idx.reshape(-1, 16).T, (8, 1)).astype(np.uint16)


def unstriped(offs):
    return offs[:16].T.reshape(-1).astype(np.int64)


E2M1 = np.array([0.0, 0.5, 1.0, 1.5, 2.0, 3.0, 4.0, 6.0, -0.0, -0.5, -1.0, -1.5, -2.0, -3.0, -4.0, -6.0])


def pack_weight(w, fmt):
    k, n = w.shape
    w = f64(np.asarray(w, np.float32).astype(ml_dtypes.bfloat16)).reshape(k // 32, 32, n)
    amax = np.abs(w).max(1)
    if fmt == "e4m3":
        byte = np.frexp(amax)[1] - 1 + 127 - 7
    else:
        mant, ex = np.frexp(amax / 6.0)
        byte = np.where(mant > 0.5, ex, ex - 1) + 127
    byte = np.clip(np.where(amax > 0, byte, 1), 1, 254)
    scaled = (w * np.exp2(127.0 - byte)[:, None, :]).reshape(k, n).astype(np.float32)
    by_word = np.ascontiguousarray(scaled.reshape(k // 512, 128, 4, n).transpose(0, 1, 3, 2))
    if fmt == "e4m3":
        words = by_word.astype(ml_dtypes.float8_e4m3fn).view(np.uint8)
    else:
        c = by_word.astype(ml_dtypes.float4_e2m1fn).view(np.uint8) & 0xF
        words = (c[..., 0::2] | (c[..., 1::2] << 4)).reshape(k // 512, 128, 2 * n)
    return np.ascontiguousarray(words), np.ascontiguousarray(byte.astype(np.uint8).reshape(k // 512, 16, n))


def unpack_weight(words, scales, fmt):
    g, _, n = scales.shape
    words = np.ascontiguousarray(words).reshape(g, 128, n, -1)
    if fmt == "e4m3":
        vals = words.view(ml_dtypes.float8_e4m3fn).astype(np.float64)
    else:
        nib = np.empty((g, 128, n, 4), np.uint8)
        nib[..., 0::2] = words & 0xF
        nib[..., 1::2] = words >> 4
        vals = E2M1[nib]
    vals = vals * np.repeat(np.exp2(scales.astype(np.float64) - 127.0), 8, axis=1)[..., None]
    return vals.transpose(0, 1, 3, 2).reshape(g * 512, n)


def gelu(v):
    return 0.5 * v * (1.0 + np.tanh(np.sqrt(2.0 / np.pi) * (v + 0.044715 * v**3)))


K, T, S, M, N = 1024, 2048, 1024, 512, 1024

def setup_inputs():
    n = np.random.standard_normal
    s = mx_kscale(K)[:, None]
    u = mx_kscale(S)
    idx = np.random.permutation(T)[:S]
    tab_words, tab_scales = pack_weight(1.5 * n((K, T)) / np.sqrt(K) * s, "e4m3")
    w4_words, w4_scales = pack_weight(0.6 * n((K, N)) / np.sqrt(K) * s, "e2m1")
    wdT = 1.5 * n((N, T)) / np.sqrt(S)
    wdT[:, idx] /= u
    return {"tab_words": tab_words, "tab_scales": tab_scales, "offs": striped(idx),
            "x": (n((K, M)) / s).astype(np.float32),
            "w4_words": w4_words, "w4_scales": w4_scales,
            "wdT": wdT.astype(np.float32),
            "g": (np.exp(0.3 * n(S)) * u).astype(np.float32),
            "bo": (0.3 * n(N)).astype(np.float32)}

def reference(tab_words, tab_scales, offs, x, w4_words, w4_scales, wdT, g, bo):
    v = unpack_weight(tab_words, tab_scales, "e4m3")[:, unstriped(offs)]
    w4 = unpack_weight(w4_words, w4_scales, "e2m1")
    wd = f64(wdT)[:, unstriped(offs)]
    xq = mxq(f64(x), 0, "e4m3")
    p = v.T @ xq
    h = 1.0 / (1.0 + np.exp(-p))
    h = h * f64(g)[:, None]
    y = mxq(wd, 1, "e4m3") @ mxq(h, 0, "e4m3") + w4.T @ xq
    return np.tanh(y + f64(bo)[:, None])

@@ -1,0 +1,233 @@
+from contextlib import ExitStack
+
+import concourse.mybir as mybir
+from concourse.masks import make_identity
+
+K, T, S, M, N = 1024, 2048, 1024, 512, 1024
+FLOPS = 2 * M * (K * S + S * N + K * N)
+
+F32 = mybir.dt.float32
+BF16 = mybir.dt.bfloat16
+I32 = mybir.dt.int32
+U32 = mybir.dt.uint32
+U16 = mybir.dt.uint16
+U8 = mybir.dt.uint8
+FP8X4 = mybir.dt.float8_e4m3fn_x4
+FP4X4 = mybir.dt.float4_e2m1fn_x4
+ACT = mybir.ActivationFunctionType
+
+P = 128
+PASSES = 2
+TILES = N // P
+XS = 56
+GAIN_ON_POOL = True
+ALU = mybir.AluOpType
+
+
+def tile_list_listed_rating_autoencoder_kernel(tc, tab_words, tab_scales, offs, x, w4_words, w4_scales, wdT, g, bo, out):
+    nc = tc.nc
+    with ExitStack() as ctx:
+        keep = ctx.enter_context(tc.tile_pool(name="keep", bufs=1))
+        ring = ctx.enter_context(tc.tile_pool(name="ring", bufs=4))
+        banks = ctx.enter_context(tc.psum_pool(name="banks", bufs=1))
+
+        offsets = keep.tile([P, S // 16], U16, name="offsets")
+        nc.sync.dma_start(offsets[:], offs)
+
+        tab_plane = keep.tile([P, T // 4], I32, name="tab_plane", align_bytes=64)
+        w4_plane = keep.tile([P, PASSES, N // 4], I32, name="w4_plane", align_bytes=64)
+        rows = keep.tile([P, PASSES * P], F32, name="rows")
+        nc.vector.memset(tab_plane[:], 0)
+        nc.vector.memset(w4_plane[:], 0)
+        nc.vector.memset(rows[:], 0.0)
+        ident = keep.tile([P, P], F32, name="ident")
+        make_identity(nc, ident[:])
+
+        for quad in range(4):
+            nc.sync.dma_start(tab_plane[32 * quad : 32 * quad + 8, :], tab_scales[:, 4 * quad : 4 * quad + 4, :].bitcast(I32))
+
+        nc.sync.dma_start(rows[0:4, :].rearrange("t (b r) -> t b r", r=8), g.rearrange("(b t r) -> t b r", t=4, r=8))
+        x_raw = [keep.tile([P, 4, M], F32, name=f"x_raw{a}") for a in range(PASSES)]
+        tab = [keep.tile([P, T], I32, name=f"tab{a}") for a in range(PASSES)]
+        for a in range(PASSES):
+            nc.sync.dma_start(x_raw[a][:], x[512 * a : 512 * (a + 1), :].rearrange("(p i) m -> p i m", i=4))
+        nc.sync.dma_start(rows[8:16, 0:P], bo.rearrange("(c p) -> c p", p=P))
+        for a in range(PASSES):
+            nc.sync.dma_start(tab[a][:], tab_words[a].rearrange("p t i -> p (t i)").bitcast(I32))
+
+        wd = [keep.tile([P, T], F32, name=f"wd{c}", align_bytes=64) for c in range(TILES)]
+        w4 = keep.tile([P, PASSES, N // 2], I32, name="w4", align_bytes=64)
+        for c in range(TILES):
+            nc.sync.dma_start(wd[c][:], wdT[P * c : P * (c + 1), :])
+            if c == 3:
+                for quad in range(4):
+                    nc.sync.dma_start(w4_plane[32 * quad : 32 * quad + 4, :, :], w4_scales[:, 4 * quad : 4 * quad + 4, :].bitcast(I32).rearrange("a r w -> r a w"))
+                nc.sync.dma_start(w4[:], w4_words.bitcast(I32).rearrange("a p w -> p a w"))
+
+        v_plane = keep.tile([P, S], U8, name="v_plane", align_bytes=64)
+        listed_plane = keep.tile([P, S], U8, name="listed_plane", align_bytes=64)
+        nc.vector.tensor_copy(listed_plane[:], tab_plane[:].bitcast(U8).indirect(offsets[:]))
+
+        x_codes = keep.tile([P, PASSES, M], U32, name="x_codes", align_bytes=64)
+        x_plane = keep.tile([P, PASSES, M], U8, name="x_plane", align_bytes=64)
+        v_codes = [keep.tile([P, S], U32, name=f"v_codes{a}", align_bytes=64) for a in range(PASSES)]
+        x_grouped = [keep.tile([P, M, 4], BF16, name=f"x_grouped{a}", align_bytes=64) for a in range(PASSES)]
+
+        def cast_x(a):
+            dst = x_grouped[a][:].rearrange("p (c z) i -> p c i z", z=4)
+            src = x_raw[a][:].rearrange("p i (c z) -> p c i z", z=4)
+            nc.scalar.copy(dst[:, 0:XS], src[:, 0:XS])
+            nc.vector.tensor_copy(dst[:, XS : M // 4], src[:, XS : M // 4])
+
+        def quantise_x(a):
+            nc.vector.quantize_mx(out=x_codes[:, a, :].bitcast(FP8X4), scales=x_plane[:, a, :], in_=x_grouped[a][:].rearrange("p m i -> p (m i)"))
+
+        def pick_table(a, b0, b1):
+            nc.vector.tensor_copy(
+                v_codes[a][:].rearrange("p (t b r) -> p b t r", t=4, r=8)[:, b0:b1],
+                tab[a][:].bitcast(U32).indirect(offsets[:, 2 * b0 : 2 * b1]),
+            )
+
+        cast_x(0)
+        nc.vector.tensor_copy(
+            v_plane[:].bitcast(I32).rearrange("p (t b w) -> p t b w", t=4, w=2),
+            listed_plane[:].bitcast(I32).rearrange("p (b t w) -> p t b w", t=4, w=2),
+        )
+        quantise_x(0)
+        cast_x(1)
+        quantise_x(1)
+        pick_table(0, 0, 16)
+        pick_table(0, 16, 32)
+        pick_table(1, 0, 16)
+        pick_table(1, 16, 32)
+
+        cols_ps = banks.tile([P, 4, P], F32, name="bank7")
+        for b in range(PASSES):
+            nc.tensor.transpose(cols_ps[:, b, :], rows[:, P * b : P * (b + 1)], ident[:])
+        cols = keep.tile([P, PASSES, 16], F32, name="cols")
+        nc.scalar.copy(cols[:], cols_ps[:, 0:PASSES, 0:16])
+
+        wd_codes = {}
+        wd_plane = [keep.tile([P, PASSES * P], U8, name=f"wd_plane{c}", align_bytes=64) for c in range(TILES)]
+        picked = {}
+        grouped = [keep.tile([P, S], BF16, name=f"grouped{c}", align_bytes=64) for c in range(TILES)]
+        home = {5: "h_grouped1"}
+
+        def pick_wd(c, b0, b1):
+            if b0 == 0:
+                picked[c] = keep.tile([P, S], BF16, name=home.get(c, f"picked{c}"), align_bytes=64)
+            nc.vector.tensor_copy(
+                picked[c][:].rearrange("p (u b r e) -> p b u e r", u=2, r=8, e=2)[:, 16 * b0 : 16 * b1],
+                wd[c][:].indirect(offsets[:, 32 * b0 : 32 * b1]),
+            )
+
+        def turn_wd(c, b0, b1, bank):
+            words = picked[c][:].bitcast(F32)
+            turned = banks.tile([P, 4, P], F32, name=f"bank{bank}")
+            for b in range(b0, b1):
+                for u in range(2):
+                    s = 2 * u + b
+                    nc.tensor.transpose(turned[:, s, :], words[:, P * s : P * (s + 1)], ident[:])
+            nc.scalar.copy(
+                grouped[c][:].bitcast(F32).rearrange("p (b n u) -> p b n u", b=2, u=2)[:, b0:b1],
+                turned[:].rearrange("p (u b) n -> p b n u", u=2)[:, b0:b1],
+            )
+
+        def quantise_wd(c, b0, b1):
+            if b0 == 0:
+                wd_codes[c] = keep.tile([P, PASSES * P], U32, name=f"wd{c + 1}" if 3 <= c < TILES - 1 else f"wd_codes{c}", align_bytes=64)
+            nc.vector.quantize_mx(out=wd_codes[c][:, P * b0 : P * b1].bitcast(FP8X4), scales=wd_plane[c][:, P * b0 : P * b1], in_=grouped[c][:, 512 * b0 : 512 * b1])
+
+        h_codes = keep.tile([P, PASSES, M], U32, name="h_codes", align_bytes=64)
+        h_plane = keep.tile([P, PASSES, M], U8, name="h_plane", align_bytes=64)
+        h_rows = [keep.tile([P, 4, M], BF16, name=f"h_rows{b}") for b in range(PASSES)]
+        h_grouped = [keep.tile([P, M, 4], BF16, name=f"h_grouped{b}", align_bytes=64) for b in range(PASSES)]
+
+        sig = [keep.tile([P, 4, M], F32, name=f"sig{b}") for b in range(PASSES)]
+
+        def encode(b, t):
+            col = slice(256 * t + P * b, 256 * t + P * (b + 1))
+            acc = banks.tile([P, M], F32, name=f"bank{t}")
+            for a in range(PASSES):
+                nc.tensor.matmul_mx(
+                    out=acc[:], lhsT=v_codes[a][:, col].bitcast(FP8X4), lhsT_scale=v_plane[4 * a : P, col],
+                    rhs=x_codes[:, a, :].bitcast(FP8X4), rhs_scale=x_plane[:, a, :], start=(a == 0), stop=(a == PASSES - 1),
+                )
+            nc.scalar.activation(sig[b][:, t, :], acc[:], ACT.Sigmoid)
+
+        def gain(b, t):
+            if GAIN_ON_POOL:
+                nc.gpsimd.tensor_scalar(h_rows[b][:, t, :], sig[b][:, t, :], cols[:, b, t : t + 1], 0.0, ALU.mult, ALU.add)
+            else:
+                nc.scalar.activation(h_rows[b][:, t, :], sig[b][:, t, :], ACT.Copy, scale=cols[:, b, t : t + 1])
+
+        def group_h(b):
+            nc.scalar.copy(
+                h_grouped[b][:].rearrange("p (c z) t -> p c t z", z=4),
+                h_rows[b][:].rearrange("p t (c z) -> p c t z", z=4),
+            )
+
+        def quantise_h(b):
+            nc.vector.quantize_mx(out=h_codes[:, b, :].bitcast(FP8X4), scales=h_plane[:, b, :], in_=h_grouped[b][:].rearrange("p m t -> p (m t)"))
+
+        def decode(c, bank):
+            acc = banks.tile([P, M], F32, name=f"bank{bank}")
+            for a in range(PASSES):
+                nc.tensor.matmul_mx(
+                    out=acc[:], lhsT=w4[:, a, :].bitcast(U8)[:, 2 * P * c : 2 * P * (c + 1)].bitcast(FP4X4),
+                    lhsT_scale=w4_plane[:, a, :].bitcast(U8)[:, P * c : P * (c + 1)],
+                    rhs=x_codes[:, a, :].bitcast(FP8X4), rhs_scale=x_plane[:, a, :], start=(a == 0), stop=False,
+                )
+            for b in range(PASSES):
+                nc.tensor.matmul_mx(
+                    out=acc[:], lhsT=wd_codes[c][:, P * b : P * (b + 1)].bitcast(FP8X4), lhsT_scale=wd_plane[c][:, P * b : P * (b + 1)],
+                    rhs=h_codes[:, b, :].bitcast(FP8X4), rhs_scale=h_plane[:, b, :], start=False, stop=(b == PASSES - 1),
+                )
+            parts = 2 if c == TILES - 1 else 1
+            width = M // parts
+            for part in range(parts):
+                rated = ring.tile([P, width], F32, name="rated")
+                nc.scalar.activation(rated[:], acc[:, width * part : width * (part + 1)], ACT.Tanh, bias=cols[:, 0, 8 + c : 9 + c])
+                nc.sync.dma_start(out[P * c : P * (c + 1), width * part : width * (part + 1)], rated[:])
+
+        pick_wd(0, 0, 2)
+        for b in range(PASSES):
+            for t in range(4):
+                encode(b, t)
+                gain(b, t)
+        pick_wd(1, 0, 2)
+        pick_wd(2, 0, 2)
+        turn_wd(0, 0, 2, 2)
+        turn_wd(1, 0, 2, 3)
+        group_h(0)
+        quantise_wd(0, 0, 2)
+        quantise_wd(1, 0, 2)
+        pick_wd(3, 0, 2)
+        group_h(1)
+        turn_wd(2, 0, 2, 2)
+        turn_wd(3, 0, 2, 3)
+        quantise_h(0)
+        pick_wd(4, 0, 2)
+        quantise_h(1)
+        quantise_wd(2, 0, 2)
+        quantise_wd(3, 0, 2)
+        turn_wd(4, 0, 2, 2)
+        pick_wd(5, 0, 2)
+        for c in range(4):
+            decode(c, 4 + c)
+        turn_wd(5, 0, 2, 3)
+        quantise_wd(4, 0, 2)
+        pick_wd(6, 0, 2)
+        decode(4, 0)
+        turn_wd(6, 0, 2, 2)
+        quantise_wd(5, 0, 2)
+        pick_wd(7, 0, 1)
+        pick_wd(7, 1, 2)
+        decode(5, 1)
+        turn_wd(7, 0, 1, 3)
+        turn_wd(7, 1, 2, 2)
+        quantise_wd(6, 0, 2)
+        quantise_wd(7, 0, 1)
+        quantise_wd(7, 1, 2)
+        decode(6, 4)
+        decode(7, 5)

@@ -19,8 +19,9 @@ ACT = mybir.ActivationFunctionType
 P = 128
 PASSES = 2
 TILES = N // P
-XS = 56
-GAIN_ON_POOL = True
+XS = (88, 48)
+HS = (128, 64)
+GAIN_ON_POOL = False
 ALU = mybir.AluOpType
 
 
@@ -37,69 +38,71 @@ def tile_list_listed_rating_autoencoder_kernel(tc, tab_words, tab_scales, offs, 
         tab_plane = keep.tile([P, T // 4], I32, name="tab_plane", align_bytes=64)
         w4_plane = keep.tile([P, PASSES, N // 4], I32, name="w4_plane", align_bytes=64)
         rows = keep.tile([P, PASSES * P], F32, name="rows")
-        nc.vector.memset(tab_plane[:], 0)
-        nc.vector.memset(w4_plane[:], 0)
+        nc.gpsimd.memset(tab_plane[:], 0)
         nc.vector.memset(rows[:], 0.0)
+        nc.vector.memset(w4_plane[:], 0)
+        for quad in range(4):
+            nc.sync.dma_start(tab_plane[32 * quad : 32 * quad + 8, :], tab_scales[:, 4 * quad : 4 * quad + 4, :].bitcast(I32))
         ident = keep.tile([P, P], F32, name="ident")
         make_identity(nc, ident[:])
 
-        for quad in range(4):
-            nc.sync.dma_start(tab_plane[32 * quad : 32 * quad + 8, :], tab_scales[:, 4 * quad : 4 * quad + 4, :].bitcast(I32))
-
-        nc.sync.dma_start(rows[0:4, :].rearrange("t (b r) -> t b r", r=8), g.rearrange("(b t r) -> t b r", t=4, r=8))
         x_raw = [keep.tile([P, 4, M], F32, name=f"x_raw{a}") for a in range(PASSES)]
         tab = [keep.tile([P, T], I32, name=f"tab{a}") for a in range(PASSES)]
         for a in range(PASSES):
-            nc.sync.dma_start(x_raw[a][:], x[512 * a : 512 * (a + 1), :].rearrange("(p i) m -> p i m", i=4))
-        nc.sync.dma_start(rows[8:16, 0:P], bo.rearrange("(c p) -> c p", p=P))
-        for a in range(PASSES):
             nc.sync.dma_start(tab[a][:], tab_words[a].rearrange("p t i -> p (t i)").bitcast(I32))
+            nc.sync.dma_start(x_raw[a][:], x[512 * a : 512 * (a + 1), :].rearrange("(p i) m -> p i m", i=4))
 
         wd = [keep.tile([P, T], F32, name=f"wd{c}", align_bytes=64) for c in range(TILES)]
         w4 = keep.tile([P, PASSES, N // 2], I32, name="w4", align_bytes=64)
         for c in range(TILES):
             nc.sync.dma_start(wd[c][:], wdT[P * c : P * (c + 1), :])
-            if c == 3:
+            if c == 0:
+                nc.sync.dma_start(rows[0:4, :].rearrange("t (b r) -> t b r", r=8), g.rearrange("(b t r) -> t b r", t=4, r=8))
+                nc.sync.dma_start(rows[8:16, 0:P], bo.rearrange("(c p) -> c p", p=P))
+            if c == 4:
                 for quad in range(4):
                     nc.sync.dma_start(w4_plane[32 * quad : 32 * quad + 4, :, :], w4_scales[:, 4 * quad : 4 * quad + 4, :].bitcast(I32).rearrange("a r w -> r a w"))
                 nc.sync.dma_start(w4[:], w4_words.bitcast(I32).rearrange("a p w -> p a w"))
 
         v_plane = keep.tile([P, S], U8, name="v_plane", align_bytes=64)
         listed_plane = keep.tile([P, S], U8, name="listed_plane", align_bytes=64)
-        nc.vector.tensor_copy(listed_plane[:], tab_plane[:].bitcast(U8).indirect(offsets[:]))
 
         x_codes = keep.tile([P, PASSES, M], U32, name="x_codes", align_bytes=64)
         x_plane = keep.tile([P, PASSES, M], U8, name="x_plane", align_bytes=64)
-        v_codes = [keep.tile([P, S], U32, name=f"v_codes{a}", align_bytes=64) for a in range(PASSES)]
+        v_codes = {}
         x_grouped = [keep.tile([P, M, 4], BF16, name=f"x_grouped{a}", align_bytes=64) for a in range(PASSES)]
 
         def cast_x(a):
             dst = x_grouped[a][:].rearrange("p (c z) i -> p c i z", z=4)
             src = x_raw[a][:].rearrange("p i (c z) -> p c i z", z=4)
-            nc.scalar.copy(dst[:, 0:XS], src[:, 0:XS])
-            nc.vector.tensor_copy(dst[:, XS : M // 4], src[:, XS : M // 4])
+            nc.scalar.copy(dst[:, 0 : XS[a]], src[:, 0 : XS[a]])
+            if XS[a] < M // 4:
+                nc.vector.tensor_copy(dst[:, XS[a] : M // 4], src[:, XS[a] : M // 4])
 
         def quantise_x(a):
             nc.vector.quantize_mx(out=x_codes[:, a, :].bitcast(FP8X4), scales=x_plane[:, a, :], in_=x_grouped[a][:].rearrange("p m i -> p (m i)"))
 
-        def pick_table(a, b0, b1):
+        def pick_table(a, b0, b1, home):
+            codes = keep.tile([P, 4, P * (b1 - b0)], U32, name=home, align_bytes=64)
             nc.vector.tensor_copy(
-                v_codes[a][:].rearrange("p (t b r) -> p b t r", t=4, r=8)[:, b0:b1],
-                tab[a][:].bitcast(U32).indirect(offsets[:, 2 * b0 : 2 * b1]),
+                codes[:].rearrange("p t (b r) -> p b t r", r=8),
+                tab[a][:].bitcast(U32).indirect(offsets[:, 32 * b0 : 32 * b1]),
             )
+            for b in range(b0, b1):
+                v_codes[a, b] = codes[:, :, P * (b - b0) : P * (b - b0 + 1)]
 
-        cast_x(0)
+        nc.vector.tensor_copy(listed_plane[:], tab_plane[:].bitcast(U8).indirect(offsets[:]))
+        pick_table(0, 0, 2, "v_codes0")
         nc.vector.tensor_copy(
             v_plane[:].bitcast(I32).rearrange("p (t b w) -> p t b w", t=4, w=2),
             listed_plane[:].bitcast(I32).rearrange("p (b t w) -> p t b w", t=4, w=2),
         )
+        cast_x(0)
+        pick_table(1, 0, 1, "v_codes1")
         quantise_x(0)
+        pick_table(1, 1, 2, "x_grouped0")
         cast_x(1)
         quantise_x(1)
-        pick_table(0, 0, 16)
-        pick_table(0, 16, 32)
-        pick_table(1, 0, 16)
-        pick_table(1, 16, 32)
 
         cols_ps = banks.tile([P, 4, P], F32, name="bank7")
         for b in range(PASSES):
@@ -111,7 +114,7 @@ def tile_list_listed_rating_autoencoder_kernel(tc, tab_words, tab_scales, offs, 
         wd_plane = [keep.tile([P, PASSES * P], U8, name=f"wd_plane{c}", align_bytes=64) for c in range(TILES)]
         picked = {}
         grouped = [keep.tile([P, S], BF16, name=f"grouped{c}", align_bytes=64) for c in range(TILES)]
-        home = {5: "h_grouped1"}
+        home = {6: "h_grouped1"}
 
         def pick_wd(c, b0, b1):
             if b0 == 0:
@@ -135,7 +138,7 @@ def tile_list_listed_rating_autoencoder_kernel(tc, tab_words, tab_scales, offs, 
 
         def quantise_wd(c, b0, b1):
             if b0 == 0:
-                wd_codes[c] = keep.tile([P, PASSES * P], U32, name=f"wd{c + 1}" if 3 <= c < TILES - 1 else f"wd_codes{c}", align_bytes=64)
+                wd_codes[c] = keep.tile([P, PASSES * P], U32, name=f"wd{c + 1}" if 4 <= c < TILES - 1 else f"wd_codes{c}", align_bytes=64)
             nc.vector.quantize_mx(out=wd_codes[c][:, P * b0 : P * b1].bitcast(FP8X4), scales=wd_plane[c][:, P * b0 : P * b1], in_=grouped[c][:, 512 * b0 : 512 * b1])
 
         h_codes = keep.tile([P, PASSES, M], U32, name="h_codes", align_bytes=64)
@@ -147,10 +150,10 @@ def tile_list_listed_rating_autoencoder_kernel(tc, tab_words, tab_scales, offs, 
 
         def encode(b, t):
             col = slice(256 * t + P * b, 256 * t + P * (b + 1))
-            acc = banks.tile([P, M], F32, name=f"bank{t}")
+            acc = banks.tile([P, M], F32, name=f"bank{4 * b + t}")
             for a in range(PASSES):
                 nc.tensor.matmul_mx(
-                    out=acc[:], lhsT=v_codes[a][:, col].bitcast(FP8X4), lhsT_scale=v_plane[4 * a : P, col],
+                    out=acc[:], lhsT=v_codes[a, b][:, t, :].bitcast(FP8X4), lhsT_scale=v_plane[4 * a : P, col],
                     rhs=x_codes[:, a, :].bitcast(FP8X4), rhs_scale=x_plane[:, a, :], start=(a == 0), stop=(a == PASSES - 1),
                 )
             nc.scalar.activation(sig[b][:, t, :], acc[:], ACT.Sigmoid)
@@ -162,10 +165,11 @@ def tile_list_listed_rating_autoencoder_kernel(tc, tab_words, tab_scales, offs, 
                 nc.scalar.activation(h_rows[b][:, t, :], sig[b][:, t, :], ACT.Copy, scale=cols[:, b, t : t + 1])
 
         def group_h(b):
-            nc.scalar.copy(
-                h_grouped[b][:].rearrange("p (c z) t -> p c t z", z=4),
-                h_rows[b][:].rearrange("p t (c z) -> p c t z", z=4),
-            )
+            dst = h_grouped[b][:].rearrange("p (c z) t -> p c t z", z=4)
+            src = h_rows[b][:].rearrange("p t (c z) -> p c t z", z=4)
+            nc.scalar.copy(dst[:, 0 : HS[b]], src[:, 0 : HS[b]])
+            if HS[b] < M // 4:
+                nc.vector.tensor_copy(dst[:, HS[b] : M // 4], src[:, HS[b] : M // 4])
 
         def quantise_h(b):
             nc.vector.quantize_mx(out=h_codes[:, b, :].bitcast(FP8X4), scales=h_plane[:, b, :], in_=h_grouped[b][:].rearrange("p m t -> p (m t)"))
@@ -191,43 +195,45 @@ def tile_list_listed_rating_autoencoder_kernel(tc, tab_words, tab_scales, offs, 
                 nc.sync.dma_start(out[P * c : P * (c + 1), width * part : width * (part + 1)], rated[:])
 
         pick_wd(0, 0, 2)
-        for b in range(PASSES):
-            for t in range(4):
-                encode(b, t)
-                gain(b, t)
-        pick_wd(1, 0, 2)
-        pick_wd(2, 0, 2)
-        turn_wd(0, 0, 2, 2)
-        turn_wd(1, 0, 2, 3)
+        steps = [(b, t) for b in range(PASSES) for t in range(4)]
+        for i in range(len(steps) + 1):
+            if i < len(steps):
+                encode(*steps[i])
+            if i > 0:
+                gain(*steps[i - 1])
+        for c in range(1, 5):
+            pick_wd(c, 0, 2)
         group_h(0)
+        pick_wd(5, 0, 2)
+        group_h(1)
+        quantise_h(0)
+        turn_wd(0, 0, 2, 6)
+        turn_wd(1, 0, 2, 7)
+        quantise_h(1)
         quantise_wd(0, 0, 2)
         quantise_wd(1, 0, 2)
-        pick_wd(3, 0, 2)
-        group_h(1)
-        turn_wd(2, 0, 2, 2)
-        turn_wd(3, 0, 2, 3)
-        quantise_h(0)
-        pick_wd(4, 0, 2)
-        quantise_h(1)
+        turn_wd(2, 0, 2, 4)
+        turn_wd(3, 0, 2, 5)
+        pick_wd(6, 0, 2)
+        decode(0, 0)
+        turn_wd(4, 0, 2, 6)
+        decode(1, 1)
+        turn_wd(5, 0, 2, 7)
         quantise_wd(2, 0, 2)
         quantise_wd(3, 0, 2)
-        turn_wd(4, 0, 2, 2)
-        pick_wd(5, 0, 2)
-        for c in range(4):
-            decode(c, 4 + c)
-        turn_wd(5, 0, 2, 3)
         quantise_wd(4, 0, 2)
-        pick_wd(6, 0, 2)
-        decode(4, 0)
-        turn_wd(6, 0, 2, 2)
         quantise_wd(5, 0, 2)
         pick_wd(7, 0, 1)
         pick_wd(7, 1, 2)
+        decode(2, 2)
+        decode(3, 3)
+        turn_wd(6, 0, 2, 4)
+        decode(4, 0)
         decode(5, 1)
-        turn_wd(7, 0, 1, 3)
-        turn_wd(7, 1, 2, 2)
+        turn_wd(7, 0, 1, 5)
+        turn_wd(7, 1, 2, 6)
         quantise_wd(6, 0, 2)
         quantise_wd(7, 0, 1)
         quantise_wd(7, 1, 2)
-        decode(6, 4)
-        decode(7, 5)
+        decode(6, 2)
+        decode(7, 3)

@@ -19,9 +19,9 @@ ACT = mybir.ActivationFunctionType
 P = 128
 PASSES = 2
 TILES = N // P
-XS = (88, 48)
-HS = (128, 64)
-GAIN_ON_POOL = False
+XS = (80, 40)
+HS = (128, 128)
+GAIN_ON_POOL = True
 ALU = mybir.AluOpType
 
 
@@ -39,27 +39,31 @@ def tile_list_listed_rating_autoencoder_kernel(tc, tab_words, tab_scales, offs, 
         w4_plane = keep.tile([P, PASSES, N // 4], I32, name="w4_plane", align_bytes=64)
         rows = keep.tile([P, PASSES * P], F32, name="rows")
         nc.gpsimd.memset(tab_plane[:], 0)
+        warm_in = keep.tile([P, 1], F32, name="warm_in")
+        warm_out = keep.tile([P, 1], F32, name="warm_out")
+        nc.vector.memset(warm_in[:], 0.0)
+        nc.scalar.activation(warm_out[:], warm_in[:], ACT.Sigmoid)
         nc.vector.memset(rows[:], 0.0)
         nc.vector.memset(w4_plane[:], 0)
         for quad in range(4):
             nc.sync.dma_start(tab_plane[32 * quad : 32 * quad + 8, :], tab_scales[:, 4 * quad : 4 * quad + 4, :].bitcast(I32))
+        nc.sync.dma_start(rows[0:4, :].rearrange("t (b r) -> t b r", r=8), g.rearrange("(b t r) -> t b r", t=4, r=8))
+        nc.sync.dma_start(rows[8:16, 0:P], bo.rearrange("(c p) -> c p", p=P))
         ident = keep.tile([P, P], F32, name="ident")
         make_identity(nc, ident[:])
 
         x_raw = [keep.tile([P, 4, M], F32, name=f"x_raw{a}") for a in range(PASSES)]
         tab = [keep.tile([P, T], I32, name=f"tab{a}") for a in range(PASSES)]
+        nc.sync.dma_start(tab[0][:], tab_words[0].rearrange("p t i -> p (t i)").bitcast(I32))
         for a in range(PASSES):
-            nc.sync.dma_start(tab[a][:], tab_words[a].rearrange("p t i -> p (t i)").bitcast(I32))
             nc.sync.dma_start(x_raw[a][:], x[512 * a : 512 * (a + 1), :].rearrange("(p i) m -> p i m", i=4))
+        nc.sync.dma_start(tab[1][:], tab_words[1].rearrange("p t i -> p (t i)").bitcast(I32))
 
         wd = [keep.tile([P, T], F32, name=f"wd{c}", align_bytes=64) for c in range(TILES)]
         w4 = keep.tile([P, PASSES, N // 2], I32, name="w4", align_bytes=64)
         for c in range(TILES):
             nc.sync.dma_start(wd[c][:], wdT[P * c : P * (c + 1), :])
-            if c == 0:
-                nc.sync.dma_start(rows[0:4, :].rearrange("t (b r) -> t b r", r=8), g.rearrange("(b t r) -> t b r", t=4, r=8))
-                nc.sync.dma_start(rows[8:16, 0:P], bo.rearrange("(c p) -> c p", p=P))
-            if c == 4:
+            if c == 3:
                 for quad in range(4):
                     nc.sync.dma_start(w4_plane[32 * quad : 32 * quad + 4, :, :], w4_scales[:, 4 * quad : 4 * quad + 4, :].bitcast(I32).rearrange("a r w -> r a w"))
                 nc.sync.dma_start(w4[:], w4_words.bitcast(I32).rearrange("a p w -> p a w"))
@@ -72,15 +76,13 @@ def tile_list_listed_rating_autoencoder_kernel(tc, tab_words, tab_scales, offs, 
         v_codes = {}
         x_grouped = [keep.tile([P, M, 4], BF16, name=f"x_grouped{a}", align_bytes=64) for a in range(PASSES)]
 
-        def cast_x(a):
+        def cast_x(engine_copy, a, c0, c1):
             dst = x_grouped[a][:].rearrange("p (c z) i -> p c i z", z=4)
             src = x_raw[a][:].rearrange("p i (c z) -> p c i z", z=4)
-            nc.scalar.copy(dst[:, 0 : XS[a]], src[:, 0 : XS[a]])
-            if XS[a] < M // 4:
-                nc.vector.tensor_copy(dst[:, XS[a] : M // 4], src[:, XS[a] : M // 4])
+            engine_copy(dst[:, c0:c1], src[:, c0:c1])
 
-        def quantise_x(a):
-            nc.vector.quantize_mx(out=x_codes[:, a, :].bitcast(FP8X4), scales=x_plane[:, a, :], in_=x_grouped[a][:].rearrange("p m i -> p (m i)"))
+        def quantise_x(a, m0, m1):
+            nc.vector.quantize_mx(out=x_codes[:, a, m0:m1].bitcast(FP8X4), scales=x_plane[:, a, m0:m1], in_=x_grouped[a][:, m0:m1, :].rearrange("p m i -> p (m i)"))
 
         def pick_table(a, b0, b1, home):
             codes = keep.tile([P, 4, P * (b1 - b0)], U32, name=home, align_bytes=64)
@@ -93,28 +95,35 @@ def tile_list_listed_rating_autoencoder_kernel(tc, tab_words, tab_scales, offs, 
 
         nc.vector.tensor_copy(listed_plane[:], tab_plane[:].bitcast(U8).indirect(offsets[:]))
         pick_table(0, 0, 2, "v_codes0")
+        cast_x(nc.scalar.copy, 0, 0, 80)
+        cast_x(nc.vector.tensor_copy, 0, 80, 128)
         nc.vector.tensor_copy(
             v_plane[:].bitcast(I32).rearrange("p (t b w) -> p t b w", t=4, w=2),
             listed_plane[:].bitcast(I32).rearrange("p (b t w) -> p t b w", t=4, w=2),
         )
-        cast_x(0)
-        pick_table(1, 0, 1, "v_codes1")
-        quantise_x(0)
-        pick_table(1, 1, 2, "x_grouped0")
-        cast_x(1)
-        quantise_x(1)
+        quantise_x(0, 0, M)
+        cast_x(nc.scalar.copy, 1, 80, 128)
+        cast_x(nc.vector.tensor_copy, 1, 0, 64)
+        cast_x(nc.vector.tensor_copy, 1, 64, 80)
+        quantise_x(1, 0, M // 2)
+        quantise_x(1, M // 2, M)
+        pick_table(1, 0, 1, "v_codes1a")
+        pick_table(1, 1, 2, "v_codes1b")
 
+        cols = keep.tile([P, PASSES, 16], F32, name="cols")
         cols_ps = banks.tile([P, 4, P], F32, name="bank7")
         for b in range(PASSES):
             nc.tensor.transpose(cols_ps[:, b, :], rows[:, P * b : P * (b + 1)], ident[:])
-        cols = keep.tile([P, PASSES, 16], F32, name="cols")
         nc.scalar.copy(cols[:], cols_ps[:, 0:PASSES, 0:16])
 
         wd_codes = {}
         wd_plane = [keep.tile([P, PASSES * P], U8, name=f"wd_plane{c}", align_bytes=64) for c in range(TILES)]
         picked = {}
-        grouped = [keep.tile([P, S], BF16, name=f"grouped{c}", align_bytes=64) for c in range(TILES)]
-        home = {6: "h_grouped1"}
+        grouped = {}
+        grouped_home = {2: "h_rows0", 3: "h_rows1"}
+        home = {4: "h_grouped0", 5: "h_grouped1", 6: "h_rows1", 7: "grouped4"}
+        codes_home = {4: "wd5", 5: "wd6", 6: "wd7"}
+        h_codes = {}
 
         def pick_wd(c, b0, b1):
             if b0 == 0:
@@ -126,6 +135,8 @@ def tile_list_listed_rating_autoencoder_kernel(tc, tab_words, tab_scales, offs, 
 
         def turn_wd(c, b0, b1, bank):
             words = picked[c][:].bitcast(F32)
+            if b0 == 0:
+                grouped[c] = keep.tile([P, S], BF16, name=grouped_home.get(c, f"grouped{c}"), align_bytes=64)
             turned = banks.tile([P, 4, P], F32, name=f"bank{bank}")
             for b in range(b0, b1):
                 for u in range(2):
@@ -137,13 +148,12 @@ def tile_list_listed_rating_autoencoder_kernel(tc, tab_words, tab_scales, offs, 
             )
 
         def quantise_wd(c, b0, b1):
-            if b0 == 0:
-                wd_codes[c] = keep.tile([P, PASSES * P], U32, name=f"wd{c + 1}" if 4 <= c < TILES - 1 else f"wd_codes{c}", align_bytes=64)
+            if c not in wd_codes:
+                wd_codes[c] = keep.tile([P, PASSES * P], U32, name=codes_home.get(c, f"wd_codes{c}"), align_bytes=64)
             nc.vector.quantize_mx(out=wd_codes[c][:, P * b0 : P * b1].bitcast(FP8X4), scales=wd_plane[c][:, P * b0 : P * b1], in_=grouped[c][:, 512 * b0 : 512 * b1])
 
-        h_codes = keep.tile([P, PASSES, M], U32, name="h_codes", align_bytes=64)
         h_plane = keep.tile([P, PASSES, M], U8, name="h_plane", align_bytes=64)
-        h_rows = [keep.tile([P, 4, M], BF16, name=f"h_rows{b}") for b in range(PASSES)]
+        h_rows = [keep.tile([P, 4, M], BF16, name=f"h_rows{b}", align_bytes=64) for b in range(PASSES)]
         h_grouped = [keep.tile([P, M, 4], BF16, name=f"h_grouped{b}", align_bytes=64) for b in range(PASSES)]
 
         sig = [keep.tile([P, 4, M], F32, name=f"sig{b}") for b in range(PASSES)]
@@ -172,21 +182,22 @@ def tile_list_listed_rating_autoencoder_kernel(tc, tab_words, tab_scales, offs, 
                 nc.vector.tensor_copy(dst[:, HS[b] : M // 4], src[:, HS[b] : M // 4])
 
         def quantise_h(b):
-            nc.vector.quantize_mx(out=h_codes[:, b, :].bitcast(FP8X4), scales=h_plane[:, b, :], in_=h_grouped[b][:].rearrange("p m t -> p (m t)"))
+            nc.vector.quantize_mx(out=h_codes[b].bitcast(FP8X4), scales=h_plane[:, b, :], in_=h_grouped[b][:].rearrange("p m t -> p (m t)"))
 
         def decode(c, bank):
             acc = banks.tile([P, M], F32, name=f"bank{bank}")
-            for a in range(PASSES):
-                nc.tensor.matmul_mx(
-                    out=acc[:], lhsT=w4[:, a, :].bitcast(U8)[:, 2 * P * c : 2 * P * (c + 1)].bitcast(FP4X4),
-                    lhsT_scale=w4_plane[:, a, :].bitcast(U8)[:, P * c : P * (c + 1)],
-                    rhs=x_codes[:, a, :].bitcast(FP8X4), rhs_scale=x_plane[:, a, :], start=(a == 0), stop=False,
-                )
-            for b in range(PASSES):
-                nc.tensor.matmul_mx(
-                    out=acc[:], lhsT=wd_codes[c][:, P * b : P * (b + 1)].bitcast(FP8X4), lhsT_scale=wd_plane[c][:, P * b : P * (b + 1)],
-                    rhs=h_codes[:, b, :].bitcast(FP8X4), rhs_scale=h_plane[:, b, :], start=False, stop=(b == PASSES - 1),
-                )
+            shortcut = [
+                (w4[:, a, :].bitcast(U8)[:, 2 * P * c : 2 * P * (c + 1)].bitcast(FP4X4), w4_plane[:, a, :].bitcast(U8)[:, P * c : P * (c + 1)],
+                 x_codes[:, a, :].bitcast(FP8X4), x_plane[:, a, :])
+                for a in range(PASSES)
+            ]
+            coded = [
+                (wd_codes[c][:, P * b : P * (b + 1)].bitcast(FP8X4), wd_plane[c][:, P * b : P * (b + 1)], h_codes[b].bitcast(FP8X4), h_plane[:, b, :])
+                for b in range(PASSES)
+            ]
+            passes = shortcut + coded if c >= 6 else coded[:1] + shortcut + coded[1:]
+            for i, (lhsT, lhsT_scale, rhs, rhs_scale) in enumerate(passes):
+                nc.tensor.matmul_mx(out=acc[:], lhsT=lhsT, lhsT_scale=lhsT_scale, rhs=rhs, rhs_scale=rhs_scale, start=(i == 0), stop=(i == len(passes) - 1))
             parts = 2 if c == TILES - 1 else 1
             width = M // parts
             for part in range(parts):
@@ -194,44 +205,47 @@ def tile_list_listed_rating_autoencoder_kernel(tc, tab_words, tab_scales, offs, 
                 nc.scalar.activation(rated[:], acc[:, width * part : width * (part + 1)], ACT.Tanh, bias=cols[:, 0, 8 + c : 9 + c])
                 nc.sync.dma_start(out[P * c : P * (c + 1), width * part : width * (part + 1)], rated[:])
 
-        pick_wd(0, 0, 2)
-        steps = [(b, t) for b in range(PASSES) for t in range(4)]
-        for i in range(len(steps) + 1):
-            if i < len(steps):
-                encode(*steps[i])
-            if i > 0:
-                gain(*steps[i - 1])
-        for c in range(1, 5):
+        for c in range(4):
             pick_wd(c, 0, 2)
-        group_h(0)
-        pick_wd(5, 0, 2)
-        group_h(1)
-        quantise_h(0)
+        for b in range(PASSES):
+            for t in range(4):
+                encode(b, t)
+                gain(b, t)
         turn_wd(0, 0, 2, 6)
         turn_wd(1, 0, 2, 7)
-        quantise_h(1)
+        after3 = keep.tile([P, M + 3 * 256], U32, name="wd3", align_bytes=64)
+        h_codes[0] = after3[:, 0:M]
+        for c in range(3):
+            wd_codes[c] = after3[:, M + 256 * c : M + 256 * (c + 1)]
         quantise_wd(0, 0, 2)
         quantise_wd(1, 0, 2)
-        turn_wd(2, 0, 2, 4)
-        turn_wd(3, 0, 2, 5)
-        pick_wd(6, 0, 2)
-        decode(0, 0)
-        turn_wd(4, 0, 2, 6)
-        decode(1, 1)
-        turn_wd(5, 0, 2, 7)
+        group_h(0)
+        turn_wd(2, 0, 2, 6)
+        quantise_h(0)
         quantise_wd(2, 0, 2)
+        pick_wd(4, 0, 2)
+        after4 = keep.tile([P, M + 256], U32, name="wd4", align_bytes=64)
+        h_codes[1] = after4[:, 0:M]
+        wd_codes[3] = after4[:, M : M + 256]
+        group_h(1)
+        turn_wd(3, 0, 2, 7)
+        quantise_h(1)
         quantise_wd(3, 0, 2)
+        turn_wd(4, 0, 2, 7)
+        pick_wd(5, 0, 2)
+        for c in range(4):
+            decode(c, c)
+        turn_wd(5, 0, 2, 6)
         quantise_wd(4, 0, 2)
+        pick_wd(6, 0, 2)
+        decode(4, 4)
+        turn_wd(6, 0, 2, 7)
         quantise_wd(5, 0, 2)
         pick_wd(7, 0, 1)
         pick_wd(7, 1, 2)
-        decode(2, 2)
-        decode(3, 3)
-        turn_wd(6, 0, 2, 4)
-        decode(4, 0)
-        decode(5, 1)
-        turn_wd(7, 0, 1, 5)
-        turn_wd(7, 1, 2, 6)
+        decode(5, 5)
+        turn_wd(7, 0, 1, 6)
+        turn_wd(7, 1, 2, 7)
         quantise_wd(6, 0, 2)
         quantise_wd(7, 0, 1)
         quantise_wd(7, 1, 2)

@@ -19,9 +19,7 @@ ACT = mybir.ActivationFunctionType
 P = 128
 PASSES = 2
 TILES = N // P
-XS = (80, 40)
-HS = (128, 128)
-GAIN_ON_POOL = True
+CHUNK = 512
 ALU = mybir.AluOpType
 
 
@@ -30,6 +28,8 @@ def tile_list_listed_rating_autoencoder_kernel(tc, tab_words, tab_scales, offs, 
     with ExitStack() as ctx:
         keep = ctx.enter_context(tc.tile_pool(name="keep", bufs=1))
         ring = ctx.enter_context(tc.tile_pool(name="ring", bufs=4))
+        late = ctx.enter_context(tc.tile_pool(name="late", bufs=1))
+        mid = ctx.enter_context(tc.tile_pool(name="mid", bufs=1))
         banks = ctx.enter_context(tc.psum_pool(name="banks", bufs=1))
 
         offsets = keep.tile([P, S // 16], U16, name="offsets")
@@ -59,14 +59,23 @@ def tile_list_listed_rating_autoencoder_kernel(tc, tab_words, tab_scales, offs, 
             nc.sync.dma_start(x_raw[a][:], x[512 * a : 512 * (a + 1), :].rearrange("(p i) m -> p i m", i=4))
         nc.sync.dma_start(tab[1][:], tab_words[1].rearrange("p t i -> p (t i)").bitcast(I32))
 
-        wd = [keep.tile([P, T], F32, name=f"wd{c}", align_bytes=64) for c in range(TILES)]
-        w4 = keep.tile([P, PASSES, N // 2], I32, name="w4", align_bytes=64)
-        for c in range(TILES):
+        wd = {c: keep.tile([P, T], F32, name=f"wd{c}", align_bytes=64) for c in (0, 1, 2, 6, 7)}
+        wd[3] = mid.tile([P, T], F32, name="wd3", align_bytes=64, offset=0)
+        w4 = [keep.tile([P, PASSES, N // 4], I32, name=f"w4_{half}", align_bytes=64) for half in range(2)]
+        pair_raw = [keep.tile([P, 2, CHUNK], F32, name=f"pair_raw{i}", align_bytes=64) for i in range(T // CHUNK - 1)]
+        pair_raw.append(late.tile([P, 2, CHUNK], F32, name="pair_raw_last", align_bytes=64, offset=0))
+        pair_rows = wdT[4 * P : 6 * P, :].rearrange("(p e) t -> p e t", e=2)
+        w4_all = w4_words.bitcast(I32).rearrange("a p w -> p a w")
+        for c in range(4):
             nc.sync.dma_start(wd[c][:], wdT[P * c : P * (c + 1), :])
-            if c == 3:
-                for quad in range(4):
-                    nc.sync.dma_start(w4_plane[32 * quad : 32 * quad + 4, :, :], w4_scales[:, 4 * quad : 4 * quad + 4, :].bitcast(I32).rearrange("a r w -> r a w"))
-                nc.sync.dma_start(w4[:], w4_words.bitcast(I32).rearrange("a p w -> p a w"))
+        for quad in range(4):
+            nc.sync.dma_start(w4_plane[32 * quad : 32 * quad + 4, :, :], w4_scales[:, 4 * quad : 4 * quad + 4, :].bitcast(I32).rearrange("a r w -> r a w"))
+        nc.sync.dma_start(w4[0][:], w4_all[:, :, 0 : N // 4])
+        for i in range(T // CHUNK):
+            nc.sync.dma_start(pair_raw[i][:], pair_rows[:, :, CHUNK * i : CHUNK * (i + 1)])
+        nc.sync.dma_start(w4[1][:], w4_all[:, :, N // 4 : N // 2])
+        for c in (6, 7):
+            nc.sync.dma_start(wd[c][:], wdT[P * c : P * (c + 1), :])
 
         v_plane = keep.tile([P, S], U8, name="v_plane", align_bytes=64)
         listed_plane = keep.tile([P, S], U8, name="listed_plane", align_bytes=64)
@@ -117,12 +126,13 @@ def tile_list_listed_rating_autoencoder_kernel(tc, tab_words, tab_scales, offs, 
         nc.scalar.copy(cols[:], cols_ps[:, 0:PASSES, 0:16])
 
         wd_codes = {}
-        wd_plane = [keep.tile([P, PASSES * P], U8, name=f"wd_plane{c}", align_bytes=64) for c in range(TILES)]
+        wd_plane = {c: keep.tile([P, PASSES * P], U8, name=f"wd_plane{c}", align_bytes=64) for c in (0, 1, 2, 3, 6, 7)}
+        coded_wd = {}
         picked = {}
         grouped = {}
-        grouped_home = {2: "h_rows0", 3: "h_rows1"}
-        home = {4: "h_grouped0", 5: "h_grouped1", 6: "h_rows1", 7: "grouped4"}
-        codes_home = {4: "wd5", 5: "wd6", 6: "wd7"}
+        grouped_home = {2: "h_rows0"}
+        home = {}
+        codes_home = {6: "wd7"}
         h_codes = {}
 
         def pick_wd(c, b0, b1):
@@ -135,7 +145,9 @@ def tile_list_listed_rating_autoencoder_kernel(tc, tab_words, tab_scales, offs, 
 
         def turn_wd(c, b0, b1, bank):
             words = picked[c][:].bitcast(F32)
-            if b0 == 0:
+            if c == 3:
+                grouped[c] = late.tile([P, S], BF16, name="grouped3", align_bytes=64, offset=0)
+            elif b0 == 0:
                 grouped[c] = keep.tile([P, S], BF16, name=grouped_home.get(c, f"grouped{c}"), align_bytes=64)
             turned = banks.tile([P, 4, P], F32, name=f"bank{bank}")
             for b in range(b0, b1):
@@ -151,10 +163,47 @@ def tile_list_listed_rating_autoencoder_kernel(tc, tab_words, tab_scales, offs, 
             if c not in wd_codes:
                 wd_codes[c] = keep.tile([P, PASSES * P], U32, name=codes_home.get(c, f"wd_codes{c}"), align_bytes=64)
             nc.vector.quantize_mx(out=wd_codes[c][:, P * b0 : P * b1].bitcast(FP8X4), scales=wd_plane[c][:, P * b0 : P * b1], in_=grouped[c][:, 512 * b0 : 512 * b1])
+            for b in range(b0, b1):
+                coded_wd[c, b] = (wd_codes[c][:, P * b : P * (b + 1)].bitcast(FP8X4), wd_plane[c][:, P * b : P * (b + 1)])
+
+        pair_words = keep.tile([P, 2 * T], BF16, name="pair_words", align_bytes=64)
+        pair_picked = keep.tile([P, S], U32, name="pair_picked", align_bytes=64)
+        pair_grouped = keep.tile([P, 2 * S], BF16, name="pair_grouped", align_bytes=64)
+        pair_plane = keep.tile([P, PASSES * 2 * P], U8, name="pair_plane", align_bytes=64)
+
+        def cast_pair(i, engine_copy):
+            engine_copy(
+                pair_words[:, 2 * CHUNK * i : 2 * CHUNK * (i + 1)].rearrange("p (t e) -> p t e", e=2),
+                pair_raw[i][:].rearrange("p e t -> p t e"),
+            )
+
+        def pick_pair():
+            nc.vector.tensor_copy(
+                pair_picked[:].rearrange("p (b t q r) -> p b q t r", b=2, t=4, r=8),
+                pair_words[:].bitcast(U32).indirect(offsets[:]),
+            )
+
+        def turn_pair(b, bank):
+            words = pair_picked[:].bitcast(F32)
+            turned = banks.tile([P, 4, P], F32, name=f"bank{bank}")
+            for t in range(4):
+                nc.tensor.transpose(turned[:, t, :], words[:, 512 * b + P * t : 512 * b + P * (t + 1)], ident[:])
+            nc.scalar.copy(
+                pair_grouped[:, S * b : S * (b + 1)].rearrange("p (n t) -> p n t", t=4),
+                turned[:].bitcast(BF16).rearrange("p t n -> p n t"),
+            )
+
+        def quantise_pair():
+            codes = keep.tile([P, PASSES * 2 * P], U32, name="wd6", align_bytes=64)
+            nc.vector.quantize_mx(out=codes[:].bitcast(FP8X4), scales=pair_plane[:], in_=pair_grouped[:])
+            for c in (4, 5):
+                for b in range(PASSES):
+                    cols_c = slice(2 * P * b + P * (c - 4), 2 * P * b + P * (c - 3))
+                    coded_wd[c, b] = (codes[:, cols_c].bitcast(FP8X4), pair_plane[:, cols_c])
 
         h_plane = keep.tile([P, PASSES, M], U8, name="h_plane", align_bytes=64)
-        h_rows = [keep.tile([P, 4, M], BF16, name=f"h_rows{b}", align_bytes=64) for b in range(PASSES)]
-        h_grouped = [keep.tile([P, M, 4], BF16, name=f"h_grouped{b}", align_bytes=64) for b in range(PASSES)]
+        h_rows = [keep.tile([P, 4 * M], BF16, name=f"h_rows{b}", align_bytes=64) for b in range(PASSES)]
+        h_grouped = {0: keep.tile([P, 4 * M], BF16, name="h_grouped0", align_bytes=64)}
 
         sig = [keep.tile([P, 4, M], F32, name=f"sig{b}") for b in range(PASSES)]
 
@@ -169,41 +218,38 @@ def tile_list_listed_rating_autoencoder_kernel(tc, tab_words, tab_scales, offs, 
             nc.scalar.activation(sig[b][:, t, :], acc[:], ACT.Sigmoid)
 
         def gain(b, t):
-            if GAIN_ON_POOL:
-                nc.gpsimd.tensor_scalar(h_rows[b][:, t, :], sig[b][:, t, :], cols[:, b, t : t + 1], 0.0, ALU.mult, ALU.add)
-            else:
-                nc.scalar.activation(h_rows[b][:, t, :], sig[b][:, t, :], ACT.Copy, scale=cols[:, b, t : t + 1])
+            pairs = h_rows[b][:].rearrange("p (u m e) -> p u m e", u=2, e=2)
+            nc.gpsimd.tensor_scalar(pairs[:, t // 2, :, t % 2], sig[b][:, t, :], cols[:, b, t : t + 1], 0.0, ALU.mult, ALU.add)
 
-        def group_h(b):
-            dst = h_grouped[b][:].rearrange("p (c z) t -> p c t z", z=4)
-            src = h_rows[b][:].rearrange("p t (c z) -> p c t z", z=4)
-            nc.scalar.copy(dst[:, 0 : HS[b]], src[:, 0 : HS[b]])
-            if HS[b] < M // 4:
-                nc.vector.tensor_copy(dst[:, HS[b] : M // 4], src[:, HS[b] : M // 4])
+        def group_h(b, engine_copy):
+            engine_copy(
+                h_grouped[b][:].bitcast(F32).rearrange("p (m u) -> p m u", u=2),
+                h_rows[b][:].bitcast(F32).rearrange("p (u m) -> p m u", u=2),
+            )
 
         def quantise_h(b):
-            nc.vector.quantize_mx(out=h_codes[b].bitcast(FP8X4), scales=h_plane[:, b, :], in_=h_grouped[b][:].rearrange("p m t -> p (m t)"))
+            nc.vector.quantize_mx(out=h_codes[b].bitcast(FP8X4), scales=h_plane[:, b, :], in_=h_grouped[b][:])
 
         def decode(c, bank):
             acc = banks.tile([P, M], F32, name=f"bank{bank}")
             shortcut = [
-                (w4[:, a, :].bitcast(U8)[:, 2 * P * c : 2 * P * (c + 1)].bitcast(FP4X4), w4_plane[:, a, :].bitcast(U8)[:, P * c : P * (c + 1)],
+                (w4[c // 4][:, a, :].bitcast(U8)[:, 2 * P * (c % 4) : 2 * P * (c % 4 + 1)].bitcast(FP4X4), w4_plane[:, a, :].bitcast(U8)[:, P * c : P * (c + 1)],
                  x_codes[:, a, :].bitcast(FP8X4), x_plane[:, a, :])
                 for a in range(PASSES)
             ]
             coded = [
-                (wd_codes[c][:, P * b : P * (b + 1)].bitcast(FP8X4), wd_plane[c][:, P * b : P * (b + 1)], h_codes[b].bitcast(FP8X4), h_plane[:, b, :])
+                (coded_wd[c, b][0], coded_wd[c, b][1], h_codes[b].bitcast(FP8X4), h_plane[:, b, :])
                 for b in range(PASSES)
             ]
-            passes = shortcut + coded if c >= 6 else coded[:1] + shortcut + coded[1:]
+            passes = shortcut + coded
             for i, (lhsT, lhsT_scale, rhs, rhs_scale) in enumerate(passes):
                 nc.tensor.matmul_mx(out=acc[:], lhsT=lhsT, lhsT_scale=lhsT_scale, rhs=rhs, rhs_scale=rhs_scale, start=(i == 0), stop=(i == len(passes) - 1))
             parts = 2 if c == TILES - 1 else 1
             width = M // parts
             for part in range(parts):
-                rated = ring.tile([P, width], F32, name="rated")
-                nc.scalar.activation(rated[:], acc[:, width * part : width * (part + 1)], ACT.Tanh, bias=cols[:, 0, 8 + c : 9 + c])
-                nc.sync.dma_start(out[P * c : P * (c + 1), width * part : width * (part + 1)], rated[:])
+                rated = rated_early[:, c, :] if c < 3 else ring.tile([P, width], F32, name="rated")[:]
+                nc.scalar.activation(rated, acc[:, width * part : width * (part + 1)], ACT.Tanh, bias=cols[:, 0, 8 + c : 9 + c])
+                nc.sync.dma_start(out[P * c : P * (c + 1), width * part : width * (part + 1)], rated)
 
         for c in range(4):
             pick_wd(c, 0, 2)
@@ -213,41 +259,44 @@ def tile_list_listed_rating_autoencoder_kernel(tc, tab_words, tab_scales, offs, 
                 gain(b, t)
         turn_wd(0, 0, 2, 6)
         turn_wd(1, 0, 2, 7)
-        after3 = keep.tile([P, M + 3 * 256], U32, name="wd3", align_bytes=64)
-        h_codes[0] = after3[:, 0:M]
-        for c in range(3):
-            wd_codes[c] = after3[:, M + 256 * c : M + 256 * (c + 1)]
+        after3 = mid.tile([P, 2 * M + 4 * 256], U32, name="after3", align_bytes=64, offset=8 * M)
+        h_grouped[1] = mid.tile([P, 4 * M], BF16, name="h_grouped1", align_bytes=64, offset=0)
+        for b in range(PASSES):
+            h_codes[b] = after3[:, M * b : M * (b + 1)]
+        for c in range(4):
+            wd_codes[c] = after3[:, 2 * M + 256 * c : 2 * M + 256 * (c + 1)]
         quantise_wd(0, 0, 2)
         quantise_wd(1, 0, 2)
-        group_h(0)
+        group_h(0, nc.scalar.copy)
         turn_wd(2, 0, 2, 6)
         quantise_h(0)
         quantise_wd(2, 0, 2)
-        pick_wd(4, 0, 2)
-        after4 = keep.tile([P, M + 256], U32, name="wd4", align_bytes=64)
-        h_codes[1] = after4[:, 0:M]
-        wd_codes[3] = after4[:, M : M + 256]
-        group_h(1)
-        turn_wd(3, 0, 2, 7)
+        group_h(1, nc.vector.tensor_copy)
         quantise_h(1)
+        cast_pair(0, nc.scalar.copy)
+        cast_pair(1, nc.scalar.copy)
+        cast_pair(2, nc.scalar.copy)
+        cast_pair(3, nc.scalar.copy)
+        pick_pair()
+        turn_wd(3, 0, 2, 7)
         quantise_wd(3, 0, 2)
-        turn_wd(4, 0, 2, 7)
-        pick_wd(5, 0, 2)
-        for c in range(4):
+        rated_early = late.tile([P, 3, M], F32, name="rated_early", align_bytes=64, offset=2 * S)
+        for c in range(3):
             decode(c, c)
-        turn_wd(5, 0, 2, 6)
-        quantise_wd(4, 0, 2)
+        turn_pair(0, 6)
+        turn_pair(1, 7)
+        decode(3, 3)
         pick_wd(6, 0, 2)
-        decode(4, 4)
-        turn_wd(6, 0, 2, 7)
-        quantise_wd(5, 0, 2)
+        quantise_pair()
+        turn_wd(6, 0, 2, 6)
         pick_wd(7, 0, 1)
         pick_wd(7, 1, 2)
+        decode(4, 4)
         decode(5, 5)
-        turn_wd(7, 0, 1, 6)
-        turn_wd(7, 1, 2, 7)
+        turn_wd(7, 0, 1, 7)
+        turn_wd(7, 1, 2, 6)
         quantise_wd(6, 0, 2)
         quantise_wd(7, 0, 1)
         quantise_wd(7, 1, 2)
-        decode(6, 2)
-        decode(7, 3)
+        decode(6, 0)
+        decode(7, 1)

@@ -20,6 +20,7 @@ P = 128
 PASSES = 2
 TILES = N // P
 CHUNK = 512
+X_SPLIT = 76
 ALU = mybir.AluOpType
 
 
@@ -27,7 +28,7 @@ def tile_list_listed_rating_autoencoder_kernel(tc, tab_words, tab_scales, offs, 
     nc = tc.nc
     with ExitStack() as ctx:
         keep = ctx.enter_context(tc.tile_pool(name="keep", bufs=1))
-        ring = ctx.enter_context(tc.tile_pool(name="ring", bufs=4))
+        ring = ctx.enter_context(tc.tile_pool(name="ring", bufs=6))
         late = ctx.enter_context(tc.tile_pool(name="late", bufs=1))
         mid = ctx.enter_context(tc.tile_pool(name="mid", bufs=1))
         banks = ctx.enter_context(tc.psum_pool(name="banks", bufs=1))
@@ -45,37 +46,59 @@ def tile_list_listed_rating_autoencoder_kernel(tc, tab_words, tab_scales, offs, 
         nc.scalar.activation(warm_out[:], warm_in[:], ACT.Sigmoid)
         nc.vector.memset(rows[:], 0.0)
         nc.vector.memset(w4_plane[:], 0)
-        for quad in range(4):
-            nc.sync.dma_start(tab_plane[32 * quad : 32 * quad + 8, :], tab_scales[:, 4 * quad : 4 * quad + 4, :].bitcast(I32))
-        nc.sync.dma_start(rows[0:4, :].rearrange("t (b r) -> t b r", r=8), g.rearrange("(b t r) -> t b r", t=4, r=8))
-        nc.sync.dma_start(rows[8:16, 0:P], bo.rearrange("(c p) -> c p", p=P))
         ident = keep.tile([P, P], F32, name="ident")
         make_identity(nc, ident[:])
 
         x_raw = [keep.tile([P, 4, M], F32, name=f"x_raw{a}") for a in range(PASSES)]
         tab = [keep.tile([P, T], I32, name=f"tab{a}") for a in range(PASSES)]
-        nc.sync.dma_start(tab[0][:], tab_words[0].rearrange("p t i -> p (t i)").bitcast(I32))
-        for a in range(PASSES):
-            nc.sync.dma_start(x_raw[a][:], x[512 * a : 512 * (a + 1), :].rearrange("(p i) m -> p i m", i=4))
-        nc.sync.dma_start(tab[1][:], tab_words[1].rearrange("p t i -> p (t i)").bitcast(I32))
-
         wd = {c: keep.tile([P, T], F32, name=f"wd{c}", align_bytes=64) for c in (0, 1, 2, 6, 7)}
         wd[3] = mid.tile([P, T], F32, name="wd3", align_bytes=64, offset=0)
         w4 = [keep.tile([P, PASSES, N // 4], I32, name=f"w4_{half}", align_bytes=64) for half in range(2)]
         pair_raw = [keep.tile([P, 2, CHUNK], F32, name=f"pair_raw{i}", align_bytes=64) for i in range(T // CHUNK - 1)]
         pair_raw.append(late.tile([P, 2, CHUNK], F32, name="pair_raw_last", align_bytes=64, offset=0))
         pair_rows = wdT[4 * P : 6 * P, :].rearrange("(p e) t -> p e t", e=2)
-        w4_all = w4_words.bitcast(I32).rearrange("a p w -> p a w")
-        for c in range(4):
+
+        def load_table(a, t0, t1):
+            nc.sync.dma_start(tab[a][:, t0:t1], tab_words[a].rearrange("p t i -> p (t i)").bitcast(I32)[:, t0:t1])
+
+        def load_x(a):
+            nc.sync.dma_start(x_raw[a][:], x[512 * a : 512 * (a + 1), :].rearrange("(p i) m -> p i m", i=4))
+
+        def load_wd(c):
             nc.sync.dma_start(wd[c][:], wdT[P * c : P * (c + 1), :])
-        for quad in range(4):
-            nc.sync.dma_start(w4_plane[32 * quad : 32 * quad + 4, :, :], w4_scales[:, 4 * quad : 4 * quad + 4, :].bitcast(I32).rearrange("a r w -> r a w"))
-        nc.sync.dma_start(w4[0][:], w4_all[:, :, 0 : N // 4])
-        for i in range(T // CHUNK):
+
+        def load_shortcut(half):
+            nc.sync.dma_start(w4[half][:], w4_words.bitcast(I32).rearrange("a p w -> p a w")[:, :, N // 4 * half : N // 4 * (half + 1)])
+
+        def load_shortcut_scales():
+            for quad in range(4):
+                nc.sync.dma_start(w4_plane[32 * quad : 32 * quad + 4, :, :], w4_scales[:, 4 * quad : 4 * quad + 4, :].bitcast(I32).rearrange("a r w -> r a w"))
+
+        def load_pair(i):
             nc.sync.dma_start(pair_raw[i][:], pair_rows[:, :, CHUNK * i : CHUNK * (i + 1)])
-        nc.sync.dma_start(w4[1][:], w4_all[:, :, N // 4 : N // 2])
-        for c in (6, 7):
-            nc.sync.dma_start(wd[c][:], wdT[P * c : P * (c + 1), :])
+
+        load_table(0, 0, T // 2)
+        for quad in range(4):
+            nc.sync.dma_start(tab_plane[32 * quad : 32 * quad + 8, :], tab_scales[:, 4 * quad : 4 * quad + 4, :].bitcast(I32))
+        load_table(0, T // 2, T)
+        load_x(0)
+        load_x(1)
+        nc.sync.dma_start(rows[0:4, :].rearrange("t (b r) -> t b r", r=8), g.rearrange("(b t r) -> t b r", t=4, r=8))
+        nc.sync.dma_start(rows[8:16, 0:P], bo.rearrange("(c p) -> c p", p=P))
+        load_table(1, 0, T)
+        load_wd(0)
+        load_wd(1)
+        load_wd(2)
+        load_pair(0)
+        load_wd(3)
+        load_shortcut_scales()
+        load_shortcut(0)
+        load_pair(1)
+        load_pair(2)
+        load_pair(3)
+        load_shortcut(1)
+        load_wd(6)
+        load_wd(7)
 
         v_plane = keep.tile([P, S], U8, name="v_plane", align_bytes=64)
         listed_plane = keep.tile([P, S], U8, name="listed_plane", align_bytes=64)
@@ -104,23 +127,20 @@ def tile_list_listed_rating_autoencoder_kernel(tc, tab_words, tab_scales, offs, 
 
         nc.vector.tensor_copy(listed_plane[:], tab_plane[:].bitcast(U8).indirect(offsets[:]))
         pick_table(0, 0, 2, "v_codes0")
-        cast_x(nc.scalar.copy, 0, 0, 80)
-        cast_x(nc.vector.tensor_copy, 0, 80, 128)
         nc.vector.tensor_copy(
             v_plane[:].bitcast(I32).rearrange("p (t b w) -> p t b w", t=4, w=2),
             listed_plane[:].bitcast(I32).rearrange("p (b t w) -> p t b w", t=4, w=2),
         )
+        cast_x(nc.scalar.copy, 0, 0, 128)
         quantise_x(0, 0, M)
-        cast_x(nc.scalar.copy, 1, 80, 128)
-        cast_x(nc.vector.tensor_copy, 1, 0, 64)
-        cast_x(nc.vector.tensor_copy, 1, 64, 80)
-        quantise_x(1, 0, M // 2)
-        quantise_x(1, M // 2, M)
+        cast_x(nc.scalar.copy, 1, 0, X_SPLIT)
+        cast_x(nc.vector.tensor_copy, 1, X_SPLIT, 128)
+        quantise_x(1, 0, M)
         pick_table(1, 0, 1, "v_codes1a")
         pick_table(1, 1, 2, "v_codes1b")
 
         cols = keep.tile([P, PASSES, 16], F32, name="cols")
-        cols_ps = banks.tile([P, 4, P], F32, name="bank7")
+        cols_ps = banks.tile([P, 4, P], F32, name="bank5")
         for b in range(PASSES):
             nc.tensor.transpose(cols_ps[:, b, :], rows[:, P * b : P * (b + 1)], ident[:])
         nc.scalar.copy(cols[:], cols_ps[:, 0:PASSES, 0:16])
@@ -130,21 +150,20 @@ def tile_list_listed_rating_autoencoder_kernel(tc, tab_words, tab_scales, offs, 
         coded_wd = {}
         picked = {}
         grouped = {}
-        grouped_home = {2: "h_rows0"}
-        home = {}
+        grouped_home = {}
+        home = {(7, 1): "pair_grouped"}
         codes_home = {6: "wd7"}
         h_codes = {}
 
         def pick_wd(c, b0, b1):
-            if b0 == 0:
-                picked[c] = keep.tile([P, S], BF16, name=home.get(c, f"picked{c}"), align_bytes=64)
+            picked[c, b0] = keep.tile([P, 512 * (b1 - b0)], BF16, name=home.get((c, b0), f"picked{c}_{b0}"), align_bytes=64)
             nc.vector.tensor_copy(
-                picked[c][:].rearrange("p (u b r e) -> p b u e r", u=2, r=8, e=2)[:, 16 * b0 : 16 * b1],
+                picked[c, b0][:].rearrange("p (u b r e) -> p b u e r", u=2, r=8, e=2),
                 wd[c][:].indirect(offsets[:, 32 * b0 : 32 * b1]),
             )
 
         def turn_wd(c, b0, b1, bank):
-            words = picked[c][:].bitcast(F32)
+            words = picked[c, b0][:].bitcast(F32)
             if c == 3:
                 grouped[c] = late.tile([P, S], BF16, name="grouped3", align_bytes=64, offset=0)
             elif b0 == 0:
@@ -152,8 +171,8 @@ def tile_list_listed_rating_autoencoder_kernel(tc, tab_words, tab_scales, offs, 
             turned = banks.tile([P, 4, P], F32, name=f"bank{bank}")
             for b in range(b0, b1):
                 for u in range(2):
-                    s = 2 * u + b
-                    nc.tensor.transpose(turned[:, s, :], words[:, P * s : P * (s + 1)], ident[:])
+                    s = (b1 - b0) * u + b - b0
+                    nc.tensor.transpose(turned[:, 2 * u + b, :], words[:, P * s : P * (s + 1)], ident[:])
             nc.scalar.copy(
                 grouped[c][:].bitcast(F32).rearrange("p (b n u) -> p b n u", b=2, u=2)[:, b0:b1],
                 turned[:].rearrange("p (u b) n -> p b n u", u=2)[:, b0:b1],
@@ -167,27 +186,27 @@ def tile_list_listed_rating_autoencoder_kernel(tc, tab_words, tab_scales, offs, 
                 coded_wd[c, b] = (wd_codes[c][:, P * b : P * (b + 1)].bitcast(FP8X4), wd_plane[c][:, P * b : P * (b + 1)])
 
         pair_words = keep.tile([P, 2 * T], BF16, name="pair_words", align_bytes=64)
-        pair_picked = keep.tile([P, S], U32, name="pair_picked", align_bytes=64)
+        pair_picked = [keep.tile([P, S // 2], U32, name=f"pair_picked{b}", align_bytes=64) for b in range(PASSES)]
         pair_grouped = keep.tile([P, 2 * S], BF16, name="pair_grouped", align_bytes=64)
         pair_plane = keep.tile([P, PASSES * 2 * P], U8, name="pair_plane", align_bytes=64)
 
-        def cast_pair(i, engine_copy):
+        def cast_pair(i, engine_copy, t0=0, t1=CHUNK):
             engine_copy(
-                pair_words[:, 2 * CHUNK * i : 2 * CHUNK * (i + 1)].rearrange("p (t e) -> p t e", e=2),
-                pair_raw[i][:].rearrange("p e t -> p t e"),
+                pair_words[:, 2 * (CHUNK * i + t0) : 2 * (CHUNK * i + t1)].rearrange("p (t e) -> p t e", e=2),
+                pair_raw[i][:, :, t0:t1].rearrange("p e t -> p t e"),
             )
 
-        def pick_pair():
+        def pick_pair(b):
             nc.vector.tensor_copy(
-                pair_picked[:].rearrange("p (b t q r) -> p b q t r", b=2, t=4, r=8),
-                pair_words[:].bitcast(U32).indirect(offsets[:]),
+                pair_picked[b][:].rearrange("p (t q r) -> p q t r", t=4, r=8),
+                pair_words[:].bitcast(U32).indirect(offsets[:, 32 * b : 32 * (b + 1)]),
             )
 
         def turn_pair(b, bank):
-            words = pair_picked[:].bitcast(F32)
+            words = pair_picked[b][:].bitcast(F32)
             turned = banks.tile([P, 4, P], F32, name=f"bank{bank}")
             for t in range(4):
-                nc.tensor.transpose(turned[:, t, :], words[:, 512 * b + P * t : 512 * b + P * (t + 1)], ident[:])
+                nc.tensor.transpose(turned[:, t, :], words[:, P * t : P * (t + 1)], ident[:])
             nc.scalar.copy(
                 pair_grouped[:, S * b : S * (b + 1)].rearrange("p (n t) -> p n t", t=4),
                 turned[:].bitcast(BF16).rearrange("p t n -> p n t"),
@@ -209,7 +228,7 @@ def tile_list_listed_rating_autoencoder_kernel(tc, tab_words, tab_scales, offs, 
 
         def encode(b, t):
             col = slice(256 * t + P * b, 256 * t + P * (b + 1))
-            acc = banks.tile([P, M], F32, name=f"bank{4 * b + t}")
+            acc = banks.tile([P, M], F32, name=f"bank{(4 * b + t + 6) % 8}")
             for a in range(PASSES):
                 nc.tensor.matmul_mx(
                     out=acc[:], lhsT=v_codes[a, b][:, t, :].bitcast(FP8X4), lhsT_scale=v_plane[4 * a : P, col],
@@ -230,20 +249,25 @@ def tile_list_listed_rating_autoencoder_kernel(tc, tab_words, tab_scales, offs, 
         def quantise_h(b):
             nc.vector.quantize_mx(out=h_codes[b].bitcast(FP8X4), scales=h_plane[:, b, :], in_=h_grouped[b][:])
 
-        def decode(c, bank):
-            acc = banks.tile([P, M], F32, name=f"bank{bank}")
-            shortcut = [
-                (w4[c // 4][:, a, :].bitcast(U8)[:, 2 * P * (c % 4) : 2 * P * (c % 4 + 1)].bitcast(FP4X4), w4_plane[:, a, :].bitcast(U8)[:, P * c : P * (c + 1)],
-                 x_codes[:, a, :].bitcast(FP8X4), x_plane[:, a, :])
-                for a in range(PASSES)
-            ]
-            coded = [
-                (coded_wd[c, b][0], coded_wd[c, b][1], h_codes[b].bitcast(FP8X4), h_plane[:, b, :])
-                for b in range(PASSES)
-            ]
-            passes = shortcut + coded
-            for i, (lhsT, lhsT_scale, rhs, rhs_scale) in enumerate(passes):
-                nc.tensor.matmul_mx(out=acc[:], lhsT=lhsT, lhsT_scale=lhsT_scale, rhs=rhs, rhs_scale=rhs_scale, start=(i == 0), stop=(i == len(passes) - 1))
+        acc_of = {}
+
+        def shortcut(c, bank):
+            acc_of[c] = banks.tile([P, M], F32, name=f"bank{bank}")
+            for a in range(PASSES):
+                nc.tensor.matmul_mx(
+                    out=acc_of[c][:],
+                    lhsT=(w4[c // 4][:, a, :].bitcast(U8)[:, 2 * P * (c % 4) : 2 * P * (c % 4 + 1)].bitcast(FP4X4)),
+                    lhsT_scale=w4_plane[:, a, :].bitcast(U8)[:, P * c : P * (c + 1)],
+                    rhs=x_codes[:, a, :].bitcast(FP8X4), rhs_scale=x_plane[:, a, :], start=(a == 0), stop=False,
+                )
+
+        def decode(c):
+            acc = acc_of[c]
+            for b in range(PASSES):
+                nc.tensor.matmul_mx(
+                    out=acc[:], lhsT=coded_wd[c, b][0], lhsT_scale=coded_wd[c, b][1],
+                    rhs=h_codes[b].bitcast(FP8X4), rhs_scale=h_plane[:, b, :], start=False, stop=(b == PASSES - 1),
+                )
             parts = 2 if c == TILES - 1 else 1
             width = M // parts
             for part in range(parts):
@@ -257,7 +281,10 @@ def tile_list_listed_rating_autoencoder_kernel(tc, tab_words, tab_scales, offs, 
             for t in range(4):
                 encode(b, t)
                 gain(b, t)
+        for c in range(6):
+            shortcut(c, c)
         turn_wd(0, 0, 2, 6)
+        group_h(0, nc.scalar.copy)
         turn_wd(1, 0, 2, 7)
         after3 = mid.tile([P, 2 * M + 4 * 256], U32, name="after3", align_bytes=64, offset=8 * M)
         h_grouped[1] = mid.tile([P, 4 * M], BF16, name="h_grouped1", align_bytes=64, offset=0)
@@ -265,38 +292,40 @@ def tile_list_listed_rating_autoencoder_kernel(tc, tab_words, tab_scales, offs, 
             h_codes[b] = after3[:, M * b : M * (b + 1)]
         for c in range(4):
             wd_codes[c] = after3[:, 2 * M + 256 * c : 2 * M + 256 * (c + 1)]
+        group_h(1, nc.vector.tensor_copy)
         quantise_wd(0, 0, 2)
         quantise_wd(1, 0, 2)
-        group_h(0, nc.scalar.copy)
         turn_wd(2, 0, 2, 6)
         quantise_h(0)
-        quantise_wd(2, 0, 2)
-        group_h(1, nc.vector.tensor_copy)
         quantise_h(1)
+        quantise_wd(2, 0, 2)
         cast_pair(0, nc.scalar.copy)
         cast_pair(1, nc.scalar.copy)
         cast_pair(2, nc.scalar.copy)
         cast_pair(3, nc.scalar.copy)
-        pick_pair()
+        pick_pair(0)
+        pick_pair(1)
         turn_wd(3, 0, 2, 7)
         quantise_wd(3, 0, 2)
         rated_early = late.tile([P, 3, M], F32, name="rated_early", align_bytes=64, offset=2 * S)
         for c in range(3):
-            decode(c, c)
+            decode(c)
         turn_pair(0, 6)
         turn_pair(1, 7)
-        decode(3, 3)
+        decode(3)
+        shortcut(6, 0)
+        shortcut(7, 1)
         pick_wd(6, 0, 2)
         quantise_pair()
         turn_wd(6, 0, 2, 6)
         pick_wd(7, 0, 1)
         pick_wd(7, 1, 2)
-        decode(4, 4)
-        decode(5, 5)
+        decode(4)
+        decode(5)
         turn_wd(7, 0, 1, 7)
         turn_wd(7, 1, 2, 6)
         quantise_wd(6, 0, 2)
         quantise_wd(7, 0, 1)
         quantise_wd(7, 1, 2)
-        decode(6, 0)
-        decode(7, 1)
+        decode(6)
+        decode(7)

@@ -20,7 +20,7 @@ P = 128
 PASSES = 2
 TILES = N // P
 CHUNK = 512
-X_SPLIT = 76
+X_SPLIT = (72, 44)
 ALU = mybir.AluOpType
 
 
@@ -38,7 +38,9 @@ def tile_list_listed_rating_autoencoder_kernel(tc, tab_words, tab_scales, offs, 
 
         tab_plane = keep.tile([P, T // 4], I32, name="tab_plane", align_bytes=64)
         w4_plane = keep.tile([P, PASSES, N // 4], I32, name="w4_plane", align_bytes=64)
-        rows = keep.tile([P, PASSES * P], F32, name="rows")
+        rows = keep.tile([P, 4 * P], F32, name="rows")
+        g_rows = keep.tile([PASSES, 4 * P], F32, name="g_rows")
+        nc.sync.dma_start(g_rows[:], g.rearrange("(b j) -> b j", b=PASSES))
         nc.gpsimd.memset(tab_plane[:], 0)
         warm_in = keep.tile([P, 1], F32, name="warm_in")
         warm_out = keep.tile([P, 1], F32, name="warm_out")
@@ -77,14 +79,12 @@ def tile_list_listed_rating_autoencoder_kernel(tc, tab_words, tab_scales, offs, 
         def load_pair(i):
             nc.sync.dma_start(pair_raw[i][:], pair_rows[:, :, CHUNK * i : CHUNK * (i + 1)])
 
-        load_table(0, 0, T // 2)
         for quad in range(4):
             nc.sync.dma_start(tab_plane[32 * quad : 32 * quad + 8, :], tab_scales[:, 4 * quad : 4 * quad + 4, :].bitcast(I32))
-        load_table(0, T // 2, T)
+        load_table(0, 0, T)
+        nc.sync.dma_start(rows[8:16, 0:P], bo.rearrange("(c p) -> c p", p=P))
         load_x(0)
         load_x(1)
-        nc.sync.dma_start(rows[0:4, :].rearrange("t (b r) -> t b r", r=8), g.rearrange("(b t r) -> t b r", t=4, r=8))
-        nc.sync.dma_start(rows[8:16, 0:P], bo.rearrange("(c p) -> c p", p=P))
         load_table(1, 0, T)
         load_wd(0)
         load_wd(1)
@@ -99,6 +99,13 @@ def tile_list_listed_rating_autoencoder_kernel(tc, tab_words, tab_scales, offs, 
         load_shortcut(1)
         load_wd(6)
         load_wd(7)
+
+        cols = keep.tile([P, 4, 16], F32, name="cols")
+        cols_ps = banks.tile([P, 4, P], F32, name="bank5")
+        nc.scalar.copy(rows[0:PASSES, :].rearrange("b (t q r) -> b t q r", t=4, r=8), g_rows[:].rearrange("b (q t r) -> b t q r", t=4, r=8))
+        for t in range(4):
+            nc.tensor.transpose(cols_ps[:, t, :], rows[:, P * t : P * (t + 1)], ident[:])
+        nc.scalar.copy(cols[:], cols_ps[:, :, 0:16])
 
         v_plane = keep.tile([P, S], U8, name="v_plane", align_bytes=64)
         listed_plane = keep.tile([P, S], U8, name="listed_plane", align_bytes=64)
@@ -131,19 +138,12 @@ def tile_list_listed_rating_autoencoder_kernel(tc, tab_words, tab_scales, offs, 
             v_plane[:].bitcast(I32).rearrange("p (t b w) -> p t b w", t=4, w=2),
             listed_plane[:].bitcast(I32).rearrange("p (b t w) -> p t b w", t=4, w=2),
         )
-        cast_x(nc.scalar.copy, 0, 0, 128)
-        quantise_x(0, 0, M)
-        cast_x(nc.scalar.copy, 1, 0, X_SPLIT)
-        cast_x(nc.vector.tensor_copy, 1, X_SPLIT, 128)
-        quantise_x(1, 0, M)
+        for a in range(PASSES):
+            cast_x(nc.scalar.copy, a, 0, X_SPLIT[a])
+            cast_x(nc.vector.tensor_copy, a, X_SPLIT[a], M // 4)
+            quantise_x(a, 0, M)
         pick_table(1, 0, 1, "v_codes1a")
         pick_table(1, 1, 2, "v_codes1b")
-
-        cols = keep.tile([P, PASSES, 16], F32, name="cols")
-        cols_ps = banks.tile([P, 4, P], F32, name="bank5")
-        for b in range(PASSES):
-            nc.tensor.transpose(cols_ps[:, b, :], rows[:, P * b : P * (b + 1)], ident[:])
-        nc.scalar.copy(cols[:], cols_ps[:, 0:PASSES, 0:16])
 
         wd_codes = {}
         wd_plane = {c: keep.tile([P, PASSES * P], U8, name=f"wd_plane{c}", align_bytes=64) for c in (0, 1, 2, 3, 6, 7)}
@@ -238,7 +238,7 @@ def tile_list_listed_rating_autoencoder_kernel(tc, tab_words, tab_scales, offs, 
 
         def gain(b, t):
             pairs = h_rows[b][:].rearrange("p (u m e) -> p u m e", u=2, e=2)
-            nc.gpsimd.tensor_scalar(pairs[:, t // 2, :, t % 2], sig[b][:, t, :], cols[:, b, t : t + 1], 0.0, ALU.mult, ALU.add)
+            nc.gpsimd.tensor_scalar(pairs[:, t // 2, :, t % 2], sig[b][:, t, :], cols[:, t, b : b + 1], 0.0, ALU.mult, ALU.add)
 
         def group_h(b, engine_copy):
             engine_copy(
@@ -292,13 +292,13 @@ def tile_list_listed_rating_autoencoder_kernel(tc, tab_words, tab_scales, offs, 
             h_codes[b] = after3[:, M * b : M * (b + 1)]
         for c in range(4):
             wd_codes[c] = after3[:, 2 * M + 256 * c : 2 * M + 256 * (c + 1)]
-        group_h(1, nc.vector.tensor_copy)
         quantise_wd(0, 0, 2)
         quantise_wd(1, 0, 2)
         turn_wd(2, 0, 2, 6)
         quantise_h(0)
-        quantise_h(1)
+        group_h(1, nc.vector.tensor_copy)
         quantise_wd(2, 0, 2)
+        quantise_h(1)
         cast_pair(0, nc.scalar.copy)
         cast_pair(1, nc.scalar.copy)
         cast_pair(2, nc.scalar.copy)

@@ -40,8 +40,10 @@ def tile_list_listed_rating_autoencoder_kernel(tc, tab_words, tab_scales, offs, 
         w4_plane = keep.tile([P, PASSES, N // 4], I32, name="w4_plane", align_bytes=64)
         rows = keep.tile([P, 4 * P], F32, name="rows")
         g_rows = keep.tile([PASSES, 4 * P], F32, name="g_rows")
-        nc.sync.dma_start(g_rows[:], g.rearrange("(b j) -> b j", b=PASSES))
-        nc.gpsimd.memset(tab_plane[:], 0)
+        for a in range(PASSES):
+            nc.sync.dma_start(tab_plane[16 * a : 16 * (a + 1), :], tab_scales[a].bitcast(I32).rearrange("(quad r) w -> r quad w", r=4))
+        nc.gpsimd.memset(tab_plane[32:64, :], 0)
+        nc.vector.memset(tab_plane[64:P, :], 0)
         warm_in = keep.tile([P, 1], F32, name="warm_in")
         warm_out = keep.tile([P, 1], F32, name="warm_out")
         nc.vector.memset(warm_in[:], 0.0)
@@ -79,12 +81,23 @@ def tile_list_listed_rating_autoencoder_kernel(tc, tab_words, tab_scales, offs, 
         def load_pair(i):
             nc.sync.dma_start(pair_raw[i][:], pair_rows[:, :, CHUNK * i : CHUNK * (i + 1)])
 
-        for quad in range(4):
-            nc.sync.dma_start(tab_plane[32 * quad : 32 * quad + 8, :], tab_scales[:, 4 * quad : 4 * quad + 4, :].bitcast(I32))
         load_table(0, 0, T)
-        nc.sync.dma_start(rows[8:16, 0:P], bo.rearrange("(c p) -> c p", p=P))
+        nc.sync.dma_start(g_rows[:], g.rearrange("(b j) -> b j", b=PASSES))
         load_x(0)
         load_x(1)
+
+        v_plane = keep.tile([P, S // 4], I32, name="v_plane", align_bytes=64)
+        listed_plane = keep.tile([P, S], U8, name="listed_plane", align_bytes=64)
+        ordered_plane = keep.tile([P, S // 4], I32, name="ordered_plane", align_bytes=64)
+        nc.gpsimd.memset(v_plane[:], 0)
+        nc.vector.tensor_copy(listed_plane[:], tab_plane[:].bitcast(U8).indirect(offsets[:]))
+        nc.vector.tensor_copy(
+            ordered_plane[:].rearrange("p (t b w) -> p t b w", t=4, w=2),
+            listed_plane[:].bitcast(I32).rearrange("p (b t w) -> p t b w", t=4, w=2),
+        )
+        for quad in range(4):
+            nc.sync.dma_start(v_plane[32 * quad : 32 * quad + 8, :], ordered_plane[quad:32:4, :])
+        nc.sync.dma_start(rows[8:16, 0:P], bo.rearrange("(c p) -> c p", p=P))
         load_table(1, 0, T)
         load_wd(0)
         load_wd(1)
@@ -106,9 +119,6 @@ def tile_list_listed_rating_autoencoder_kernel(tc, tab_words, tab_scales, offs, 
         for t in range(4):
             nc.tensor.transpose(cols_ps[:, t, :], rows[:, P * t : P * (t + 1)], ident[:])
         nc.scalar.copy(cols[:], cols_ps[:, :, 0:16])
-
-        v_plane = keep.tile([P, S], U8, name="v_plane", align_bytes=64)
-        listed_plane = keep.tile([P, S], U8, name="listed_plane", align_bytes=64)
 
         x_codes = keep.tile([P, PASSES, M], U32, name="x_codes", align_bytes=64)
         x_plane = keep.tile([P, PASSES, M], U8, name="x_plane", align_bytes=64)
@@ -132,12 +142,7 @@ def tile_list_listed_rating_autoencoder_kernel(tc, tab_words, tab_scales, offs, 
             for b in range(b0, b1):
                 v_codes[a, b] = codes[:, :, P * (b - b0) : P * (b - b0 + 1)]
 
-        nc.vector.tensor_copy(listed_plane[:], tab_plane[:].bitcast(U8).indirect(offsets[:]))
         pick_table(0, 0, 2, "v_codes0")
-        nc.vector.tensor_copy(
-            v_plane[:].bitcast(I32).rearrange("p (t b w) -> p t b w", t=4, w=2),
-            listed_plane[:].bitcast(I32).rearrange("p (b t w) -> p t b w", t=4, w=2),
-        )
         for a in range(PASSES):
             cast_x(nc.scalar.copy, a, 0, X_SPLIT[a])
             cast_x(nc.vector.tensor_copy, a, X_SPLIT[a], M // 4)
@@ -231,7 +236,7 @@ def tile_list_listed_rating_autoencoder_kernel(tc, tab_words, tab_scales, offs, 
             acc = banks.tile([P, M], F32, name=f"bank{(4 * b + t + 6) % 8}")
             for a in range(PASSES):
                 nc.tensor.matmul_mx(
-                    out=acc[:], lhsT=v_codes[a, b][:, t, :].bitcast(FP8X4), lhsT_scale=v_plane[4 * a : P, col],
+                    out=acc[:], lhsT=v_codes[a, b][:, t, :].bitcast(FP8X4), lhsT_scale=v_plane[:].bitcast(U8)[4 * a : P, col],
                     rhs=x_codes[:, a, :].bitcast(FP8X4), rhs_scale=x_plane[:, a, :], start=(a == 0), stop=(a == PASSES - 1),
                 )
             nc.scalar.activation(sig[b][:, t, :], acc[:], ACT.Sigmoid)

@@ -92,8 +92,8 @@ def tile_list_listed_rating_autoencoder_kernel(tc, tab_words, tab_scales, offs, 
         nc.gpsimd.memset(v_plane[:], 0)
         nc.vector.tensor_copy(listed_plane[:], tab_plane[:].bitcast(U8).indirect(offsets[:]))
         nc.vector.tensor_copy(
-            ordered_plane[:].rearrange("p (t b w) -> p t b w", t=4, w=2),
-            listed_plane[:].bitcast(I32).rearrange("p (b t w) -> p t b w", t=4, w=2),
+            ordered_plane[:].rearrange("p (t c) -> p t c", t=4),
+            listed_plane[:].bitcast(I32).rearrange("p (c t) -> p t c", t=4),
         )
         for quad in range(4):
             nc.sync.dma_start(v_plane[32 * quad : 32 * quad + 8, :], ordered_plane[quad:32:4, :])
@@ -115,7 +115,7 @@ def tile_list_listed_rating_autoencoder_kernel(tc, tab_words, tab_scales, offs, 
 
         cols = keep.tile([P, 4, 16], F32, name="cols")
         cols_ps = banks.tile([P, 4, P], F32, name="bank5")
-        nc.scalar.copy(rows[0:PASSES, :].rearrange("b (t q r) -> b t q r", t=4, r=8), g_rows[:].rearrange("b (q t r) -> b t q r", t=4, r=8))
+        nc.scalar.copy(rows[0:PASSES, :].rearrange("b (t c l) -> b t c l", t=4, l=4), g_rows[:].rearrange("b (c t l) -> b t c l", t=4, l=4))
         for t in range(4):
             nc.tensor.transpose(cols_ps[:, t, :], rows[:, P * t : P * (t + 1)], ident[:])
         nc.scalar.copy(cols[:], cols_ps[:, :, 0:16])
@@ -136,7 +136,7 @@ def tile_list_listed_rating_autoencoder_kernel(tc, tab_words, tab_scales, offs, 
         def pick_table(a, b0, b1, home):
             codes = keep.tile([P, 4, P * (b1 - b0)], U32, name=home, align_bytes=64)
             nc.vector.tensor_copy(
-                codes[:].rearrange("p t (b r) -> p b t r", r=8),
+                codes[:].rearrange("p t (c l) -> p c t l", l=4),
                 tab[a][:].bitcast(U32).indirect(offsets[:, 32 * b0 : 32 * b1]),
             )
             for b in range(b0, b1):
@@ -163,7 +163,7 @@ def tile_list_listed_rating_autoencoder_kernel(tc, tab_words, tab_scales, offs, 
         def pick_wd(c, b0, b1):
             picked[c, b0] = keep.tile([P, 512 * (b1 - b0)], BF16, name=home.get((c, b0), f"picked{c}_{b0}"), align_bytes=64)
             nc.vector.tensor_copy(
-                picked[c, b0][:].rearrange("p (u b r e) -> p b u e r", u=2, r=8, e=2),
+                picked[c, b0][:].rearrange("p (u c l e) -> p c u e l", u=2, l=4, e=2),
                 wd[c][:].indirect(offsets[:, 32 * b0 : 32 * b1]),
             )
 
@@ -203,7 +203,7 @@ def tile_list_listed_rating_autoencoder_kernel(tc, tab_words, tab_scales, offs, 
 
         def pick_pair(b):
             nc.vector.tensor_copy(
-                pair_picked[b][:].rearrange("p (t q r) -> p q t r", t=4, r=8),
+                pair_picked[b][:].rearrange("p (t c l) -> p c t l", t=4, l=4),
                 pair_words[:].bitcast(U32).indirect(offsets[:, 32 * b : 32 * (b + 1)]),
             )
 

@@ -19,7 +19,8 @@ ACT = mybir.ActivationFunctionType
 P = 128
 PASSES = 2
 TILES = N // P
-CHUNK = 512
+CHUNKS = (256, 768, 768, 256)
+CHUNK_START = [sum(CHUNKS[:i]) for i in range(len(CHUNKS) + 1)]
 X_SPLIT = (72, 44)
 ALU = mybir.AluOpType
 
@@ -38,7 +39,7 @@ def tile_list_listed_rating_autoencoder_kernel(tc, tab_words, tab_scales, offs, 
 
         tab_plane = keep.tile([P, T // 4], I32, name="tab_plane", align_bytes=64)
         w4_plane = keep.tile([P, PASSES, N // 4], I32, name="w4_plane", align_bytes=64)
-        rows = keep.tile([P, 4 * P], F32, name="rows")
+        rows = keep.tile([P, 5 * P], F32, name="rows")
         g_rows = keep.tile([PASSES, 4 * P], F32, name="g_rows")
         for a in range(PASSES):
             nc.sync.dma_start(tab_plane[16 * a : 16 * (a + 1), :], tab_scales[a].bitcast(I32).rearrange("(quad r) w -> r quad w", r=4))
@@ -58,8 +59,8 @@ def tile_list_listed_rating_autoencoder_kernel(tc, tab_words, tab_scales, offs, 
         wd = {c: keep.tile([P, T], F32, name=f"wd{c}", align_bytes=64) for c in (0, 1, 2, 6, 7)}
         wd[3] = mid.tile([P, T], F32, name="wd3", align_bytes=64, offset=0)
         w4 = [keep.tile([P, PASSES, N // 4], I32, name=f"w4_{half}", align_bytes=64) for half in range(2)]
-        pair_raw = [keep.tile([P, 2, CHUNK], F32, name=f"pair_raw{i}", align_bytes=64) for i in range(T // CHUNK - 1)]
-        pair_raw.append(late.tile([P, 2, CHUNK], F32, name="pair_raw_last", align_bytes=64, offset=0))
+        pair_raw = [keep.tile([P, 2, CHUNKS[i]], F32, name=f"pair_raw{i}", align_bytes=64) for i in range(len(CHUNKS) - 1)]
+        pair_raw.append(late.tile([P, 2, CHUNKS[-1]], F32, name="pair_raw_last", align_bytes=64, offset=2 * S - 64))
         pair_rows = wdT[4 * P : 6 * P, :].rearrange("(p e) t -> p e t", e=2)
 
         def load_table(a, t0, t1):
@@ -79,12 +80,13 @@ def tile_list_listed_rating_autoencoder_kernel(tc, tab_words, tab_scales, offs, 
                 nc.sync.dma_start(w4_plane[32 * quad : 32 * quad + 4, :, :], w4_scales[:, 4 * quad : 4 * quad + 4, :].bitcast(I32).rearrange("a r w -> r a w"))
 
         def load_pair(i):
-            nc.sync.dma_start(pair_raw[i][:], pair_rows[:, :, CHUNK * i : CHUNK * (i + 1)])
+            nc.sync.dma_start(pair_raw[i][:], pair_rows[:, :, CHUNK_START[i] : CHUNK_START[i + 1]])
 
         load_table(0, 0, T)
-        nc.sync.dma_start(g_rows[:], g.rearrange("(b j) -> b j", b=PASSES))
         load_x(0)
+        nc.sync.dma_start(g_rows[:], g.rearrange("(b j) -> b j", b=PASSES))
         load_x(1)
+        load_table(1, 0, T)
 
         v_plane = keep.tile([P, S // 4], I32, name="v_plane", align_bytes=64)
         listed_plane = keep.tile([P, S], U8, name="listed_plane", align_bytes=64)
@@ -97,28 +99,27 @@ def tile_list_listed_rating_autoencoder_kernel(tc, tab_words, tab_scales, offs, 
         )
         for quad in range(4):
             nc.sync.dma_start(v_plane[32 * quad : 32 * quad + 8, :], ordered_plane[quad:32:4, :])
-        nc.sync.dma_start(rows[8:16, 0:P], bo.rearrange("(c p) -> c p", p=P))
-        load_table(1, 0, T)
         load_wd(0)
         load_wd(1)
+        nc.sync.dma_start(rows[0:TILES, 4 * P : 5 * P], bo.rearrange("(c p) -> c p", p=P))
         load_wd(2)
         load_pair(0)
         load_wd(3)
-        load_shortcut_scales()
-        load_shortcut(0)
         load_pair(1)
         load_pair(2)
+        load_shortcut_scales()
+        load_shortcut(0)
         load_pair(3)
         load_shortcut(1)
         load_wd(6)
         load_wd(7)
 
-        cols = keep.tile([P, 4, 16], F32, name="cols")
+        cols = keep.tile([P, 4, PASSES], F32, name="cols")
         cols_ps = banks.tile([P, 4, P], F32, name="bank5")
-        nc.scalar.copy(rows[0:PASSES, :].rearrange("b (t c l) -> b t c l", t=4, l=4), g_rows[:].rearrange("b (c t l) -> b t c l", t=4, l=4))
+        nc.scalar.copy(rows[0:PASSES, 0 : 4 * P].rearrange("b (t c l) -> b t c l", t=4, l=4), g_rows[:].rearrange("b (c t l) -> b t c l", t=4, l=4))
         for t in range(4):
             nc.tensor.transpose(cols_ps[:, t, :], rows[:, P * t : P * (t + 1)], ident[:])
-        nc.scalar.copy(cols[:], cols_ps[:, :, 0:16])
+        nc.scalar.copy(cols[:], cols_ps[:, :, 0:PASSES])
 
         x_codes = keep.tile([P, PASSES, M], U32, name="x_codes", align_bytes=64)
         x_plane = keep.tile([P, PASSES, M], U8, name="x_plane", align_bytes=64)
@@ -157,7 +158,7 @@ def tile_list_listed_rating_autoencoder_kernel(tc, tab_words, tab_scales, offs, 
         grouped = {}
         grouped_home = {}
         home = {(7, 1): "pair_grouped"}
-        codes_home = {6: "wd7"}
+        codes_home = {}
         h_codes = {}
 
         def pick_wd(c, b0, b1):
@@ -167,7 +168,7 @@ def tile_list_listed_rating_autoencoder_kernel(tc, tab_words, tab_scales, offs, 
                 wd[c][:].indirect(offsets[:, 32 * b0 : 32 * b1]),
             )
 
-        def turn_wd(c, b0, b1, bank):
+        def turn_wd(c, b0, b1, bank, engine_copy=nc.scalar.copy):
             words = picked[c, b0][:].bitcast(F32)
             if c == 3:
                 grouped[c] = late.tile([P, S], BF16, name="grouped3", align_bytes=64, offset=0)
@@ -178,7 +179,7 @@ def tile_list_listed_rating_autoencoder_kernel(tc, tab_words, tab_scales, offs, 
                 for u in range(2):
                     s = (b1 - b0) * u + b - b0
                     nc.tensor.transpose(turned[:, 2 * u + b, :], words[:, P * s : P * (s + 1)], ident[:])
-            nc.scalar.copy(
+            engine_copy(
                 grouped[c][:].bitcast(F32).rearrange("p (b n u) -> p b n u", b=2, u=2)[:, b0:b1],
                 turned[:].rearrange("p (u b) n -> p b n u", u=2)[:, b0:b1],
             )
@@ -195,10 +196,10 @@ def tile_list_listed_rating_autoencoder_kernel(tc, tab_words, tab_scales, offs, 
         pair_grouped = keep.tile([P, 2 * S], BF16, name="pair_grouped", align_bytes=64)
         pair_plane = keep.tile([P, PASSES * 2 * P], U8, name="pair_plane", align_bytes=64)
 
-        def cast_pair(i, engine_copy, t0=0, t1=CHUNK):
+        def cast_pair(i, engine_copy):
             engine_copy(
-                pair_words[:, 2 * (CHUNK * i + t0) : 2 * (CHUNK * i + t1)].rearrange("p (t e) -> p t e", e=2),
-                pair_raw[i][:, :, t0:t1].rearrange("p e t -> p t e"),
+                pair_words[:, 2 * CHUNK_START[i] : 2 * CHUNK_START[i + 1]].rearrange("p (t e) -> p t e", e=2),
+                pair_raw[i][:].rearrange("p e t -> p t e"),
             )
 
         def pick_pair(b):
@@ -256,28 +257,35 @@ def tile_list_listed_rating_autoencoder_kernel(tc, tab_words, tab_scales, offs, 
 
         acc_of = {}
 
-        def shortcut(c, bank):
-            acc_of[c] = banks.tile([P, M], F32, name=f"bank{bank}")
+        def shortcut(c, first):
+            if first:
+                acc_of[c] = banks.tile([P, M], F32, name=f"bank{c % 6}")
             for a in range(PASSES):
                 nc.tensor.matmul_mx(
                     out=acc_of[c][:],
-                    lhsT=(w4[c // 4][:, a, :].bitcast(U8)[:, 2 * P * (c % 4) : 2 * P * (c % 4 + 1)].bitcast(FP4X4)),
+                    lhsT=w4[c // 4][:, a, :].bitcast(U8)[:, 2 * P * (c % 4) : 2 * P * (c % 4 + 1)].bitcast(FP4X4),
                     lhsT_scale=w4_plane[:, a, :].bitcast(U8)[:, P * c : P * (c + 1)],
-                    rhs=x_codes[:, a, :].bitcast(FP8X4), rhs_scale=x_plane[:, a, :], start=(a == 0), stop=False,
+                    rhs=x_codes[:, a, :].bitcast(FP8X4), rhs_scale=x_plane[:, a, :],
+                    start=(first and a == 0), stop=(not first and a == PASSES - 1),
                 )
 
-        def decode(c):
-            acc = acc_of[c]
+        def decode(c, first):
+            if first:
+                acc_of[c] = banks.tile([P, M], F32, name=f"bank{c % 6}")
             for b in range(PASSES):
                 nc.tensor.matmul_mx(
-                    out=acc[:], lhsT=coded_wd[c, b][0], lhsT_scale=coded_wd[c, b][1],
-                    rhs=h_codes[b].bitcast(FP8X4), rhs_scale=h_plane[:, b, :], start=False, stop=(b == PASSES - 1),
+                    out=acc_of[c][:], lhsT=coded_wd[c, b][0], lhsT_scale=coded_wd[c, b][1],
+                    rhs=h_codes[b].bitcast(FP8X4), rhs_scale=h_plane[:, b, :],
+                    start=(first and b == 0), stop=(not first and b == PASSES - 1),
                 )
+
+        def rate(c):
+            acc = acc_of[c]
             parts = 2 if c == TILES - 1 else 1
             width = M // parts
             for part in range(parts):
                 rated = rated_early[:, c, :] if c < 3 else ring.tile([P, width], F32, name="rated")[:]
-                nc.scalar.activation(rated, acc[:, width * part : width * (part + 1)], ACT.Tanh, bias=cols[:, 0, 8 + c : 9 + c])
+                nc.scalar.activation(rated, acc[:, width * part : width * (part + 1)], ACT.Tanh, bias=bias[:, c : c + 1])
                 nc.sync.dma_start(out[P * c : P * (c + 1), width * part : width * (part + 1)], rated)
 
         for c in range(4):
@@ -286,8 +294,10 @@ def tile_list_listed_rating_autoencoder_kernel(tc, tab_words, tab_scales, offs, 
             for t in range(4):
                 encode(b, t)
                 gain(b, t)
-        for c in range(6):
-            shortcut(c, c)
+        bias = keep.tile([P, TILES], F32, name="bias")
+        bias_ps = banks.tile([P, P], F32, name="bank5")
+        nc.tensor.transpose(bias_ps[:], rows[:, 4 * P : 5 * P], ident[:])
+        nc.scalar.copy(bias[:], bias_ps[:, 0:TILES])
         turn_wd(0, 0, 2, 6)
         group_h(0, nc.scalar.copy)
         turn_wd(1, 0, 2, 7)
@@ -314,23 +324,29 @@ def tile_list_listed_rating_autoencoder_kernel(tc, tab_words, tab_scales, offs, 
         quantise_wd(3, 0, 2)
         rated_early = late.tile([P, 3, M], F32, name="rated_early", align_bytes=64, offset=2 * S)
         for c in range(3):
-            decode(c)
+            decode(c, True)
+            shortcut(c, False)
+            rate(c)
         turn_pair(0, 6)
         turn_pair(1, 7)
-        decode(3)
-        shortcut(6, 0)
-        shortcut(7, 1)
+        shortcut(3, True)
+        decode(3, False)
+        rate(3)
         pick_wd(6, 0, 2)
-        quantise_pair()
         turn_wd(6, 0, 2, 6)
+        for c in range(4, TILES):
+            shortcut(c, True)
+        quantise_pair()
         pick_wd(7, 0, 1)
-        pick_wd(7, 1, 2)
-        decode(4)
-        decode(5)
-        turn_wd(7, 0, 1, 7)
-        turn_wd(7, 1, 2, 6)
         quantise_wd(6, 0, 2)
+        pick_wd(7, 1, 2)
+        for c in (4, 5):
+            decode(c, False)
+            rate(c)
+        turn_wd(7, 0, 1, 7)
         quantise_wd(7, 0, 1)
+        turn_wd(7, 1, 2, 6, nc.vector.tensor_copy)
         quantise_wd(7, 1, 2)
-        decode(6)
-        decode(7)
+        for c in (6, 7):
+            decode(c, False)
+            rate(c)

@@ -15,14 +15,19 @@ U8 = mybir.dt.uint8
 FP8X4 = mybir.dt.float8_e4m3fn_x4
 FP4X4 = mybir.dt.float4_e2m1fn_x4
 ACT = mybir.ActivationFunctionType
+ALU = mybir.AluOpType
 
 P = 128
+PASS = 4 * P
 PASSES = 2
 TILES = N // P
+PAIR = (4, 5)
+SINGLES = (0, 1, 2, 3, 6, 7)
+EARLY = 3
+SUM_BANKS = 6
 CHUNKS = (256, 768, 768, 256)
 CHUNK_START = [sum(CHUNKS[:i]) for i in range(len(CHUNKS) + 1)]
-X_SPLIT = (72, 44)
-ALU = mybir.AluOpType
+X_ON_SCALAR = (72, 44)
 
 
 def tile_list_listed_rating_autoencoder_kernel(tc, tab_words, tab_scales, offs, x, w4_words, w4_scales, wdT, g, bo, out):
@@ -30,8 +35,8 @@ def tile_list_listed_rating_autoencoder_kernel(tc, tab_words, tab_scales, offs, 
     with ExitStack() as ctx:
         keep = ctx.enter_context(tc.tile_pool(name="keep", bufs=1))
         ring = ctx.enter_context(tc.tile_pool(name="ring", bufs=6))
-        late = ctx.enter_context(tc.tile_pool(name="late", bufs=1))
-        mid = ctx.enter_context(tc.tile_pool(name="mid", bufs=1))
+        on_last_chunk = ctx.enter_context(tc.tile_pool(name="late", bufs=1))
+        on_wd3 = ctx.enter_context(tc.tile_pool(name="mid", bufs=1))
         banks = ctx.enter_context(tc.psum_pool(name="banks", bufs=1))
 
         offsets = keep.tile([P, S // 16], U16, name="offsets")
@@ -40,15 +45,11 @@ def tile_list_listed_rating_autoencoder_kernel(tc, tab_words, tab_scales, offs, 
         tab_plane = keep.tile([P, T // 4], I32, name="tab_plane", align_bytes=64)
         w4_plane = keep.tile([P, PASSES, N // 4], I32, name="w4_plane", align_bytes=64)
         rows = keep.tile([P, 5 * P], F32, name="rows")
-        g_rows = keep.tile([PASSES, 4 * P], F32, name="g_rows")
+        g_rows = keep.tile([PASSES, PASS], F32, name="g_rows")
         for a in range(PASSES):
             nc.sync.dma_start(tab_plane[16 * a : 16 * (a + 1), :], tab_scales[a].bitcast(I32).rearrange("(quad r) w -> r quad w", r=4))
         nc.gpsimd.memset(tab_plane[32:64, :], 0)
         nc.vector.memset(tab_plane[64:P, :], 0)
-        warm_in = keep.tile([P, 1], F32, name="warm_in")
-        warm_out = keep.tile([P, 1], F32, name="warm_out")
-        nc.vector.memset(warm_in[:], 0.0)
-        nc.scalar.activation(warm_out[:], warm_in[:], ACT.Sigmoid)
         nc.vector.memset(rows[:], 0.0)
         nc.vector.memset(w4_plane[:], 0)
         ident = keep.tile([P, P], F32, name="ident")
@@ -56,18 +57,18 @@ def tile_list_listed_rating_autoencoder_kernel(tc, tab_words, tab_scales, offs, 
 
         x_raw = [keep.tile([P, 4, M], F32, name=f"x_raw{a}") for a in range(PASSES)]
         tab = [keep.tile([P, T], I32, name=f"tab{a}") for a in range(PASSES)]
-        wd = {c: keep.tile([P, T], F32, name=f"wd{c}", align_bytes=64) for c in (0, 1, 2, 6, 7)}
-        wd[3] = mid.tile([P, T], F32, name="wd3", align_bytes=64, offset=0)
+        wd = {c: keep.tile([P, T], F32, name=f"wd{c}", align_bytes=64) for c in SINGLES if c != 3}
+        wd[3] = on_wd3.tile([P, T], F32, name="wd3", align_bytes=64, offset=0)
         w4 = [keep.tile([P, PASSES, N // 4], I32, name=f"w4_{half}", align_bytes=64) for half in range(2)]
         pair_raw = [keep.tile([P, 2, CHUNKS[i]], F32, name=f"pair_raw{i}", align_bytes=64) for i in range(len(CHUNKS) - 1)]
-        pair_raw.append(late.tile([P, 2, CHUNKS[-1]], F32, name="pair_raw_last", align_bytes=64, offset=2 * S - 64))
-        pair_rows = wdT[4 * P : 6 * P, :].rearrange("(p e) t -> p e t", e=2)
+        pair_raw.append(on_last_chunk.tile([P, 2, CHUNKS[-1]], F32, name="pair_raw_last", align_bytes=64, offset=2 * S - 64))
+        pair_rows = wdT[PAIR[0] * P : (PAIR[1] + 1) * P, :].rearrange("(p e) col -> p e col", e=2)
 
-        def load_table(a, t0, t1):
-            nc.sync.dma_start(tab[a][:, t0:t1], tab_words[a].rearrange("p t i -> p (t i)").bitcast(I32)[:, t0:t1])
+        def load_table(a):
+            nc.sync.dma_start(tab[a][:], tab_words[a].rearrange("p col t -> p (col t)").bitcast(I32))
 
         def load_x(a):
-            nc.sync.dma_start(x_raw[a][:], x[512 * a : 512 * (a + 1), :].rearrange("(p i) m -> p i m", i=4))
+            nc.sync.dma_start(x_raw[a][:], x[PASS * a : PASS * (a + 1), :].rearrange("(p t) m -> p t m", t=4))
 
         def load_wd(c):
             nc.sync.dma_start(wd[c][:], wdT[P * c : P * (c + 1), :])
@@ -82,11 +83,11 @@ def tile_list_listed_rating_autoencoder_kernel(tc, tab_words, tab_scales, offs, 
         def load_pair(i):
             nc.sync.dma_start(pair_raw[i][:], pair_rows[:, :, CHUNK_START[i] : CHUNK_START[i + 1]])
 
-        load_table(0, 0, T)
+        load_table(0)
         load_x(0)
         nc.sync.dma_start(g_rows[:], g.rearrange("(b j) -> b j", b=PASSES))
         load_x(1)
-        load_table(1, 0, T)
+        load_table(1)
 
         v_plane = keep.tile([P, S // 4], I32, name="v_plane", align_bytes=64)
         listed_plane = keep.tile([P, S], U8, name="listed_plane", align_bytes=64)
@@ -94,14 +95,15 @@ def tile_list_listed_rating_autoencoder_kernel(tc, tab_words, tab_scales, offs, 
         nc.gpsimd.memset(v_plane[:], 0)
         nc.vector.tensor_copy(listed_plane[:], tab_plane[:].bitcast(U8).indirect(offsets[:]))
         nc.vector.tensor_copy(
-            ordered_plane[:].rearrange("p (t c) -> p t c", t=4),
-            listed_plane[:].bitcast(I32).rearrange("p (c t) -> p t c", t=4),
+            ordered_plane[:].rearrange("p (t d) -> p t d", t=4),
+            listed_plane[:].bitcast(I32).rearrange("p (d t) -> p t d", t=4),
         )
         for quad in range(4):
             nc.sync.dma_start(v_plane[32 * quad : 32 * quad + 8, :], ordered_plane[quad:32:4, :])
+
         load_wd(0)
         load_wd(1)
-        nc.sync.dma_start(rows[0:TILES, 4 * P : 5 * P], bo.rearrange("(c p) -> c p", p=P))
+        nc.sync.dma_start(rows[0:TILES, PASS : PASS + P], bo.rearrange("(c p) -> c p", p=P))
         load_wd(2)
         load_pair(0)
         load_wd(3)
@@ -114,97 +116,84 @@ def tile_list_listed_rating_autoencoder_kernel(tc, tab_words, tab_scales, offs, 
         load_wd(6)
         load_wd(7)
 
-        cols = keep.tile([P, 4, PASSES], F32, name="cols")
-        cols_ps = banks.tile([P, 4, P], F32, name="bank5")
-        nc.scalar.copy(rows[0:PASSES, 0 : 4 * P].rearrange("b (t c l) -> b t c l", t=4, l=4), g_rows[:].rearrange("b (c t l) -> b t c l", t=4, l=4))
+        gains = keep.tile([P, 4, PASSES], F32, name="gains")
+        gains_ps = banks.tile([P, 4, P], F32, name="bank5")
+        nc.scalar.copy(rows[0:PASSES, 0:PASS].rearrange("b (t d l) -> b t d l", t=4, l=4), g_rows[:].rearrange("b (d t l) -> b t d l", t=4, l=4))
         for t in range(4):
-            nc.tensor.transpose(cols_ps[:, t, :], rows[:, P * t : P * (t + 1)], ident[:])
-        nc.scalar.copy(cols[:], cols_ps[:, :, 0:PASSES])
+            nc.tensor.transpose(gains_ps[:, t, :], rows[:, P * t : P * (t + 1)], ident[:])
+        nc.scalar.copy(gains[:], gains_ps[:, :, 0:PASSES])
 
         x_codes = keep.tile([P, PASSES, M], U32, name="x_codes", align_bytes=64)
         x_plane = keep.tile([P, PASSES, M], U8, name="x_plane", align_bytes=64)
-        v_codes = {}
         x_grouped = [keep.tile([P, M, 4], BF16, name=f"x_grouped{a}", align_bytes=64) for a in range(PASSES)]
+        v_codes = {}
 
-        def cast_x(engine_copy, a, c0, c1):
-            dst = x_grouped[a][:].rearrange("p (c z) i -> p c i z", z=4)
-            src = x_raw[a][:].rearrange("p i (c z) -> p c i z", z=4)
-            engine_copy(dst[:, c0:c1], src[:, c0:c1])
+        def round_x(engine_copy, a, lo, hi):
+            dst = x_grouped[a][:].rearrange("p (s z) t -> p s t z", z=4)
+            src = x_raw[a][:].rearrange("p t (s z) -> p s t z", z=4)
+            engine_copy(dst[:, lo:hi], src[:, lo:hi])
 
-        def quantise_x(a, m0, m1):
-            nc.vector.quantize_mx(out=x_codes[:, a, m0:m1].bitcast(FP8X4), scales=x_plane[:, a, m0:m1], in_=x_grouped[a][:, m0:m1, :].rearrange("p m i -> p (m i)"))
-
-        def pick_table(a, b0, b1, home):
-            codes = keep.tile([P, 4, P * (b1 - b0)], U32, name=home, align_bytes=64)
+        def pick_table(a, b0, b1, name):
+            codes = keep.tile([P, 4, P * (b1 - b0)], U32, name=name, align_bytes=64)
             nc.vector.tensor_copy(
-                codes[:].rearrange("p t (c l) -> p c t l", l=4),
+                codes[:].rearrange("p t (d l) -> p d t l", l=4),
                 tab[a][:].bitcast(U32).indirect(offsets[:, 32 * b0 : 32 * b1]),
             )
             for b in range(b0, b1):
                 v_codes[a, b] = codes[:, :, P * (b - b0) : P * (b - b0 + 1)]
 
-        pick_table(0, 0, 2, "v_codes0")
+        pick_table(0, 0, PASSES, "v_codes0")
         for a in range(PASSES):
-            cast_x(nc.scalar.copy, a, 0, X_SPLIT[a])
-            cast_x(nc.vector.tensor_copy, a, X_SPLIT[a], M // 4)
-            quantise_x(a, 0, M)
+            round_x(nc.scalar.copy, a, 0, X_ON_SCALAR[a])
+            round_x(nc.vector.tensor_copy, a, X_ON_SCALAR[a], M // 4)
+            nc.vector.quantize_mx(out=x_codes[:, a, :].bitcast(FP8X4), scales=x_plane[:, a, :], in_=x_grouped[a][:].rearrange("p m t -> p (m t)"))
         pick_table(1, 0, 1, "v_codes1a")
         pick_table(1, 1, 2, "v_codes1b")
 
         wd_codes = {}
-        wd_plane = {c: keep.tile([P, PASSES * P], U8, name=f"wd_plane{c}", align_bytes=64) for c in (0, 1, 2, 3, 6, 7)}
-        coded_wd = {}
+        wd_plane = {c: keep.tile([P, PASSES * P], U8, name=f"wd_plane{c}", align_bytes=64) for c in SINGLES}
+        wd_operand = {}
         picked = {}
         grouped = {}
-        grouped_home = {}
-        home = {(7, 1): "pair_grouped"}
-        codes_home = {}
-        h_codes = {}
 
-        def pick_wd(c, b0, b1):
-            picked[c, b0] = keep.tile([P, 512 * (b1 - b0)], BF16, name=home.get((c, b0), f"picked{c}_{b0}"), align_bytes=64)
+        def pick_wd(c, b0, b1, name):
+            picked[c, b0] = keep.tile([P, PASS * (b1 - b0)], BF16, name=name, align_bytes=64)
             nc.vector.tensor_copy(
-                picked[c, b0][:].rearrange("p (u c l e) -> p c u e l", u=2, l=4, e=2),
+                picked[c, b0][:].rearrange("p (u d l e) -> p d u e l", u=2, l=4, e=2),
                 wd[c][:].indirect(offsets[:, 32 * b0 : 32 * b1]),
             )
 
-        def turn_wd(c, b0, b1, bank, engine_copy=nc.scalar.copy):
+        def turn_wd(c, b0, b1, bank, engine_copy):
             words = picked[c, b0][:].bitcast(F32)
-            if c == 3:
-                grouped[c] = late.tile([P, S], BF16, name="grouped3", align_bytes=64, offset=0)
-            elif b0 == 0:
-                grouped[c] = keep.tile([P, S], BF16, name=grouped_home.get(c, f"grouped{c}"), align_bytes=64)
             turned = banks.tile([P, 4, P], F32, name=f"bank{bank}")
             for b in range(b0, b1):
                 for u in range(2):
-                    s = (b1 - b0) * u + b - b0
-                    nc.tensor.transpose(turned[:, 2 * u + b, :], words[:, P * s : P * (s + 1)], ident[:])
+                    start = P * ((b1 - b0) * u + b - b0)
+                    nc.tensor.transpose(turned[:, 2 * u + b, :], words[:, start : start + P], ident[:])
             engine_copy(
                 grouped[c][:].bitcast(F32).rearrange("p (b n u) -> p b n u", b=2, u=2)[:, b0:b1],
                 turned[:].rearrange("p (u b) n -> p b n u", u=2)[:, b0:b1],
             )
 
         def quantise_wd(c, b0, b1):
-            if c not in wd_codes:
-                wd_codes[c] = keep.tile([P, PASSES * P], U32, name=codes_home.get(c, f"wd_codes{c}"), align_bytes=64)
-            nc.vector.quantize_mx(out=wd_codes[c][:, P * b0 : P * b1].bitcast(FP8X4), scales=wd_plane[c][:, P * b0 : P * b1], in_=grouped[c][:, 512 * b0 : 512 * b1])
+            nc.vector.quantize_mx(out=wd_codes[c][:, P * b0 : P * b1].bitcast(FP8X4), scales=wd_plane[c][:, P * b0 : P * b1], in_=grouped[c][:, PASS * b0 : PASS * b1])
             for b in range(b0, b1):
-                coded_wd[c, b] = (wd_codes[c][:, P * b : P * (b + 1)].bitcast(FP8X4), wd_plane[c][:, P * b : P * (b + 1)])
+                wd_operand[c, b] = (wd_codes[c][:, P * b : P * (b + 1)].bitcast(FP8X4), wd_plane[c][:, P * b : P * (b + 1)])
 
         pair_words = keep.tile([P, 2 * T], BF16, name="pair_words", align_bytes=64)
-        pair_picked = [keep.tile([P, S // 2], U32, name=f"pair_picked{b}", align_bytes=64) for b in range(PASSES)]
+        pair_picked = [keep.tile([P, PASS], U32, name=f"pair_picked{b}", align_bytes=64) for b in range(PASSES)]
         pair_grouped = keep.tile([P, 2 * S], BF16, name="pair_grouped", align_bytes=64)
         pair_plane = keep.tile([P, PASSES * 2 * P], U8, name="pair_plane", align_bytes=64)
 
-        def cast_pair(i, engine_copy):
-            engine_copy(
-                pair_words[:, 2 * CHUNK_START[i] : 2 * CHUNK_START[i + 1]].rearrange("p (t e) -> p t e", e=2),
-                pair_raw[i][:].rearrange("p e t -> p t e"),
+        def round_pair(i):
+            nc.scalar.copy(
+                pair_words[:, 2 * CHUNK_START[i] : 2 * CHUNK_START[i + 1]].rearrange("p (col e) -> p col e", e=2),
+                pair_raw[i][:].rearrange("p e col -> p col e"),
             )
 
         def pick_pair(b):
             nc.vector.tensor_copy(
-                pair_picked[b][:].rearrange("p (t c l) -> p c t l", t=4, l=4),
+                pair_picked[b][:].rearrange("p (t d l) -> p d t l", t=4, l=4),
                 pair_words[:].bitcast(U32).indirect(offsets[:, 32 * b : 32 * (b + 1)]),
             )
 
@@ -221,132 +210,142 @@ def tile_list_listed_rating_autoencoder_kernel(tc, tab_words, tab_scales, offs, 
         def quantise_pair():
             codes = keep.tile([P, PASSES * 2 * P], U32, name="wd6", align_bytes=64)
             nc.vector.quantize_mx(out=codes[:].bitcast(FP8X4), scales=pair_plane[:], in_=pair_grouped[:])
-            for c in (4, 5):
+            for half, c in enumerate(PAIR):
                 for b in range(PASSES):
-                    cols_c = slice(2 * P * b + P * (c - 4), 2 * P * b + P * (c - 3))
-                    coded_wd[c, b] = (codes[:, cols_c].bitcast(FP8X4), pair_plane[:, cols_c])
+                    columns = slice(2 * P * b + P * half, 2 * P * b + P * (half + 1))
+                    wd_operand[c, b] = (codes[:, columns].bitcast(FP8X4), pair_plane[:, columns])
 
         h_plane = keep.tile([P, PASSES, M], U8, name="h_plane", align_bytes=64)
-        h_rows = [keep.tile([P, 4 * M], BF16, name=f"h_rows{b}", align_bytes=64) for b in range(PASSES)]
+        h_pairs = [keep.tile([P, 4 * M], BF16, name=f"h_rows{b}", align_bytes=64) for b in range(PASSES)]
         h_grouped = {0: keep.tile([P, 4 * M], BF16, name="h_grouped0", align_bytes=64)}
-
+        h_codes = {}
         sig = [keep.tile([P, 4, M], F32, name=f"sig{b}") for b in range(PASSES)]
 
         def encode(b, t):
-            col = slice(256 * t + P * b, 256 * t + P * (b + 1))
-            acc = banks.tile([P, M], F32, name=f"bank{(4 * b + t + 6) % 8}")
+            columns = slice(PASSES * P * t + P * b, PASSES * P * t + P * (b + 1))
+            acc = banks.tile([P, M], F32, name=f"bank{(4 * b + t + SUM_BANKS) % 8}")
             for a in range(PASSES):
                 nc.tensor.matmul_mx(
-                    out=acc[:], lhsT=v_codes[a, b][:, t, :].bitcast(FP8X4), lhsT_scale=v_plane[:].bitcast(U8)[4 * a : P, col],
+                    out=acc[:], lhsT=v_codes[a, b][:, t, :].bitcast(FP8X4), lhsT_scale=v_plane[:].bitcast(U8)[4 * a : P, columns],
                     rhs=x_codes[:, a, :].bitcast(FP8X4), rhs_scale=x_plane[:, a, :], start=(a == 0), stop=(a == PASSES - 1),
                 )
             nc.scalar.activation(sig[b][:, t, :], acc[:], ACT.Sigmoid)
 
-        def gain(b, t):
-            pairs = h_rows[b][:].rearrange("p (u m e) -> p u m e", u=2, e=2)
-            nc.gpsimd.tensor_scalar(pairs[:, t // 2, :, t % 2], sig[b][:, t, :], cols[:, t, b : b + 1], 0.0, ALU.mult, ALU.add)
+        def apply_gain(b, t):
+            pairs = h_pairs[b][:].rearrange("p (u m e) -> p u m e", u=2, e=2)
+            nc.gpsimd.tensor_scalar(pairs[:, t // 2, :, t % 2], sig[b][:, t, :], gains[:, t, b : b + 1], 0.0, ALU.mult, ALU.add)
 
         def group_h(b, engine_copy):
             engine_copy(
                 h_grouped[b][:].bitcast(F32).rearrange("p (m u) -> p m u", u=2),
-                h_rows[b][:].bitcast(F32).rearrange("p (u m) -> p m u", u=2),
+                h_pairs[b][:].bitcast(F32).rearrange("p (u m) -> p m u", u=2),
             )
 
         def quantise_h(b):
             nc.vector.quantize_mx(out=h_codes[b].bitcast(FP8X4), scales=h_plane[:, b, :], in_=h_grouped[b][:])
 
-        acc_of = {}
+        sums = {}
 
-        def shortcut(c, first):
+        def add_shortcut(c, first):
             if first:
-                acc_of[c] = banks.tile([P, M], F32, name=f"bank{c % 6}")
+                sums[c] = banks.tile([P, M], F32, name=f"bank{c % SUM_BANKS}")
             for a in range(PASSES):
                 nc.tensor.matmul_mx(
-                    out=acc_of[c][:],
+                    out=sums[c][:],
                     lhsT=w4[c // 4][:, a, :].bitcast(U8)[:, 2 * P * (c % 4) : 2 * P * (c % 4 + 1)].bitcast(FP4X4),
                     lhsT_scale=w4_plane[:, a, :].bitcast(U8)[:, P * c : P * (c + 1)],
                     rhs=x_codes[:, a, :].bitcast(FP8X4), rhs_scale=x_plane[:, a, :],
                     start=(first and a == 0), stop=(not first and a == PASSES - 1),
                 )
 
-        def decode(c, first):
+        def add_decoded(c, first):
             if first:
-                acc_of[c] = banks.tile([P, M], F32, name=f"bank{c % 6}")
+                sums[c] = banks.tile([P, M], F32, name=f"bank{c % SUM_BANKS}")
             for b in range(PASSES):
                 nc.tensor.matmul_mx(
-                    out=acc_of[c][:], lhsT=coded_wd[c, b][0], lhsT_scale=coded_wd[c, b][1],
+                    out=sums[c][:], lhsT=wd_operand[c, b][0], lhsT_scale=wd_operand[c, b][1],
                     rhs=h_codes[b].bitcast(FP8X4), rhs_scale=h_plane[:, b, :],
                     start=(first and b == 0), stop=(not first and b == PASSES - 1),
                 )
 
         def rate(c):
-            acc = acc_of[c]
             parts = 2 if c == TILES - 1 else 1
             width = M // parts
             for part in range(parts):
-                rated = rated_early[:, c, :] if c < 3 else ring.tile([P, width], F32, name="rated")[:]
-                nc.scalar.activation(rated, acc[:, width * part : width * (part + 1)], ACT.Tanh, bias=bias[:, c : c + 1])
-                nc.sync.dma_start(out[P * c : P * (c + 1), width * part : width * (part + 1)], rated)
+                users = slice(width * part, width * (part + 1))
+                rated = rated_early[:, c, :] if c < EARLY else ring.tile([P, width], F32, name="rated")[:]
+                nc.scalar.activation(rated, sums[c][:, users], ACT.Tanh, bias=bias[:, c : c + 1])
+                nc.sync.dma_start(out[P * c : P * (c + 1), users], rated)
 
         for c in range(4):
-            pick_wd(c, 0, 2)
+            pick_wd(c, 0, PASSES, f"picked{c}_0")
         for b in range(PASSES):
             for t in range(4):
                 encode(b, t)
-                gain(b, t)
+                apply_gain(b, t)
         bias = keep.tile([P, TILES], F32, name="bias")
         bias_ps = banks.tile([P, P], F32, name="bank5")
-        nc.tensor.transpose(bias_ps[:], rows[:, 4 * P : 5 * P], ident[:])
+        nc.tensor.transpose(bias_ps[:], rows[:, PASS : PASS + P], ident[:])
         nc.scalar.copy(bias[:], bias_ps[:, 0:TILES])
-        turn_wd(0, 0, 2, 6)
+
+        grouped[0] = keep.tile([P, S], BF16, name="grouped0", align_bytes=64)
+        turn_wd(0, 0, PASSES, 6, nc.scalar.copy)
         group_h(0, nc.scalar.copy)
-        turn_wd(1, 0, 2, 7)
-        after3 = mid.tile([P, 2 * M + 4 * 256], U32, name="after3", align_bytes=64, offset=8 * M)
-        h_grouped[1] = mid.tile([P, 4 * M], BF16, name="h_grouped1", align_bytes=64, offset=0)
+        grouped[1] = keep.tile([P, S], BF16, name="grouped1", align_bytes=64)
+        turn_wd(1, 0, PASSES, 7, nc.scalar.copy)
+
+        after3 = on_wd3.tile([P, PASSES * M + 4 * PASSES * P], U32, name="after3", align_bytes=64, offset=8 * M)
+        h_grouped[1] = on_wd3.tile([P, 4 * M], BF16, name="h_grouped1", align_bytes=64, offset=0)
         for b in range(PASSES):
             h_codes[b] = after3[:, M * b : M * (b + 1)]
         for c in range(4):
-            wd_codes[c] = after3[:, 2 * M + 256 * c : 2 * M + 256 * (c + 1)]
-        quantise_wd(0, 0, 2)
-        quantise_wd(1, 0, 2)
-        turn_wd(2, 0, 2, 6)
+            wd_codes[c] = after3[:, PASSES * (M + P * c) : PASSES * (M + P * (c + 1))]
+        quantise_wd(0, 0, PASSES)
+        quantise_wd(1, 0, PASSES)
+        grouped[2] = keep.tile([P, S], BF16, name="grouped2", align_bytes=64)
+        turn_wd(2, 0, PASSES, 6, nc.scalar.copy)
         quantise_h(0)
         group_h(1, nc.vector.tensor_copy)
-        quantise_wd(2, 0, 2)
+        quantise_wd(2, 0, PASSES)
         quantise_h(1)
-        cast_pair(0, nc.scalar.copy)
-        cast_pair(1, nc.scalar.copy)
-        cast_pair(2, nc.scalar.copy)
-        cast_pair(3, nc.scalar.copy)
+
+        for i in range(len(CHUNKS)):
+            round_pair(i)
         pick_pair(0)
         pick_pair(1)
-        turn_wd(3, 0, 2, 7)
-        quantise_wd(3, 0, 2)
-        rated_early = late.tile([P, 3, M], F32, name="rated_early", align_bytes=64, offset=2 * S)
-        for c in range(3):
-            decode(c, True)
-            shortcut(c, False)
+        grouped[3] = on_last_chunk.tile([P, S], BF16, name="grouped3", align_bytes=64, offset=0)
+        turn_wd(3, 0, PASSES, 7, nc.scalar.copy)
+        quantise_wd(3, 0, PASSES)
+        rated_early = on_last_chunk.tile([P, EARLY, M], F32, name="rated_early", align_bytes=64, offset=2 * S)
+        for c in range(EARLY):
+            add_decoded(c, True)
+            add_shortcut(c, False)
             rate(c)
         turn_pair(0, 6)
         turn_pair(1, 7)
-        shortcut(3, True)
-        decode(3, False)
+        add_shortcut(3, True)
+        add_decoded(3, False)
         rate(3)
-        pick_wd(6, 0, 2)
-        turn_wd(6, 0, 2, 6)
-        for c in range(4, TILES):
-            shortcut(c, True)
+
+        pick_wd(6, 0, PASSES, "picked6_0")
+        grouped[6] = keep.tile([P, S], BF16, name="grouped6", align_bytes=64)
+        turn_wd(6, 0, PASSES, 6, nc.scalar.copy)
+        for c in range(PAIR[0], TILES):
+            add_shortcut(c, True)
         quantise_pair()
-        pick_wd(7, 0, 1)
-        quantise_wd(6, 0, 2)
-        pick_wd(7, 1, 2)
-        for c in (4, 5):
-            decode(c, False)
+        pick_wd(7, 0, 1, "picked7_0")
+        wd_codes[6] = keep.tile([P, PASSES * P], U32, name="wd_codes6", align_bytes=64)
+        quantise_wd(6, 0, PASSES)
+        pick_wd(7, 1, 2, "pair_grouped")
+        for c in PAIR:
+            add_decoded(c, False)
             rate(c)
-        turn_wd(7, 0, 1, 7)
+        grouped[7] = keep.tile([P, S], BF16, name="grouped7", align_bytes=64)
+        turn_wd(7, 0, 1, 7, nc.scalar.copy)
+        wd_codes[7] = keep.tile([P, PASSES * P], U32, name="wd_codes7", align_bytes=64)
         quantise_wd(7, 0, 1)
         turn_wd(7, 1, 2, 6, nc.vector.tensor_copy)
         quantise_wd(7, 1, 2)
         for c in (6, 7):
-            decode(c, False)
+            add_decoded(c, False)
             rate(c)

@@ -21,13 +21,13 @@ P = 128
 PASS = 4 * P
 PASSES = 2
 TILES = N // P
-PAIR = (4, 5)
-SINGLES = (0, 1, 2, 3, 6, 7)
-EARLY = 3
+PAIR = (5, 6)
+SINGLES = (0, 1, 2, 3, 4, 7)
+EARLY = 4
 SUM_BANKS = 6
-CHUNKS = (256, 768, 768, 256)
+CHUNKS = (512, 768, 512, 256)
 CHUNK_START = [sum(CHUNKS[:i]) for i in range(len(CHUNKS) + 1)]
-X_ON_SCALAR = (72, 44)
+X_ON_SCALAR = (80, 44)
 
 
 def tile_list_listed_rating_autoencoder_kernel(tc, tab_words, tab_scales, offs, x, w4_words, w4_scales, wdT, g, bo, out):
@@ -55,8 +55,11 @@ def tile_list_listed_rating_autoencoder_kernel(tc, tab_words, tab_scales, offs, 
         ident = keep.tile([P, P], F32, name="ident")
         make_identity(nc, ident[:])
 
+        warm = keep.tile([P, 1], F32, name="warm")
+        nc.scalar.activation(warm[:], rows[:, 0:1], ACT.Sigmoid)
+
         x_raw = [keep.tile([P, 4, M], F32, name=f"x_raw{a}") for a in range(PASSES)]
-        tab = [keep.tile([P, T], I32, name=f"tab{a}") for a in range(PASSES)]
+        tab = [keep.tile([P, T], I32, name=f"tab{a}", align_bytes=64) for a in range(PASSES)]
         wd = {c: keep.tile([P, T], F32, name=f"wd{c}", align_bytes=64) for c in SINGLES if c != 3}
         wd[3] = on_wd3.tile([P, T], F32, name="wd3", align_bytes=64, offset=0)
         w4 = [keep.tile([P, PASSES, N // 4], I32, name=f"w4_{half}", align_bytes=64) for half in range(2)]
@@ -84,10 +87,10 @@ def tile_list_listed_rating_autoencoder_kernel(tc, tab_words, tab_scales, offs, 
             nc.sync.dma_start(pair_raw[i][:], pair_rows[:, :, CHUNK_START[i] : CHUNK_START[i + 1]])
 
         load_table(0)
-        load_x(0)
         nc.sync.dma_start(g_rows[:], g.rearrange("(b j) -> b j", b=PASSES))
-        load_x(1)
+        load_wd(0)
         load_table(1)
+        load_x(0)
 
         v_plane = keep.tile([P, S // 4], I32, name="v_plane", align_bytes=64)
         listed_plane = keep.tile([P, S], U8, name="listed_plane", align_bytes=64)
@@ -101,19 +104,19 @@ def tile_list_listed_rating_autoencoder_kernel(tc, tab_words, tab_scales, offs, 
         for quad in range(4):
             nc.sync.dma_start(v_plane[32 * quad : 32 * quad + 8, :], ordered_plane[quad:32:4, :])
 
-        load_wd(0)
+        load_x(1)
         load_wd(1)
         nc.sync.dma_start(rows[0:TILES, PASS : PASS + P], bo.rearrange("(c p) -> c p", p=P))
         load_wd(2)
-        load_pair(0)
         load_wd(3)
+        load_pair(0)
         load_pair(1)
-        load_pair(2)
         load_shortcut_scales()
         load_shortcut(0)
+        load_wd(4)
+        load_pair(2)
         load_pair(3)
         load_shortcut(1)
-        load_wd(6)
         load_wd(7)
 
         gains = keep.tile([P, 4, PASSES], F32, name="gains")
@@ -141,14 +144,6 @@ def tile_list_listed_rating_autoencoder_kernel(tc, tab_words, tab_scales, offs, 
             )
             for b in range(b0, b1):
                 v_codes[a, b] = codes[:, :, P * (b - b0) : P * (b - b0 + 1)]
-
-        pick_table(0, 0, PASSES, "v_codes0")
-        for a in range(PASSES):
-            round_x(nc.scalar.copy, a, 0, X_ON_SCALAR[a])
-            round_x(nc.vector.tensor_copy, a, X_ON_SCALAR[a], M // 4)
-            nc.vector.quantize_mx(out=x_codes[:, a, :].bitcast(FP8X4), scales=x_plane[:, a, :], in_=x_grouped[a][:].rearrange("p m t -> p (m t)"))
-        pick_table(1, 0, 1, "v_codes1a")
-        pick_table(1, 1, 2, "v_codes1b")
 
         wd_codes = {}
         wd_plane = {c: keep.tile([P, PASSES * P], U8, name=f"wd_plane{c}", align_bytes=64) for c in SINGLES}
@@ -208,7 +203,7 @@ def tile_list_listed_rating_autoencoder_kernel(tc, tab_words, tab_scales, offs, 
             )
 
         def quantise_pair():
-            codes = keep.tile([P, PASSES * 2 * P], U32, name="wd6", align_bytes=64)
+            codes = keep.tile([P, PASSES * 2 * P], U32, name="pair_codes", align_bytes=64)
             nc.vector.quantize_mx(out=codes[:].bitcast(FP8X4), scales=pair_plane[:], in_=pair_grouped[:])
             for half, c in enumerate(PAIR):
                 for b in range(PASSES):
@@ -223,7 +218,7 @@ def tile_list_listed_rating_autoencoder_kernel(tc, tab_words, tab_scales, offs, 
 
         def encode(b, t):
             columns = slice(PASSES * P * t + P * b, PASSES * P * t + P * (b + 1))
-            acc = banks.tile([P, M], F32, name=f"bank{(4 * b + t + SUM_BANKS) % 8}")
+            acc = banks.tile([P, M], F32, name=f"bank{t}")
             for a in range(PASSES):
                 nc.tensor.matmul_mx(
                     out=acc[:], lhsT=v_codes[a, b][:, t, :].bitcast(FP8X4), lhsT_scale=v_plane[:].bitcast(U8)[4 * a : P, columns],
@@ -277,7 +272,19 @@ def tile_list_listed_rating_autoencoder_kernel(tc, tab_words, tab_scales, offs, 
                 nc.scalar.activation(rated, sums[c][:, users], ACT.Tanh, bias=bias[:, c : c + 1])
                 nc.sync.dma_start(out[P * c : P * (c + 1), users], rated)
 
-        for c in range(4):
+        pick_table(0, 0, PASSES, "v_codes0")
+        pick_wd(0, 0, PASSES, "picked0_0")
+        pick_table(1, 0, PASSES, "v_codes1")
+        grouped[0] = keep.tile([P, S], BF16, name="grouped0", align_bytes=64)
+        turn_wd(0, 0, PASSES, 6, nc.scalar.copy)
+        wd_codes[0] = keep.tile([P, PASSES * P], U32, name="tab1", align_bytes=64)
+        quantise_wd(0, 0, PASSES)
+        for a in range(PASSES):
+            round_x(nc.scalar.copy, a, 0, X_ON_SCALAR[a])
+            round_x(nc.vector.tensor_copy, a, X_ON_SCALAR[a], M // 4)
+            nc.vector.quantize_mx(out=x_codes[:, a, :].bitcast(FP8X4), scales=x_plane[:, a, :], in_=x_grouped[a][:].rearrange("p m t -> p (m t)"))
+
+        for c in (1, 2, 3):
             pick_wd(c, 0, PASSES, f"picked{c}_0")
         for b in range(PASSES):
             for t in range(4):
@@ -288,64 +295,64 @@ def tile_list_listed_rating_autoencoder_kernel(tc, tab_words, tab_scales, offs, 
         nc.tensor.transpose(bias_ps[:], rows[:, PASS : PASS + P], ident[:])
         nc.scalar.copy(bias[:], bias_ps[:, 0:TILES])
 
-        grouped[0] = keep.tile([P, S], BF16, name="grouped0", align_bytes=64)
-        turn_wd(0, 0, PASSES, 6, nc.scalar.copy)
-        group_h(0, nc.scalar.copy)
         grouped[1] = keep.tile([P, S], BF16, name="grouped1", align_bytes=64)
         turn_wd(1, 0, PASSES, 7, nc.scalar.copy)
+        group_h(0, nc.scalar.copy)
+        grouped[2] = keep.tile([P, S], BF16, name="grouped2", align_bytes=64)
+        turn_wd(2, 0, PASSES, 6, nc.scalar.copy)
 
         after3 = on_wd3.tile([P, PASSES * M + 4 * PASSES * P], U32, name="after3", align_bytes=64, offset=8 * M)
         h_grouped[1] = on_wd3.tile([P, 4 * M], BF16, name="h_grouped1", align_bytes=64, offset=0)
         for b in range(PASSES):
             h_codes[b] = after3[:, M * b : M * (b + 1)]
-        for c in range(4):
-            wd_codes[c] = after3[:, PASSES * (M + P * c) : PASSES * (M + P * (c + 1))]
-        quantise_wd(0, 0, PASSES)
+        for c in range(1, 5):
+            wd_codes[c] = after3[:, PASSES * (M + P * (c - 1)) : PASSES * (M + P * c)]
         quantise_wd(1, 0, PASSES)
-        grouped[2] = keep.tile([P, S], BF16, name="grouped2", align_bytes=64)
-        turn_wd(2, 0, PASSES, 6, nc.scalar.copy)
+        quantise_wd(2, 0, PASSES)
         quantise_h(0)
         group_h(1, nc.vector.tensor_copy)
-        quantise_wd(2, 0, PASSES)
+        round_pair(0)
+        grouped[3] = keep.tile([P, S], BF16, name="grouped3", align_bytes=64)
+        turn_wd(3, 0, PASSES, 7, nc.scalar.copy)
+        quantise_wd(3, 0, PASSES)
         quantise_h(1)
+        pick_wd(4, 0, PASSES, "picked4_0")
 
-        for i in range(len(CHUNKS)):
+        for i in range(1, len(CHUNKS)):
             round_pair(i)
         pick_pair(0)
         pick_pair(1)
-        grouped[3] = on_last_chunk.tile([P, S], BF16, name="grouped3", align_bytes=64, offset=0)
-        turn_wd(3, 0, PASSES, 7, nc.scalar.copy)
-        quantise_wd(3, 0, PASSES)
         rated_early = on_last_chunk.tile([P, EARLY, M], F32, name="rated_early", align_bytes=64, offset=2 * S)
         for c in range(EARLY):
-            add_decoded(c, True)
-            add_shortcut(c, False)
-            rate(c)
-        turn_pair(0, 6)
-        turn_pair(1, 7)
-        add_shortcut(3, True)
-        add_decoded(3, False)
+            add_shortcut(c, True)
+        for c in range(EARLY):
+            add_decoded(c, False)
+        rate(0)
+        rate(1)
+        grouped[4] = on_last_chunk.tile([P, S], BF16, name="grouped4", align_bytes=64, offset=0)
+        turn_wd(4, 0, PASSES, 6, nc.scalar.copy)
+        quantise_wd(4, 0, PASSES)
+        rate(2)
+        turn_pair(0, 7)
+        turn_pair(1, 6)
         rate(3)
-
-        pick_wd(6, 0, PASSES, "picked6_0")
-        grouped[6] = keep.tile([P, S], BF16, name="grouped6", align_bytes=64)
-        turn_wd(6, 0, PASSES, 6, nc.scalar.copy)
+        add_shortcut(4, True)
+        add_decoded(4, False)
+        rate(4)
         for c in range(PAIR[0], TILES):
             add_shortcut(c, True)
-        quantise_pair()
+
         pick_wd(7, 0, 1, "picked7_0")
-        wd_codes[6] = keep.tile([P, PASSES * P], U32, name="wd_codes6", align_bytes=64)
-        quantise_wd(6, 0, PASSES)
-        pick_wd(7, 1, 2, "pair_grouped")
+        pick_wd(7, 1, 2, "picked7_1")
+        quantise_pair()
+        grouped[7] = keep.tile([P, S], BF16, name="grouped7", align_bytes=64)
+        turn_wd(7, 0, 1, 7, nc.scalar.copy)
         for c in PAIR:
             add_decoded(c, False)
             rate(c)
-        grouped[7] = keep.tile([P, S], BF16, name="grouped7", align_bytes=64)
-        turn_wd(7, 0, 1, 7, nc.scalar.copy)
         wd_codes[7] = keep.tile([P, PASSES * P], U32, name="wd_codes7", align_bytes=64)
         quantise_wd(7, 0, 1)
         turn_wd(7, 1, 2, 6, nc.vector.tensor_copy)
         quantise_wd(7, 1, 2)
-        for c in (6, 7):
-            add_decoded(c, False)
-            rate(c)
+        add_decoded(7, False)
+        rate(7)

@@ -23,11 +23,11 @@ PASSES = 2
 TILES = N // P
 PAIR = (5, 6)
 SINGLES = (0, 1, 2, 3, 4, 7)
-EARLY = 4
+EARLY = 5
 SUM_BANKS = 6
-CHUNKS = (512, 768, 512, 256)
+CHUNKS = (384, 640, 512, 512)
 CHUNK_START = [sum(CHUNKS[:i]) for i in range(len(CHUNKS) + 1)]
-X_ON_SCALAR = (80, 44)
+X_ON_SCALAR = (56, 44)
 
 
 def tile_list_listed_rating_autoencoder_kernel(tc, tab_words, tab_scales, offs, x, w4_words, w4_scales, wdT, g, bo, out):
@@ -58,10 +58,10 @@ def tile_list_listed_rating_autoencoder_kernel(tc, tab_words, tab_scales, offs, 
         warm = keep.tile([P, 1], F32, name="warm")
         nc.scalar.activation(warm[:], rows[:, 0:1], ACT.Sigmoid)
 
-        x_raw = [keep.tile([P, 4, M], F32, name=f"x_raw{a}") for a in range(PASSES)]
+        x_raw = [keep.tile([P, 4, M], F32, name=f"x_raw{a}", align_bytes=64) for a in range(PASSES)]
         tab = [keep.tile([P, T], I32, name=f"tab{a}", align_bytes=64) for a in range(PASSES)]
-        wd = {c: keep.tile([P, T], F32, name=f"wd{c}", align_bytes=64) for c in SINGLES if c != 3}
-        wd[3] = on_wd3.tile([P, T], F32, name="wd3", align_bytes=64, offset=0)
+        wd = {c: keep.tile([P, T], F32, name=f"wd{c}", align_bytes=64) for c in SINGLES if c != 4}
+        wd[4] = on_wd3.tile([P, T], F32, name="wd4", align_bytes=64, offset=8 * M)
         w4 = [keep.tile([P, PASSES, N // 4], I32, name=f"w4_{half}", align_bytes=64) for half in range(2)]
         pair_raw = [keep.tile([P, 2, CHUNKS[i]], F32, name=f"pair_raw{i}", align_bytes=64) for i in range(len(CHUNKS) - 1)]
         pair_raw.append(on_last_chunk.tile([P, 2, CHUNKS[-1]], F32, name="pair_raw_last", align_bytes=64, offset=2 * S - 64))
@@ -89,8 +89,8 @@ def tile_list_listed_rating_autoencoder_kernel(tc, tab_words, tab_scales, offs, 
         load_table(0)
         nc.sync.dma_start(g_rows[:], g.rearrange("(b j) -> b j", b=PASSES))
         load_wd(0)
-        load_table(1)
         load_x(0)
+        load_x(1)
 
         v_plane = keep.tile([P, S // 4], I32, name="v_plane", align_bytes=64)
         listed_plane = keep.tile([P, S], U8, name="listed_plane", align_bytes=64)
@@ -104,19 +104,19 @@ def tile_list_listed_rating_autoencoder_kernel(tc, tab_words, tab_scales, offs, 
         for quad in range(4):
             nc.sync.dma_start(v_plane[32 * quad : 32 * quad + 8, :], ordered_plane[quad:32:4, :])
 
-        load_x(1)
+        load_table(1)
         load_wd(1)
-        nc.sync.dma_start(rows[0:TILES, PASS : PASS + P], bo.rearrange("(c p) -> c p", p=P))
         load_wd(2)
         load_wd(3)
         load_pair(0)
-        load_pair(1)
+        load_wd(4)
         load_shortcut_scales()
         load_shortcut(0)
-        load_wd(4)
+        nc.sync.dma_start(rows[0:TILES, PASS : PASS + P], bo.rearrange("(c p) -> c p", p=P))
+        load_pair(1)
+        load_shortcut(1)
         load_pair(2)
         load_pair(3)
-        load_shortcut(1)
         load_wd(7)
 
         gains = keep.tile([P, 4, PASSES], F32, name="gains")
@@ -126,8 +126,8 @@ def tile_list_listed_rating_autoencoder_kernel(tc, tab_words, tab_scales, offs, 
             nc.tensor.transpose(gains_ps[:, t, :], rows[:, P * t : P * (t + 1)], ident[:])
         nc.scalar.copy(gains[:], gains_ps[:, :, 0:PASSES])
 
-        x_codes = keep.tile([P, PASSES, M], U32, name="x_codes", align_bytes=64)
-        x_plane = keep.tile([P, PASSES, M], U8, name="x_plane", align_bytes=64)
+        x_codes = [keep.tile([P, M], U32, name=f"x_codes{a}", align_bytes=64) for a in range(PASSES)]
+        x_plane = [keep.tile([P, M], U8, name=f"x_plane{a}", align_bytes=64) for a in range(PASSES)]
         x_grouped = [keep.tile([P, M, 4], BF16, name=f"x_grouped{a}", align_bytes=64) for a in range(PASSES)]
         v_codes = {}
 
@@ -146,7 +146,6 @@ def tile_list_listed_rating_autoencoder_kernel(tc, tab_words, tab_scales, offs, 
                 v_codes[a, b] = codes[:, :, P * (b - b0) : P * (b - b0 + 1)]
 
         wd_codes = {}
-        wd_plane = {c: keep.tile([P, PASSES * P], U8, name=f"wd_plane{c}", align_bytes=64) for c in SINGLES}
         wd_operand = {}
         picked = {}
         grouped = {}
@@ -171,19 +170,20 @@ def tile_list_listed_rating_autoencoder_kernel(tc, tab_words, tab_scales, offs, 
             )
 
         def quantise_wd(c, b0, b1):
-            nc.vector.quantize_mx(out=wd_codes[c][:, P * b0 : P * b1].bitcast(FP8X4), scales=wd_plane[c][:, P * b0 : P * b1], in_=grouped[c][:, PASS * b0 : PASS * b1])
+            plane = keep.tile([P, P * (b1 - b0)], U8, name=f"wd_plane{c}_{b0}", align_bytes=64)
+            nc.vector.quantize_mx(out=wd_codes[c][:].bitcast(FP8X4), scales=plane[:], in_=grouped[c][:, PASS * b0 : PASS * b1])
             for b in range(b0, b1):
-                wd_operand[c, b] = (wd_codes[c][:, P * b : P * (b + 1)].bitcast(FP8X4), wd_plane[c][:, P * b : P * (b + 1)])
+                wd_operand[c, b] = (wd_codes[c][:, P * (b - b0) : P * (b - b0 + 1)].bitcast(FP8X4), plane[:, P * (b - b0) : P * (b - b0 + 1)])
 
         pair_words = keep.tile([P, 2 * T], BF16, name="pair_words", align_bytes=64)
         pair_picked = [keep.tile([P, PASS], U32, name=f"pair_picked{b}", align_bytes=64) for b in range(PASSES)]
         pair_grouped = keep.tile([P, 2 * S], BF16, name="pair_grouped", align_bytes=64)
         pair_plane = keep.tile([P, PASSES * 2 * P], U8, name="pair_plane", align_bytes=64)
 
-        def round_pair(i):
-            nc.scalar.copy(
-                pair_words[:, 2 * CHUNK_START[i] : 2 * CHUNK_START[i + 1]].rearrange("p (col e) -> p col e", e=2),
-                pair_raw[i][:].rearrange("p e col -> p col e"),
+        def round_pair(engine_copy, i, lo, hi):
+            engine_copy(
+                pair_words[:, 2 * (CHUNK_START[i] + lo) : 2 * (CHUNK_START[i] + hi)].rearrange("p (col e) -> p col e", e=2),
+                pair_raw[i][:, :, lo:hi].rearrange("p e col -> p col e"),
             )
 
         def pick_pair(b):
@@ -210,7 +210,7 @@ def tile_list_listed_rating_autoencoder_kernel(tc, tab_words, tab_scales, offs, 
                     columns = slice(2 * P * b + P * half, 2 * P * b + P * (half + 1))
                     wd_operand[c, b] = (codes[:, columns].bitcast(FP8X4), pair_plane[:, columns])
 
-        h_plane = keep.tile([P, PASSES, M], U8, name="h_plane", align_bytes=64)
+        h_plane = [keep.tile([P, M], U8, name=f"h_plane{b}", align_bytes=64) for b in range(PASSES)]
         h_pairs = [keep.tile([P, 4 * M], BF16, name=f"h_rows{b}", align_bytes=64) for b in range(PASSES)]
         h_grouped = {0: keep.tile([P, 4 * M], BF16, name="h_grouped0", align_bytes=64)}
         h_codes = {}
@@ -222,7 +222,7 @@ def tile_list_listed_rating_autoencoder_kernel(tc, tab_words, tab_scales, offs, 
             for a in range(PASSES):
                 nc.tensor.matmul_mx(
                     out=acc[:], lhsT=v_codes[a, b][:, t, :].bitcast(FP8X4), lhsT_scale=v_plane[:].bitcast(U8)[4 * a : P, columns],
-                    rhs=x_codes[:, a, :].bitcast(FP8X4), rhs_scale=x_plane[:, a, :], start=(a == 0), stop=(a == PASSES - 1),
+                    rhs=x_codes[a][:].bitcast(FP8X4), rhs_scale=x_plane[a][:], start=(a == 0), stop=(a == PASSES - 1),
                 )
             nc.scalar.activation(sig[b][:, t, :], acc[:], ACT.Sigmoid)
 
@@ -237,7 +237,7 @@ def tile_list_listed_rating_autoencoder_kernel(tc, tab_words, tab_scales, offs, 
             )
 
         def quantise_h(b):
-            nc.vector.quantize_mx(out=h_codes[b].bitcast(FP8X4), scales=h_plane[:, b, :], in_=h_grouped[b][:])
+            nc.vector.quantize_mx(out=h_codes[b].bitcast(FP8X4), scales=h_plane[b][:], in_=h_grouped[b][:])
 
         sums = {}
 
@@ -249,7 +249,7 @@ def tile_list_listed_rating_autoencoder_kernel(tc, tab_words, tab_scales, offs, 
                     out=sums[c][:],
                     lhsT=w4[c // 4][:, a, :].bitcast(U8)[:, 2 * P * (c % 4) : 2 * P * (c % 4 + 1)].bitcast(FP4X4),
                     lhsT_scale=w4_plane[:, a, :].bitcast(U8)[:, P * c : P * (c + 1)],
-                    rhs=x_codes[:, a, :].bitcast(FP8X4), rhs_scale=x_plane[:, a, :],
+                    rhs=x_codes[a][:].bitcast(FP8X4), rhs_scale=x_plane[a][:],
                     start=(first and a == 0), stop=(not first and a == PASSES - 1),
                 )
 
@@ -259,7 +259,7 @@ def tile_list_listed_rating_autoencoder_kernel(tc, tab_words, tab_scales, offs, 
             for b in range(PASSES):
                 nc.tensor.matmul_mx(
                     out=sums[c][:], lhsT=wd_operand[c, b][0], lhsT_scale=wd_operand[c, b][1],
-                    rhs=h_codes[b].bitcast(FP8X4), rhs_scale=h_plane[:, b, :],
+                    rhs=h_codes[b].bitcast(FP8X4), rhs_scale=h_plane[b][:],
                     start=(first and b == 0), stop=(not first and b == PASSES - 1),
                 )
 
@@ -274,26 +274,23 @@ def tile_list_listed_rating_autoencoder_kernel(tc, tab_words, tab_scales, offs, 
 
         pick_table(0, 0, PASSES, "v_codes0")
         pick_wd(0, 0, PASSES, "picked0_0")
-        pick_table(1, 0, PASSES, "v_codes1")
-        grouped[0] = keep.tile([P, S], BF16, name="grouped0", align_bytes=64)
-        turn_wd(0, 0, PASSES, 6, nc.scalar.copy)
-        wd_codes[0] = keep.tile([P, PASSES * P], U32, name="tab1", align_bytes=64)
-        quantise_wd(0, 0, PASSES)
         for a in range(PASSES):
             round_x(nc.scalar.copy, a, 0, X_ON_SCALAR[a])
             round_x(nc.vector.tensor_copy, a, X_ON_SCALAR[a], M // 4)
-            nc.vector.quantize_mx(out=x_codes[:, a, :].bitcast(FP8X4), scales=x_plane[:, a, :], in_=x_grouped[a][:].rearrange("p m t -> p (m t)"))
+            nc.vector.quantize_mx(out=x_codes[a][:].bitcast(FP8X4), scales=x_plane[a][:], in_=x_grouped[a][:].rearrange("p m t -> p (m t)"))
+        grouped[0] = keep.tile([P, S], BF16, name="x_raw0", align_bytes=64)
+        turn_wd(0, 0, PASSES, 6, nc.scalar.copy)
+        wd_codes[0] = keep.tile([P, PASSES * P], U32, name="x_grouped1", align_bytes=64)
+        quantise_wd(0, 0, PASSES)
+        pick_table(1, 0, 1, "v_codes1a")
+        pick_table(1, 1, 2, "v_codes1b")
 
-        for c in (1, 2, 3):
+        for c in (1, 2, 3, 4):
             pick_wd(c, 0, PASSES, f"picked{c}_0")
         for b in range(PASSES):
             for t in range(4):
                 encode(b, t)
                 apply_gain(b, t)
-        bias = keep.tile([P, TILES], F32, name="bias")
-        bias_ps = banks.tile([P, P], F32, name="bank5")
-        nc.tensor.transpose(bias_ps[:], rows[:, PASS : PASS + P], ident[:])
-        nc.scalar.copy(bias[:], bias_ps[:, 0:TILES])
 
         grouped[1] = keep.tile([P, S], BF16, name="grouped1", align_bytes=64)
         turn_wd(1, 0, PASSES, 7, nc.scalar.copy)
@@ -301,58 +298,63 @@ def tile_list_listed_rating_autoencoder_kernel(tc, tab_words, tab_scales, offs, 
         grouped[2] = keep.tile([P, S], BF16, name="grouped2", align_bytes=64)
         turn_wd(2, 0, PASSES, 6, nc.scalar.copy)
 
-        after3 = on_wd3.tile([P, PASSES * M + 4 * PASSES * P], U32, name="after3", align_bytes=64, offset=8 * M)
-        h_grouped[1] = on_wd3.tile([P, 4 * M], BF16, name="h_grouped1", align_bytes=64, offset=0)
         for b in range(PASSES):
-            h_codes[b] = after3[:, M * b : M * (b + 1)]
+            h_codes[b] = on_wd3.tile([P, M], U32, name=f"h_codes{b}", align_bytes=64, offset=64 + 8 * M + 4 * M * b)[:]
         for c in range(1, 5):
-            wd_codes[c] = after3[:, PASSES * (M + P * (c - 1)) : PASSES * (M + P * c)]
-        quantise_wd(1, 0, PASSES)
-        quantise_wd(2, 0, PASSES)
-        quantise_h(0)
-        group_h(1, nc.vector.tensor_copy)
-        round_pair(0)
+            wd_codes[c] = on_wd3.tile([P, PASSES * P], U32, name=f"wd_codes{c}", align_bytes=64, offset=64 + 16 * M + 8 * P * (c - 1))
+        round_pair(nc.scalar.copy, 0, 0, CHUNKS[0])
         grouped[3] = keep.tile([P, S], BF16, name="grouped3", align_bytes=64)
         turn_wd(3, 0, PASSES, 7, nc.scalar.copy)
-        quantise_wd(3, 0, PASSES)
+        h_grouped[1] = keep.tile([P, 4 * M], BF16, name="pair_raw0", align_bytes=64)
+        group_h(1, nc.scalar.copy)
+        round_pair(nc.scalar.copy, 1, 0, CHUNKS[1])
+        quantise_h(0)
         quantise_h(1)
-        pick_wd(4, 0, PASSES, "picked4_0")
+        for c in range(1, 4):
+            quantise_wd(c, 0, PASSES)
+        add_shortcut(0, True)
+        add_shortcut(1, True)
+        bias = keep.tile([P, TILES], F32, name="bias")
+        bias_ps = banks.tile([P, P], F32, name="bank6")
+        nc.tensor.transpose(bias_ps[:], rows[:, PASS : PASS + P], ident[:])
+        nc.scalar.copy(bias[:], bias_ps[:, 0:TILES])
 
-        for i in range(1, len(CHUNKS)):
-            round_pair(i)
+        round_pair(nc.scalar.copy, 2, 0, CHUNKS[2])
+        round_pair(nc.vector.tensor_copy, 3, 0, CHUNKS[3])
         pick_pair(0)
         pick_pair(1)
         rated_early = on_last_chunk.tile([P, EARLY, M], F32, name="rated_early", align_bytes=64, offset=2 * S)
-        for c in range(EARLY):
+        for c in range(2, SUM_BANKS):
             add_shortcut(c, True)
-        for c in range(EARLY):
-            add_decoded(c, False)
+        add_decoded(0, False)
         rate(0)
-        rate(1)
         grouped[4] = on_last_chunk.tile([P, S], BF16, name="grouped4", align_bytes=64, offset=0)
         turn_wd(4, 0, PASSES, 6, nc.scalar.copy)
         quantise_wd(4, 0, PASSES)
-        rate(2)
+        for c in (1, 2, 3):
+            add_decoded(c, False)
+        rate(1)
         turn_pair(0, 7)
         turn_pair(1, 6)
-        rate(3)
-        add_shortcut(4, True)
         add_decoded(4, False)
-        rate(4)
-        for c in range(PAIR[0], TILES):
+        for c in range(SUM_BANKS, TILES):
             add_shortcut(c, True)
+        rate(2)
 
         pick_wd(7, 0, 1, "picked7_0")
         pick_wd(7, 1, 2, "picked7_1")
         quantise_pair()
         grouped[7] = keep.tile([P, S], BF16, name="grouped7", align_bytes=64)
         turn_wd(7, 0, 1, 7, nc.scalar.copy)
+        rate(3)
+        rate(4)
         for c in PAIR:
             add_decoded(c, False)
             rate(c)
-        wd_codes[7] = keep.tile([P, PASSES * P], U32, name="wd_codes7", align_bytes=64)
+        wd_codes[7] = keep.tile([P, P], U32, name="wd_codes7_0", align_bytes=64)
         quantise_wd(7, 0, 1)
         turn_wd(7, 1, 2, 6, nc.vector.tensor_copy)
+        wd_codes[7] = keep.tile([P, P], U32, name="wd_codes7_1", align_bytes=64)
         quantise_wd(7, 1, 2)
         add_decoded(7, False)
         rate(7)

@@ -25,9 +25,9 @@ PAIR = (5, 6)
 SINGLES = (0, 1, 2, 3, 4, 7)
 EARLY = 5
 SUM_BANKS = 6
-CHUNKS = (384, 640, 512, 512)
+CHUNKS = (512, 512, 512, 512)
 CHUNK_START = [sum(CHUNKS[:i]) for i in range(len(CHUNKS) + 1)]
-X_ON_SCALAR = (56, 44)
+X_ON_SCALAR = (72, 44)
 
 
 def tile_list_listed_rating_autoencoder_kernel(tc, tab_words, tab_scales, offs, x, w4_words, w4_scales, wdT, g, bo, out):
@@ -54,9 +54,6 @@ def tile_list_listed_rating_autoencoder_kernel(tc, tab_words, tab_scales, offs, 
         nc.vector.memset(w4_plane[:], 0)
         ident = keep.tile([P, P], F32, name="ident")
         make_identity(nc, ident[:])
-
-        warm = keep.tile([P, 1], F32, name="warm")
-        nc.scalar.activation(warm[:], rows[:, 0:1], ACT.Sigmoid)
 
         x_raw = [keep.tile([P, 4, M], F32, name=f"x_raw{a}", align_bytes=64) for a in range(PASSES)]
         tab = [keep.tile([P, T], I32, name=f"tab{a}", align_bytes=64) for a in range(PASSES)]
@@ -87,10 +84,10 @@ def tile_list_listed_rating_autoencoder_kernel(tc, tab_words, tab_scales, offs, 
             nc.sync.dma_start(pair_raw[i][:], pair_rows[:, :, CHUNK_START[i] : CHUNK_START[i + 1]])
 
         load_table(0)
-        nc.sync.dma_start(g_rows[:], g.rearrange("(b j) -> b j", b=PASSES))
-        load_wd(0)
         load_x(0)
+        nc.sync.dma_start(g_rows[:], g.rearrange("(b j) -> b j", b=PASSES))
         load_x(1)
+        load_table(1)
 
         v_plane = keep.tile([P, S // 4], I32, name="v_plane", align_bytes=64)
         listed_plane = keep.tile([P, S], U8, name="listed_plane", align_bytes=64)
@@ -104,17 +101,17 @@ def tile_list_listed_rating_autoencoder_kernel(tc, tab_words, tab_scales, offs, 
         for quad in range(4):
             nc.sync.dma_start(v_plane[32 * quad : 32 * quad + 8, :], ordered_plane[quad:32:4, :])
 
-        load_table(1)
+        load_wd(0)
         load_wd(1)
+        nc.sync.dma_start(rows[0:TILES, PASS : PASS + P], bo.rearrange("(c p) -> c p", p=P))
         load_wd(2)
         load_wd(3)
-        load_pair(0)
-        load_wd(4)
         load_shortcut_scales()
         load_shortcut(0)
-        nc.sync.dma_start(rows[0:TILES, PASS : PASS + P], bo.rearrange("(c p) -> c p", p=P))
-        load_pair(1)
+        load_wd(4)
         load_shortcut(1)
+        load_pair(0)
+        load_pair(1)
         load_pair(2)
         load_pair(3)
         load_wd(7)
@@ -218,7 +215,7 @@ def tile_list_listed_rating_autoencoder_kernel(tc, tab_words, tab_scales, offs, 
 
         def encode(b, t):
             columns = slice(PASSES * P * t + P * b, PASSES * P * t + P * (b + 1))
-            acc = banks.tile([P, M], F32, name=f"bank{t}")
+            acc = banks.tile([P, M], F32, name=f"bank{(4 * b + t + SUM_BANKS) % 8}")
             for a in range(PASSES):
                 nc.tensor.matmul_mx(
                     out=acc[:], lhsT=v_codes[a, b][:, t, :].bitcast(FP8X4), lhsT_scale=v_plane[:].bitcast(U8)[4 * a : P, columns],
@@ -273,58 +270,55 @@ def tile_list_listed_rating_autoencoder_kernel(tc, tab_words, tab_scales, offs, 
                 nc.sync.dma_start(out[P * c : P * (c + 1), users], rated)
 
         pick_table(0, 0, PASSES, "v_codes0")
-        pick_wd(0, 0, PASSES, "picked0_0")
         for a in range(PASSES):
             round_x(nc.scalar.copy, a, 0, X_ON_SCALAR[a])
             round_x(nc.vector.tensor_copy, a, X_ON_SCALAR[a], M // 4)
             nc.vector.quantize_mx(out=x_codes[a][:].bitcast(FP8X4), scales=x_plane[a][:], in_=x_grouped[a][:].rearrange("p m t -> p (m t)"))
-        grouped[0] = keep.tile([P, S], BF16, name="x_raw0", align_bytes=64)
-        turn_wd(0, 0, PASSES, 6, nc.scalar.copy)
-        wd_codes[0] = keep.tile([P, PASSES * P], U32, name="x_grouped1", align_bytes=64)
-        quantise_wd(0, 0, PASSES)
         pick_table(1, 0, 1, "v_codes1a")
         pick_table(1, 1, 2, "v_codes1b")
 
-        for c in (1, 2, 3, 4):
+        for c in range(5):
             pick_wd(c, 0, PASSES, f"picked{c}_0")
         for b in range(PASSES):
             for t in range(4):
                 encode(b, t)
                 apply_gain(b, t)
 
+        bias = keep.tile([P, TILES], F32, name="bias")
+        bias_ps = banks.tile([P, P], F32, name="bank5")
+        nc.tensor.transpose(bias_ps[:], rows[:, PASS : PASS + P], ident[:])
+        nc.scalar.copy(bias[:], bias_ps[:, 0:TILES])
+        grouped[0] = keep.tile([P, S], BF16, name="grouped0", align_bytes=64)
+        turn_wd(0, 0, PASSES, 6, nc.scalar.copy)
+        group_h(0, nc.scalar.copy)
         grouped[1] = keep.tile([P, S], BF16, name="grouped1", align_bytes=64)
         turn_wd(1, 0, PASSES, 7, nc.scalar.copy)
-        group_h(0, nc.scalar.copy)
         grouped[2] = keep.tile([P, S], BF16, name="grouped2", align_bytes=64)
         turn_wd(2, 0, PASSES, 6, nc.scalar.copy)
 
         for b in range(PASSES):
             h_codes[b] = on_wd3.tile([P, M], U32, name=f"h_codes{b}", align_bytes=64, offset=64 + 8 * M + 4 * M * b)[:]
-        for c in range(1, 5):
-            wd_codes[c] = on_wd3.tile([P, PASSES * P], U32, name=f"wd_codes{c}", align_bytes=64, offset=64 + 16 * M + 8 * P * (c - 1))
-        round_pair(nc.scalar.copy, 0, 0, CHUNKS[0])
+        for c in range(4):
+            wd_codes[c] = on_wd3.tile([P, PASSES * P], U32, name=f"wd_codes{c}", align_bytes=64, offset=64 + 16 * M + 8 * P * c)
+        wd_codes[4] = keep.tile([P, PASSES * P], U32, name="wd_codes4", align_bytes=64)
         grouped[3] = keep.tile([P, S], BF16, name="grouped3", align_bytes=64)
         turn_wd(3, 0, PASSES, 7, nc.scalar.copy)
-        h_grouped[1] = keep.tile([P, 4 * M], BF16, name="pair_raw0", align_bytes=64)
+        h_grouped[1] = keep.tile([P, 4 * M], BF16, name="wd3", align_bytes=64)
         group_h(1, nc.scalar.copy)
-        round_pair(nc.scalar.copy, 1, 0, CHUNKS[1])
         quantise_h(0)
         quantise_h(1)
+        quantise_wd(0, 0, PASSES)
         for c in range(1, 4):
             quantise_wd(c, 0, PASSES)
-        add_shortcut(0, True)
-        add_shortcut(1, True)
-        bias = keep.tile([P, TILES], F32, name="bias")
-        bias_ps = banks.tile([P, P], F32, name="bank6")
-        nc.tensor.transpose(bias_ps[:], rows[:, PASS : PASS + P], ident[:])
-        nc.scalar.copy(bias[:], bias_ps[:, 0:TILES])
 
-        round_pair(nc.scalar.copy, 2, 0, CHUNKS[2])
-        round_pair(nc.vector.tensor_copy, 3, 0, CHUNKS[3])
+        for i in range(len(CHUNKS) - 1):
+            round_pair(nc.scalar.copy, i, 0, CHUNKS[i])
+        round_pair(nc.scalar.copy, 3, 0, 128)
+        round_pair(nc.vector.tensor_copy, 3, 128, CHUNKS[3])
         pick_pair(0)
         pick_pair(1)
         rated_early = on_last_chunk.tile([P, EARLY, M], F32, name="rated_early", align_bytes=64, offset=2 * S)
-        for c in range(2, SUM_BANKS):
+        for c in range(SUM_BANKS):
             add_shortcut(c, True)
         add_decoded(0, False)
         rate(0)

@@ -25,8 +25,9 @@ PAIR = (5, 6)
 SINGLES = (0, 1, 2, 3, 4, 7)
 EARLY = 5
 SUM_BANKS = 6
-CHUNKS = (512, 512, 512, 512)
-CHUNK_START = [sum(CHUNKS[:i]) for i in range(len(CHUNKS) + 1)]
+CHUNKS = 4
+CHUNK = T // CHUNKS
+LAST_ON_SCALAR = 192
 X_ON_SCALAR = (72, 44)
 
 
@@ -34,9 +35,9 @@ def tile_list_listed_rating_autoencoder_kernel(tc, tab_words, tab_scales, offs, 
     nc = tc.nc
     with ExitStack() as ctx:
         keep = ctx.enter_context(tc.tile_pool(name="keep", bufs=1))
-        ring = ctx.enter_context(tc.tile_pool(name="ring", bufs=6))
+        ring = ctx.enter_context(tc.tile_pool(name="ring", bufs=4))
         on_last_chunk = ctx.enter_context(tc.tile_pool(name="late", bufs=1))
-        on_wd3 = ctx.enter_context(tc.tile_pool(name="mid", bufs=1))
+        on_wd4 = ctx.enter_context(tc.tile_pool(name="mid", bufs=1))
         banks = ctx.enter_context(tc.psum_pool(name="banks", bufs=1))
 
         offsets = keep.tile([P, S // 16], U16, name="offsets")
@@ -58,10 +59,10 @@ def tile_list_listed_rating_autoencoder_kernel(tc, tab_words, tab_scales, offs, 
         x_raw = [keep.tile([P, 4, M], F32, name=f"x_raw{a}", align_bytes=64) for a in range(PASSES)]
         tab = [keep.tile([P, T], I32, name=f"tab{a}", align_bytes=64) for a in range(PASSES)]
         wd = {c: keep.tile([P, T], F32, name=f"wd{c}", align_bytes=64) for c in SINGLES if c != 4}
-        wd[4] = on_wd3.tile([P, T], F32, name="wd4", align_bytes=64, offset=8 * M)
+        wd[4] = on_wd4.tile([P, T], F32, name="wd4", align_bytes=64, offset=0)
         w4 = [keep.tile([P, PASSES, N // 4], I32, name=f"w4_{half}", align_bytes=64) for half in range(2)]
-        pair_raw = [keep.tile([P, 2, CHUNKS[i]], F32, name=f"pair_raw{i}", align_bytes=64) for i in range(len(CHUNKS) - 1)]
-        pair_raw.append(on_last_chunk.tile([P, 2, CHUNKS[-1]], F32, name="pair_raw_last", align_bytes=64, offset=2 * S - 64))
+        pair_raw = [keep.tile([P, 2, CHUNK], F32, name=f"pair_raw{i}", align_bytes=64) for i in range(CHUNKS - 1)]
+        pair_raw.append(on_last_chunk.tile([P, 2, CHUNK], F32, name="pair_raw_last", align_bytes=64, offset=0))
         pair_rows = wdT[PAIR[0] * P : (PAIR[1] + 1) * P, :].rearrange("(p e) col -> p e col", e=2)
 
         def load_table(a):
@@ -81,7 +82,7 @@ def tile_list_listed_rating_autoencoder_kernel(tc, tab_words, tab_scales, offs, 
                 nc.sync.dma_start(w4_plane[32 * quad : 32 * quad + 4, :, :], w4_scales[:, 4 * quad : 4 * quad + 4, :].bitcast(I32).rearrange("a r w -> r a w"))
 
         def load_pair(i):
-            nc.sync.dma_start(pair_raw[i][:], pair_rows[:, :, CHUNK_START[i] : CHUNK_START[i + 1]])
+            nc.sync.dma_start(pair_raw[i][:], pair_rows[:, :, CHUNK * i : CHUNK * (i + 1)])
 
         load_table(0)
         load_x(0)
@@ -109,11 +110,9 @@ def tile_list_listed_rating_autoencoder_kernel(tc, tab_words, tab_scales, offs, 
         load_shortcut_scales()
         load_shortcut(0)
         load_wd(4)
+        for i in range(CHUNKS):
+            load_pair(i)
         load_shortcut(1)
-        load_pair(0)
-        load_pair(1)
-        load_pair(2)
-        load_pair(3)
         load_wd(7)
 
         gains = keep.tile([P, 4, PASSES], F32, name="gains")
@@ -142,7 +141,6 @@ def tile_list_listed_rating_autoencoder_kernel(tc, tab_words, tab_scales, offs, 
             for b in range(b0, b1):
                 v_codes[a, b] = codes[:, :, P * (b - b0) : P * (b - b0 + 1)]
 
-        wd_codes = {}
         wd_operand = {}
         picked = {}
         grouped = {}
@@ -166,11 +164,12 @@ def tile_list_listed_rating_autoencoder_kernel(tc, tab_words, tab_scales, offs, 
                 turned[:].rearrange("p (u b) n -> p b n u", u=2)[:, b0:b1],
             )
 
-        def quantise_wd(c, b0, b1):
+        def quantise_wd(c, b0, b1, codes):
             plane = keep.tile([P, P * (b1 - b0)], U8, name=f"wd_plane{c}_{b0}", align_bytes=64)
-            nc.vector.quantize_mx(out=wd_codes[c][:].bitcast(FP8X4), scales=plane[:], in_=grouped[c][:, PASS * b0 : PASS * b1])
+            nc.vector.quantize_mx(out=codes[:].bitcast(FP8X4), scales=plane[:], in_=grouped[c][:, PASS * b0 : PASS * b1])
             for b in range(b0, b1):
-                wd_operand[c, b] = (wd_codes[c][:, P * (b - b0) : P * (b - b0 + 1)].bitcast(FP8X4), plane[:, P * (b - b0) : P * (b - b0 + 1)])
+                columns = slice(P * (b - b0), P * (b - b0 + 1))
+                wd_operand[c, b] = (codes[:, columns].bitcast(FP8X4), plane[:, columns])
 
         pair_words = keep.tile([P, 2 * T], BF16, name="pair_words", align_bytes=64)
         pair_picked = [keep.tile([P, PASS], U32, name=f"pair_picked{b}", align_bytes=64) for b in range(PASSES)]
@@ -179,7 +178,7 @@ def tile_list_listed_rating_autoencoder_kernel(tc, tab_words, tab_scales, offs, 
 
         def round_pair(engine_copy, i, lo, hi):
             engine_copy(
-                pair_words[:, 2 * (CHUNK_START[i] + lo) : 2 * (CHUNK_START[i] + hi)].rearrange("p (col e) -> p col e", e=2),
+                pair_words[:, 2 * (CHUNK * i + lo) : 2 * (CHUNK * i + hi)].rearrange("p (col e) -> p col e", e=2),
                 pair_raw[i][:, :, lo:hi].rearrange("p e col -> p col e"),
             )
 
@@ -227,37 +226,34 @@ def tile_list_listed_rating_autoencoder_kernel(tc, tab_words, tab_scales, offs, 
             pairs = h_pairs[b][:].rearrange("p (u m e) -> p u m e", u=2, e=2)
             nc.gpsimd.tensor_scalar(pairs[:, t // 2, :, t % 2], sig[b][:, t, :], gains[:, t, b : b + 1], 0.0, ALU.mult, ALU.add)
 
-        def group_h(b, engine_copy):
-            engine_copy(
+        def group_h(b):
+            nc.scalar.copy(
                 h_grouped[b][:].bitcast(F32).rearrange("p (m u) -> p m u", u=2),
                 h_pairs[b][:].bitcast(F32).rearrange("p (u m) -> p m u", u=2),
             )
 
         def quantise_h(b):
-            nc.vector.quantize_mx(out=h_codes[b].bitcast(FP8X4), scales=h_plane[b][:], in_=h_grouped[b][:])
+            nc.vector.quantize_mx(out=h_codes[b][:].bitcast(FP8X4), scales=h_plane[b][:], in_=h_grouped[b][:])
 
         sums = {}
 
-        def add_shortcut(c, first):
-            if first:
-                sums[c] = banks.tile([P, M], F32, name=f"bank{c % SUM_BANKS}")
+        def add_shortcut(c):
+            sums[c] = banks.tile([P, M], F32, name=f"bank{c % SUM_BANKS}")
             for a in range(PASSES):
                 nc.tensor.matmul_mx(
                     out=sums[c][:],
                     lhsT=w4[c // 4][:, a, :].bitcast(U8)[:, 2 * P * (c % 4) : 2 * P * (c % 4 + 1)].bitcast(FP4X4),
                     lhsT_scale=w4_plane[:, a, :].bitcast(U8)[:, P * c : P * (c + 1)],
                     rhs=x_codes[a][:].bitcast(FP8X4), rhs_scale=x_plane[a][:],
-                    start=(first and a == 0), stop=(not first and a == PASSES - 1),
+                    start=(a == 0), stop=False,
                 )
 
-        def add_decoded(c, first):
-            if first:
-                sums[c] = banks.tile([P, M], F32, name=f"bank{c % SUM_BANKS}")
+        def add_decoded(c):
             for b in range(PASSES):
                 nc.tensor.matmul_mx(
                     out=sums[c][:], lhsT=wd_operand[c, b][0], lhsT_scale=wd_operand[c, b][1],
-                    rhs=h_codes[b].bitcast(FP8X4), rhs_scale=h_plane[b][:],
-                    start=(first and b == 0), stop=(not first and b == PASSES - 1),
+                    rhs=h_codes[b][:].bitcast(FP8X4), rhs_scale=h_plane[b][:],
+                    start=False, stop=(b == PASSES - 1),
                 )
 
         def rate(c):
@@ -269,6 +265,10 @@ def tile_list_listed_rating_autoencoder_kernel(tc, tab_words, tab_scales, offs, 
                 nc.scalar.activation(rated, sums[c][:, users], ACT.Tanh, bias=bias[:, c : c + 1])
                 nc.sync.dma_start(out[P * c : P * (c + 1), users], rated)
 
+        def turn_whole(c, name):
+            grouped[c] = keep.tile([P, S], BF16, name=name, align_bytes=64)
+            turn_wd(c, 0, PASSES, SUM_BANKS + c % 2, nc.scalar.copy)
+
         pick_table(0, 0, PASSES, "v_codes0")
         for a in range(PASSES):
             round_x(nc.scalar.copy, a, 0, X_ON_SCALAR[a])
@@ -277,7 +277,7 @@ def tile_list_listed_rating_autoencoder_kernel(tc, tab_words, tab_scales, offs, 
         pick_table(1, 0, 1, "v_codes1a")
         pick_table(1, 1, 2, "v_codes1b")
 
-        for c in range(5):
+        for c in range(EARLY):
             pick_wd(c, 0, PASSES, f"picked{c}_0")
         for b in range(PASSES):
             for t in range(4):
@@ -288,51 +288,43 @@ def tile_list_listed_rating_autoencoder_kernel(tc, tab_words, tab_scales, offs, 
         bias_ps = banks.tile([P, P], F32, name="bank5")
         nc.tensor.transpose(bias_ps[:], rows[:, PASS : PASS + P], ident[:])
         nc.scalar.copy(bias[:], bias_ps[:, 0:TILES])
-        grouped[0] = keep.tile([P, S], BF16, name="grouped0", align_bytes=64)
-        turn_wd(0, 0, PASSES, 6, nc.scalar.copy)
-        group_h(0, nc.scalar.copy)
-        grouped[1] = keep.tile([P, S], BF16, name="grouped1", align_bytes=64)
-        turn_wd(1, 0, PASSES, 7, nc.scalar.copy)
-        grouped[2] = keep.tile([P, S], BF16, name="grouped2", align_bytes=64)
-        turn_wd(2, 0, PASSES, 6, nc.scalar.copy)
+        turn_whole(0, "grouped0")
+        group_h(0)
+        for c in (1, 2, 3):
+            turn_whole(c, f"grouped{c}")
+        h_grouped[1] = keep.tile([P, 4 * M], BF16, name="wd3", align_bytes=64)
+        group_h(1)
 
         for b in range(PASSES):
-            h_codes[b] = on_wd3.tile([P, M], U32, name=f"h_codes{b}", align_bytes=64, offset=64 + 8 * M + 4 * M * b)[:]
+            h_codes[b] = on_wd4.tile([P, M], U32, name=f"h_codes{b}", align_bytes=64, offset=4 * M * b)
+            quantise_h(b)
         for c in range(4):
-            wd_codes[c] = on_wd3.tile([P, PASSES * P], U32, name=f"wd_codes{c}", align_bytes=64, offset=64 + 16 * M + 8 * P * c)
-        wd_codes[4] = keep.tile([P, PASSES * P], U32, name="wd_codes4", align_bytes=64)
-        grouped[3] = keep.tile([P, S], BF16, name="grouped3", align_bytes=64)
-        turn_wd(3, 0, PASSES, 7, nc.scalar.copy)
-        h_grouped[1] = keep.tile([P, 4 * M], BF16, name="wd3", align_bytes=64)
-        group_h(1, nc.scalar.copy)
-        quantise_h(0)
-        quantise_h(1)
-        quantise_wd(0, 0, PASSES)
-        for c in range(1, 4):
-            quantise_wd(c, 0, PASSES)
+            codes = on_wd4.tile([P, PASSES * P], U32, name=f"wd_codes{c}", align_bytes=64, offset=4 * PASSES * (M + P * c))
+            quantise_wd(c, 0, PASSES, codes)
 
-        for i in range(len(CHUNKS) - 1):
-            round_pair(nc.scalar.copy, i, 0, CHUNKS[i])
-        round_pair(nc.scalar.copy, 3, 0, 128)
-        round_pair(nc.vector.tensor_copy, 3, 128, CHUNKS[3])
+        round_pair(nc.scalar.copy, 0, 0, CHUNK)
+        round_pair(nc.scalar.copy, 1, 0, CHUNK)
+        turn_whole(4, "pair_raw1")
+        quantise_wd(4, 0, PASSES, keep.tile([P, PASSES * P], U32, name="wd_codes4", align_bytes=64))
+        round_pair(nc.scalar.copy, 2, 0, CHUNK)
+        round_pair(nc.scalar.copy, 3, 0, LAST_ON_SCALAR)
+        round_pair(nc.vector.tensor_copy, 3, LAST_ON_SCALAR, CHUNK)
         pick_pair(0)
         pick_pair(1)
-        rated_early = on_last_chunk.tile([P, EARLY, M], F32, name="rated_early", align_bytes=64, offset=2 * S)
+
+        rated_early = on_last_chunk.tile([P, EARLY, M], F32, name="rated_early", align_bytes=64, offset=0)
         for c in range(SUM_BANKS):
-            add_shortcut(c, True)
-        add_decoded(0, False)
+            add_shortcut(c)
+        add_decoded(0)
         rate(0)
-        grouped[4] = on_last_chunk.tile([P, S], BF16, name="grouped4", align_bytes=64, offset=0)
-        turn_wd(4, 0, PASSES, 6, nc.scalar.copy)
-        quantise_wd(4, 0, PASSES)
         for c in (1, 2, 3):
-            add_decoded(c, False)
+            add_decoded(c)
         rate(1)
         turn_pair(0, 7)
         turn_pair(1, 6)
-        add_decoded(4, False)
+        add_decoded(4)
         for c in range(SUM_BANKS, TILES):
-            add_shortcut(c, True)
+            add_shortcut(c)
         rate(2)
 
         pick_wd(7, 0, 1, "picked7_0")
@@ -343,12 +335,10 @@ def tile_list_listed_rating_autoencoder_kernel(tc, tab_words, tab_scales, offs, 
         rate(3)
         rate(4)
         for c in PAIR:
-            add_decoded(c, False)
+            add_decoded(c)
             rate(c)
-        wd_codes[7] = keep.tile([P, P], U32, name="wd_codes7_0", align_bytes=64)
-        quantise_wd(7, 0, 1)
+        quantise_wd(7, 0, 1, keep.tile([P, P], U32, name="wd_codes7_0", align_bytes=64))
         turn_wd(7, 1, 2, 6, nc.vector.tensor_copy)
-        wd_codes[7] = keep.tile([P, P], U32, name="wd_codes7_1", align_bytes=64)
-        quantise_wd(7, 1, 2)
-        add_decoded(7, False)
+        quantise_wd(7, 1, 2, keep.tile([P, P], U32, name="wd_codes7_1", align_bytes=64))
+        add_decoded(7)
         rate(7)

@@ -25,9 +25,10 @@ PAIR = (5, 6)
 SINGLES = (0, 1, 2, 3, 4, 7)
 EARLY = 5
 SUM_BANKS = 6
-CHUNKS = 4
-CHUNK = T // CHUNKS
-LAST_ON_SCALAR = 192
+SUM_BANK = (0, 1, 2, 3, 4, 1, 0, 6)
+CHUNK_EDGES = (0, 512, 1024, 1536, 1792, 2048)
+CHUNKS = len(CHUNK_EDGES) - 1
+LAST_ON_SCALAR = 384
 X_ON_SCALAR = (72, 44)
 
 
@@ -45,7 +46,7 @@ def tile_list_listed_rating_autoencoder_kernel(tc, tab_words, tab_scales, offs, 
 
         tab_plane = keep.tile([P, T // 4], I32, name="tab_plane", align_bytes=64)
         w4_plane = keep.tile([P, PASSES, N // 4], I32, name="w4_plane", align_bytes=64)
-        rows = keep.tile([P, 5 * P], F32, name="rows")
+        rows = keep.tile([P, 5 * P], F32, name="rows", align_bytes=64)
         g_rows = keep.tile([PASSES, PASS], F32, name="g_rows")
         for a in range(PASSES):
             nc.sync.dma_start(tab_plane[16 * a : 16 * (a + 1), :], tab_scales[a].bitcast(I32).rearrange("(quad r) w -> r quad w", r=4))
@@ -58,11 +59,12 @@ def tile_list_listed_rating_autoencoder_kernel(tc, tab_words, tab_scales, offs, 
 
         x_raw = [keep.tile([P, 4, M], F32, name=f"x_raw{a}", align_bytes=64) for a in range(PASSES)]
         tab = [keep.tile([P, T], I32, name=f"tab{a}", align_bytes=64) for a in range(PASSES)]
-        wd = {c: keep.tile([P, T], F32, name=f"wd{c}", align_bytes=64) for c in SINGLES if c != 4}
-        wd[4] = on_wd4.tile([P, T], F32, name="wd4", align_bytes=64, offset=0)
+        wd = {c: keep.tile([P, T], F32, name=f"wd{c}", align_bytes=64) for c in SINGLES if c != 3}
+        wd[3] = on_wd4.tile([P, T], F32, name="wd3", align_bytes=64, offset=0)
         w4 = [keep.tile([P, PASSES, N // 4], I32, name=f"w4_{half}", align_bytes=64) for half in range(2)]
-        pair_raw = [keep.tile([P, 2, CHUNK], F32, name=f"pair_raw{i}", align_bytes=64) for i in range(CHUNKS - 1)]
-        pair_raw.append(on_last_chunk.tile([P, 2, CHUNK], F32, name="pair_raw_last", align_bytes=64, offset=0))
+        widths = [CHUNK_EDGES[i + 1] - CHUNK_EDGES[i] for i in range(CHUNKS)]
+        pair_raw = {i: keep.tile([P, 2, widths[i]], F32, name=f"pair_raw{i}", align_bytes=64) for i in range(CHUNKS) if i != 3}
+        pair_raw[3] = on_last_chunk.tile([P, 2, widths[3]], F32, name="pair_raw3", align_bytes=64, offset=3 * S)
         pair_rows = wdT[PAIR[0] * P : (PAIR[1] + 1) * P, :].rearrange("(p e) col -> p e col", e=2)
 
         def load_table(a):
@@ -78,11 +80,12 @@ def tile_list_listed_rating_autoencoder_kernel(tc, tab_words, tab_scales, offs, 
             nc.sync.dma_start(w4[half][:], w4_words.bitcast(I32).rearrange("a p w -> p a w")[:, :, N // 4 * half : N // 4 * (half + 1)])
 
         def load_shortcut_scales():
-            for quad in range(4):
-                nc.sync.dma_start(w4_plane[32 * quad : 32 * quad + 4, :, :], w4_scales[:, 4 * quad : 4 * quad + 4, :].bitcast(I32).rearrange("a r w -> r a w"))
+            rows_of_quads = w4_scales.bitcast(I32).rearrange("a (quad r) w -> r quad a w", r=4)
+            for r in range(4):
+                nc.sync.dma_start(w4_plane[r:P:32, :, :], rows_of_quads[r])
 
         def load_pair(i):
-            nc.sync.dma_start(pair_raw[i][:], pair_rows[:, :, CHUNK * i : CHUNK * (i + 1)])
+            nc.sync.dma_start(pair_raw[i][:], pair_rows[:, :, CHUNK_EDGES[i] : CHUNK_EDGES[i + 1]])
 
         load_table(0)
         load_x(0)
@@ -99,14 +102,14 @@ def tile_list_listed_rating_autoencoder_kernel(tc, tab_words, tab_scales, offs, 
             ordered_plane[:].rearrange("p (t d) -> p t d", t=4),
             listed_plane[:].bitcast(I32).rearrange("p (d t) -> p t d", t=4),
         )
-        for quad in range(4):
+        for quad in (0, 2, 1, 3):
             nc.sync.dma_start(v_plane[32 * quad : 32 * quad + 8, :], ordered_plane[quad:32:4, :])
 
         load_wd(0)
         load_wd(1)
-        nc.sync.dma_start(rows[0:TILES, PASS : PASS + P], bo.rearrange("(c p) -> c p", p=P))
         load_wd(2)
         load_wd(3)
+        nc.sync.dma_start(rows[0:TILES, PASS : PASS + P], bo.rearrange("(c p) -> c p", p=P))
         load_shortcut_scales()
         load_shortcut(0)
         load_wd(4)
@@ -152,17 +155,23 @@ def tile_list_listed_rating_autoencoder_kernel(tc, tab_words, tab_scales, offs, 
                 wd[c][:].indirect(offsets[:, 32 * b0 : 32 * b1]),
             )
 
-        def turn_wd(c, b0, b1, bank, engine_copy):
+        def transpose_wd(c, b0, b1, bank):
             words = picked[c, b0][:].bitcast(F32)
             turned = banks.tile([P, 4, P], F32, name=f"bank{bank}")
             for b in range(b0, b1):
                 for u in range(2):
                     start = P * ((b1 - b0) * u + b - b0)
                     nc.tensor.transpose(turned[:, 2 * u + b, :], words[:, start : start + P], ident[:])
+            return turned
+
+        def copy_out_wd(c, b0, b1, turned, engine_copy):
             engine_copy(
                 grouped[c][:].bitcast(F32).rearrange("p (b n u) -> p b n u", b=2, u=2)[:, b0:b1],
                 turned[:].rearrange("p (u b) n -> p b n u", u=2)[:, b0:b1],
             )
+
+        def turn_wd(c, b0, b1, bank, engine_copy):
+            copy_out_wd(c, b0, b1, transpose_wd(c, b0, b1, bank), engine_copy)
 
         def quantise_wd(c, b0, b1, codes):
             plane = keep.tile([P, P * (b1 - b0)], U8, name=f"wd_plane{c}_{b0}", align_bytes=64)
@@ -173,13 +182,12 @@ def tile_list_listed_rating_autoencoder_kernel(tc, tab_words, tab_scales, offs, 
 
         pair_words = keep.tile([P, 2 * T], BF16, name="pair_words", align_bytes=64)
         pair_picked = [keep.tile([P, PASS], U32, name=f"pair_picked{b}", align_bytes=64) for b in range(PASSES)]
-        pair_grouped = keep.tile([P, 2 * S], BF16, name="pair_grouped", align_bytes=64)
-        pair_plane = keep.tile([P, PASSES * 2 * P], U8, name="pair_plane", align_bytes=64)
+        pair_grouped = keep.tile([P, 2, S], BF16, name="pair_grouped", align_bytes=64)
 
-        def round_pair(engine_copy, i, lo, hi):
+        def round_pair(engine_copy, i):
             engine_copy(
-                pair_words[:, 2 * (CHUNK * i + lo) : 2 * (CHUNK * i + hi)].rearrange("p (col e) -> p col e", e=2),
-                pair_raw[i][:, :, lo:hi].rearrange("p e col -> p col e"),
+                pair_words[:, 2 * CHUNK_EDGES[i] : 2 * CHUNK_EDGES[i + 1]].rearrange("p (col e) -> p col e", e=2),
+                pair_raw[i][:].rearrange("p e col -> p col e"),
             )
 
         def pick_pair(b):
@@ -194,17 +202,9 @@ def tile_list_listed_rating_autoencoder_kernel(tc, tab_words, tab_scales, offs, 
             for t in range(4):
                 nc.tensor.transpose(turned[:, t, :], words[:, P * t : P * (t + 1)], ident[:])
             nc.scalar.copy(
-                pair_grouped[:, S * b : S * (b + 1)].rearrange("p (n t) -> p n t", t=4),
-                turned[:].bitcast(BF16).rearrange("p t n -> p n t"),
+                pair_grouped[:, :, PASS * b : PASS * (b + 1)].rearrange("p half (n t) -> p half n t", t=4),
+                turned[:].bitcast(BF16).rearrange("p t (half n) -> p half n t", half=2),
             )
-
-        def quantise_pair():
-            codes = keep.tile([P, PASSES * 2 * P], U32, name="pair_codes", align_bytes=64)
-            nc.vector.quantize_mx(out=codes[:].bitcast(FP8X4), scales=pair_plane[:], in_=pair_grouped[:])
-            for half, c in enumerate(PAIR):
-                for b in range(PASSES):
-                    columns = slice(2 * P * b + P * half, 2 * P * b + P * (half + 1))
-                    wd_operand[c, b] = (codes[:, columns].bitcast(FP8X4), pair_plane[:, columns])
 
         h_plane = [keep.tile([P, M], U8, name=f"h_plane{b}", align_bytes=64) for b in range(PASSES)]
         h_pairs = [keep.tile([P, 4 * M], BF16, name=f"h_rows{b}", align_bytes=64) for b in range(PASSES)]
@@ -238,7 +238,7 @@ def tile_list_listed_rating_autoencoder_kernel(tc, tab_words, tab_scales, offs, 
         sums = {}
 
         def add_shortcut(c):
-            sums[c] = banks.tile([P, M], F32, name=f"bank{c % SUM_BANKS}")
+            sums[c] = banks.tile([P, M], F32, name=f"bank{SUM_BANK[c]}")
             for a in range(PASSES):
                 nc.tensor.matmul_mx(
                     out=sums[c][:],
@@ -261,7 +261,7 @@ def tile_list_listed_rating_autoencoder_kernel(tc, tab_words, tab_scales, offs, 
             width = M // parts
             for part in range(parts):
                 users = slice(width * part, width * (part + 1))
-                rated = rated_early[:, c, :] if c < EARLY else ring.tile([P, width], F32, name="rated")[:]
+                rated = rated_early[c] if c < EARLY else ring.tile([P, width], F32, name="rated")[:]
                 nc.scalar.activation(rated, sums[c][:, users], ACT.Tanh, bias=bias[:, c : c + 1])
                 nc.sync.dma_start(out[P * c : P * (c + 1), users], rated)
 
@@ -277,7 +277,7 @@ def tile_list_listed_rating_autoencoder_kernel(tc, tab_words, tab_scales, offs, 
         pick_table(1, 0, 1, "v_codes1a")
         pick_table(1, 1, 2, "v_codes1b")
 
-        for c in range(EARLY):
+        for c in range(EARLY - 1):
             pick_wd(c, 0, PASSES, f"picked{c}_0")
         for b in range(PASSES):
             for t in range(4):
@@ -288,57 +288,80 @@ def tile_list_listed_rating_autoencoder_kernel(tc, tab_words, tab_scales, offs, 
         bias_ps = banks.tile([P, P], F32, name="bank5")
         nc.tensor.transpose(bias_ps[:], rows[:, PASS : PASS + P], ident[:])
         nc.scalar.copy(bias[:], bias_ps[:, 0:TILES])
-        turn_whole(0, "grouped0")
-        group_h(0)
-        for c in (1, 2, 3):
-            turn_whole(c, f"grouped{c}")
-        h_grouped[1] = keep.tile([P, 4 * M], BF16, name="wd3", align_bytes=64)
+        def quantise_two(c, values, codes):
+            plane = keep.tile([P, 2 * PASSES * P], U8, name=f"plane_two{c}", align_bytes=64)
+            nc.vector.quantize_mx(out=codes[:].bitcast(FP8X4), scales=plane[:], in_=values[:])
+            for n in range(2 * PASSES):
+                columns = slice(P * n, P * (n + 1))
+                wd_operand[c + n // PASSES, n % PASSES] = (codes[:, columns].bitcast(FP8X4), plane[:, columns])
+
+        grouped01 = keep.tile([P, 2 * S], BF16, name="grouped01", align_bytes=64)
+        for c in range(2):
+            grouped[c] = grouped01[:, S * c : S * (c + 1)]
+            turn_wd(c, 0, PASSES, SUM_BANKS + c, nc.scalar.copy)
+            if c == 0:
+                group_h(0)
+        turn_whole(2, "grouped2")
+        h_grouped[1] = keep.tile([P, 4 * M], BF16, name="h_grouped1", align_bytes=64)
         group_h(1)
-
-        for b in range(PASSES):
-            h_codes[b] = on_wd4.tile([P, M], U32, name=f"h_codes{b}", align_bytes=64, offset=4 * M * b)
-            quantise_h(b)
         for c in range(4):
-            codes = on_wd4.tile([P, PASSES * P], U32, name=f"wd_codes{c}", align_bytes=64, offset=4 * PASSES * (M + P * c))
-            quantise_wd(c, 0, PASSES, codes)
+            add_shortcut(c)
 
-        round_pair(nc.scalar.copy, 0, 0, CHUNK)
-        round_pair(nc.scalar.copy, 1, 0, CHUNK)
-        turn_whole(4, "pair_raw1")
-        quantise_wd(4, 0, PASSES, keep.tile([P, PASSES * P], U32, name="wd_codes4", align_bytes=64))
-        round_pair(nc.scalar.copy, 2, 0, CHUNK)
-        round_pair(nc.scalar.copy, 3, 0, LAST_ON_SCALAR)
-        round_pair(nc.vector.tensor_copy, 3, LAST_ON_SCALAR, CHUNK)
+        h_codes[0] = keep.tile([P, M], U32, name="rows", align_bytes=64)
+        quantise_h(0)
+        quantise_two(0, grouped01, on_wd4.tile([P, 2 * PASSES * P], U32, name="codes01", align_bytes=64, offset=4 * PASSES * M))
+        h_codes[1] = on_wd4.tile([P, M], U32, name="h_codes1", align_bytes=64, offset=4 * M)
+        quantise_h(1)
+        quantise_wd(2, 0, PASSES, on_wd4.tile([P, PASSES * P], U32, name="codes2", align_bytes=64, offset=4 * PASSES * (M + 2 * P)))
+        pick_wd(4, 0, PASSES, "h_grouped1")
+
+        round_pair(nc.scalar.copy, 0)
+        round_pair(nc.scalar.copy, 1)
+        nc.gpsimd.tensor_copy(pair_words[:, 2 * CHUNK_EDGES[2] : 2 * CHUNK_EDGES[3]].rearrange("p (col e) -> p e col", e=2), pair_raw[2][:])
+        rated0 = keep.tile([P, M], F32, name="pair_raw1", align_bytes=64)
+        rated_early = {0: rated0[:]}
+        add_decoded(0)
+        rate(0)
+        round_pair(nc.scalar.copy, 3)
+        round_pair(nc.vector.tensor_copy, 4)
         pick_pair(0)
         pick_pair(1)
 
-        rated_early = on_last_chunk.tile([P, EARLY, M], F32, name="rated_early", align_bytes=64, offset=0)
-        for c in range(SUM_BANKS):
-            add_shortcut(c)
-        add_decoded(0)
-        rate(0)
-        for c in (1, 2, 3):
+        rated_later = on_last_chunk.tile([P, 4, M], F32, name="rated_later", align_bytes=64, offset=4 * S)
+        for c in range(1, EARLY):
+            rated_early[c] = rated_later[:, c - 1, :]
+        grouped34 = on_last_chunk.tile([P, 2 * S], BF16, name="grouped34", align_bytes=64, offset=0)
+        for c in (1, 2):
             add_decoded(c)
-        rate(1)
-        turn_pair(0, 7)
-        turn_pair(1, 6)
+            rate(c)
+        for c in (3, 4):
+            grouped[c] = grouped34[:, S * (c - 3) : S * (c - 2)]
+            turn_wd(c, 0, PASSES, (0, 6)[c - 3], nc.scalar.copy)
+        add_shortcut(4)
+        add_shortcut(5)
+        turn_pair(0, 5)
+        turn_pair(1, 7)
+        quantise_two(3, grouped34, keep.tile([P, 2 * PASSES * P], U32, name="codes34", align_bytes=64))
+        add_shortcut(6)
+        add_decoded(3)
         add_decoded(4)
-        for c in range(SUM_BANKS, TILES):
-            add_shortcut(c)
-        rate(2)
+        add_shortcut(7)
 
         pick_wd(7, 0, 1, "picked7_0")
         pick_wd(7, 1, 2, "picked7_1")
-        quantise_pair()
+        for half, c in enumerate(PAIR):
+            grouped[c] = pair_grouped[:, half, :]
+            quantise_wd(c, 0, PASSES, keep.tile([P, PASSES * P], U32, name=f"wd_codes{c}", align_bytes=64))
         grouped[7] = keep.tile([P, S], BF16, name="grouped7", align_bytes=64)
-        turn_wd(7, 0, 1, 7, nc.scalar.copy)
         rate(3)
+        turn_wd(7, 0, 1, 5, nc.scalar.copy)
+        last_turned = transpose_wd(7, 1, 2, 2)
         rate(4)
         for c in PAIR:
             add_decoded(c)
             rate(c)
         quantise_wd(7, 0, 1, keep.tile([P, P], U32, name="wd_codes7_0", align_bytes=64))
-        turn_wd(7, 1, 2, 6, nc.vector.tensor_copy)
+        copy_out_wd(7, 1, 2, last_turned, nc.vector.tensor_copy)
         quantise_wd(7, 1, 2, keep.tile([P, P], U32, name="wd_codes7_1", align_bytes=64))
         add_decoded(7)
         rate(7)

@@ -63,8 +63,8 @@ def tile_list_listed_rating_autoencoder_kernel(tc, tab_words, tab_scales, offs, 
         wd[3] = on_wd4.tile([P, T], F32, name="wd3", align_bytes=64, offset=0)
         w4 = [keep.tile([P, PASSES, N // 4], I32, name=f"w4_{half}", align_bytes=64) for half in range(2)]
         widths = [CHUNK_EDGES[i + 1] - CHUNK_EDGES[i] for i in range(CHUNKS)]
-        pair_raw = {i: keep.tile([P, 2, widths[i]], F32, name=f"pair_raw{i}", align_bytes=64) for i in range(CHUNKS) if i != 3}
-        pair_raw[3] = on_last_chunk.tile([P, 2, widths[3]], F32, name="pair_raw3", align_bytes=64, offset=3 * S)
+        pair_raw = {i: keep.tile([P, 2, widths[i]], F32, name=f"pair_raw{i}", align_bytes=64) for i in range(CHUNKS - 1)}
+        pair_raw[4] = on_last_chunk.tile([P, 2, widths[4]], F32, name="pair_raw4", align_bytes=64, offset=3 * S)
         pair_rows = wdT[PAIR[0] * P : (PAIR[1] + 1) * P, :].rearrange("(p e) col -> p e col", e=2)
 
         def load_table(a):
@@ -323,7 +323,7 @@ def tile_list_listed_rating_autoencoder_kernel(tc, tab_words, tab_scales, offs, 
         add_decoded(0)
         rate(0)
         round_pair(nc.scalar.copy, 3)
-        round_pair(nc.vector.tensor_copy, 4)
+        round_pair(nc.scalar.copy, 4)
         pick_pair(0)
         pick_pair(1)
 

@@ -21,51 +21,54 @@ P = 128
 PASS = 4 * P
 PASSES = 2
 TILES = N // P
-PAIR = (5, 6)
-SINGLES = (0, 1, 2, 3, 4, 7)
-EARLY = 5
-SUM_BANKS = 6
-SUM_BANK = (0, 1, 2, 3, 4, 1, 0, 6)
-CHUNK_EDGES = (0, 512, 1024, 1536, 1792, 2048)
+SINGLES = 6
+PAIR = (6, 7)
+SUM_BANK = (0, 1, 2, 3, 4, 5, 0, 1)
+CHUNK_EDGES = (0, 768, 1152, 1536, 1792, 2048)
 CHUNKS = len(CHUNK_EDGES) - 1
-LAST_ON_SCALAR = 384
 X_ON_SCALAR = (72, 44)
+ALIGN = 256
 
 
 def tile_list_listed_rating_autoencoder_kernel(tc, tab_words, tab_scales, offs, x, w4_words, w4_scales, wdT, g, bo, out):
     nc = tc.nc
     with ExitStack() as ctx:
         keep = ctx.enter_context(tc.tile_pool(name="keep", bufs=1))
-        ring = ctx.enter_context(tc.tile_pool(name="ring", bufs=4))
-        on_last_chunk = ctx.enter_context(tc.tile_pool(name="late", bufs=1))
-        on_wd4 = ctx.enter_context(tc.tile_pool(name="mid", bufs=1))
+        on_rows = ctx.enter_context(tc.tile_pool(name="on_rows", bufs=1))
+        on_words = ctx.enter_context(tc.tile_pool(name="on_words", bufs=1))
         banks = ctx.enter_context(tc.psum_pool(name="banks", bufs=1))
 
-        offsets = keep.tile([P, S // 16], U16, name="offsets")
+        def sb(shape, dtype, name):
+            return keep.tile(shape, dtype, name=name, align_bytes=ALIGN)
+
+        def bank(n, shape, dtype):
+            return banks.tile(shape, dtype, name=f"bank{n}")
+
+        offsets = sb([P, S // 16], U16, "offsets")
         nc.sync.dma_start(offsets[:], offs)
 
-        tab_plane = keep.tile([P, T // 4], I32, name="tab_plane", align_bytes=64)
-        w4_plane = keep.tile([P, PASSES, N // 4], I32, name="w4_plane", align_bytes=64)
-        rows = keep.tile([P, 5 * P], F32, name="rows", align_bytes=64)
-        g_rows = keep.tile([PASSES, PASS], F32, name="g_rows")
+        tab_plane = sb([P, T // 4], I32, "tab_plane")
+        w4_plane = sb([P, PASSES, N // 4], I32, "w4_plane")
+        rows = on_rows.tile([P, 5 * P], F32, name="rows", align_bytes=ALIGN, offset=0)
+        g_rows = sb([PASSES, PASS], F32, "g_rows")
         for a in range(PASSES):
             nc.sync.dma_start(tab_plane[16 * a : 16 * (a + 1), :], tab_scales[a].bitcast(I32).rearrange("(quad r) w -> r quad w", r=4))
         nc.gpsimd.memset(tab_plane[32:64, :], 0)
         nc.vector.memset(tab_plane[64:P, :], 0)
         nc.vector.memset(rows[:], 0.0)
         nc.vector.memset(w4_plane[:], 0)
-        ident = keep.tile([P, P], F32, name="ident")
+        ident = sb([P, P], F32, "ident")
         make_identity(nc, ident[:])
+        ident_bf = sb([P, P], BF16, "ident_bf")
+        nc.gpsimd.tensor_copy(ident_bf[:], ident[:])
 
-        x_raw = [keep.tile([P, 4, M], F32, name=f"x_raw{a}", align_bytes=64) for a in range(PASSES)]
-        tab = [keep.tile([P, T], I32, name=f"tab{a}", align_bytes=64) for a in range(PASSES)]
-        wd = {c: keep.tile([P, T], F32, name=f"wd{c}", align_bytes=64) for c in SINGLES if c != 3}
-        wd[3] = on_wd4.tile([P, T], F32, name="wd3", align_bytes=64, offset=0)
-        w4 = [keep.tile([P, PASSES, N // 4], I32, name=f"w4_{half}", align_bytes=64) for half in range(2)]
+        x_raw = [sb([P, 4, M], F32, f"x_raw{a}") for a in range(PASSES)]
+        tab = [sb([P, T], I32, f"tab{a}") for a in range(PASSES)]
+        wd = [sb([P, T], F32, f"wd{c}") for c in range(SINGLES)]
+        w4 = sb([P, PASSES, N // 2], I32, "w4")
         widths = [CHUNK_EDGES[i + 1] - CHUNK_EDGES[i] for i in range(CHUNKS)]
-        pair_raw = {i: keep.tile([P, 2, widths[i]], F32, name=f"pair_raw{i}", align_bytes=64) for i in range(CHUNKS - 1)}
-        pair_raw[4] = on_last_chunk.tile([P, 2, widths[4]], F32, name="pair_raw4", align_bytes=64, offset=3 * S)
-        pair_rows = wdT[PAIR[0] * P : (PAIR[1] + 1) * P, :].rearrange("(p e) col -> p e col", e=2)
+        pair_raw = [sb([P, 2, widths[i]], F32, f"pair_raw{i}") for i in range(CHUNKS)]
+        pair_rows = wdT[PAIR[0] * P : (PAIR[1] + 1) * P, :].rearrange("(e p) col -> p e col", e=2)
 
         def load_table(a):
             nc.sync.dma_start(tab[a][:], tab_words[a].rearrange("p col t -> p (col t)").bitcast(I32))
@@ -76,14 +79,6 @@ def tile_list_listed_rating_autoencoder_kernel(tc, tab_words, tab_scales, offs, 
         def load_wd(c):
             nc.sync.dma_start(wd[c][:], wdT[P * c : P * (c + 1), :])
 
-        def load_shortcut(half):
-            nc.sync.dma_start(w4[half][:], w4_words.bitcast(I32).rearrange("a p w -> p a w")[:, :, N // 4 * half : N // 4 * (half + 1)])
-
-        def load_shortcut_scales():
-            rows_of_quads = w4_scales.bitcast(I32).rearrange("a (quad r) w -> r quad a w", r=4)
-            for r in range(4):
-                nc.sync.dma_start(w4_plane[r:P:32, :, :], rows_of_quads[r])
-
         def load_pair(i):
             nc.sync.dma_start(pair_raw[i][:], pair_rows[:, :, CHUNK_EDGES[i] : CHUNK_EDGES[i + 1]])
 
@@ -93,9 +88,9 @@ def tile_list_listed_rating_autoencoder_kernel(tc, tab_words, tab_scales, offs, 
         load_x(1)
         load_table(1)
 
-        v_plane = keep.tile([P, S // 4], I32, name="v_plane", align_bytes=64)
-        listed_plane = keep.tile([P, S], U8, name="listed_plane", align_bytes=64)
-        ordered_plane = keep.tile([P, S // 4], I32, name="ordered_plane", align_bytes=64)
+        v_plane = sb([P, S // 4], I32, "v_plane")
+        listed_plane = sb([P, S], U8, "listed_plane")
+        ordered_plane = sb([P, S // 4], I32, "ordered_plane")
         nc.gpsimd.memset(v_plane[:], 0)
         nc.vector.tensor_copy(listed_plane[:], tab_plane[:].bitcast(U8).indirect(offsets[:]))
         nc.vector.tensor_copy(
@@ -105,29 +100,29 @@ def tile_list_listed_rating_autoencoder_kernel(tc, tab_words, tab_scales, offs, 
         for quad in (0, 2, 1, 3):
             nc.sync.dma_start(v_plane[32 * quad : 32 * quad + 8, :], ordered_plane[quad:32:4, :])
 
-        load_wd(0)
-        load_wd(1)
-        load_wd(2)
-        load_wd(3)
+        for c in range(4):
+            load_wd(c)
         nc.sync.dma_start(rows[0:TILES, PASS : PASS + P], bo.rearrange("(c p) -> c p", p=P))
-        load_shortcut_scales()
-        load_shortcut(0)
+        rows_of_quads = w4_scales.bitcast(I32).rearrange("a (quad r) w -> r quad a w", r=4)
+        for r in range(4):
+            nc.sync.dma_start(w4_plane[r:P:32, :, :], rows_of_quads[r])
+        nc.sync.dma_start(w4[:], w4_words.bitcast(I32).rearrange("a p w -> p a w"))
         load_wd(4)
-        for i in range(CHUNKS):
+        load_pair(0)
+        load_wd(5)
+        for i in range(1, CHUNKS):
             load_pair(i)
-        load_shortcut(1)
-        load_wd(7)
 
         gains = keep.tile([P, 4, PASSES], F32, name="gains")
-        gains_ps = banks.tile([P, 4, P], F32, name="bank5")
+        gains_ps = bank(5, [P, 4, P], F32)
         nc.scalar.copy(rows[0:PASSES, 0:PASS].rearrange("b (t d l) -> b t d l", t=4, l=4), g_rows[:].rearrange("b (d t l) -> b t d l", t=4, l=4))
         for t in range(4):
             nc.tensor.transpose(gains_ps[:, t, :], rows[:, P * t : P * (t + 1)], ident[:])
         nc.scalar.copy(gains[:], gains_ps[:, :, 0:PASSES])
 
-        x_codes = [keep.tile([P, M], U32, name=f"x_codes{a}", align_bytes=64) for a in range(PASSES)]
-        x_plane = [keep.tile([P, M], U8, name=f"x_plane{a}", align_bytes=64) for a in range(PASSES)]
-        x_grouped = [keep.tile([P, M, 4], BF16, name=f"x_grouped{a}", align_bytes=64) for a in range(PASSES)]
+        x_codes = [sb([P, M], U32, f"x_codes{a}") for a in range(PASSES)]
+        x_plane = [sb([P, M], U8, f"x_plane{a}") for a in range(PASSES)]
+        x_grouped = [sb([P, M, 4], BF16, f"x_grouped{a}") for a in range(PASSES)]
         v_codes = {}
 
         def round_x(engine_copy, a, lo, hi):
@@ -136,7 +131,7 @@ def tile_list_listed_rating_autoencoder_kernel(tc, tab_words, tab_scales, offs, 
             engine_copy(dst[:, lo:hi], src[:, lo:hi])
 
         def pick_table(a, b0, b1, name):
-            codes = keep.tile([P, 4, P * (b1 - b0)], U32, name=name, align_bytes=64)
+            codes = sb([P, 4, P * (b1 - b0)], U32, name)
             nc.vector.tensor_copy(
                 codes[:].rearrange("p t (d l) -> p d t l", l=4),
                 tab[a][:].bitcast(U32).indirect(offsets[:, 32 * b0 : 32 * b1]),
@@ -146,75 +141,41 @@ def tile_list_listed_rating_autoencoder_kernel(tc, tab_words, tab_scales, offs, 
 
         wd_operand = {}
         picked = {}
-        grouped = {}
 
-        def pick_wd(c, b0, b1, name):
-            picked[c, b0] = keep.tile([P, PASS * (b1 - b0)], BF16, name=name, align_bytes=64)
+        def pick_wd(c, name):
+            picked[c] = sb([P, S], BF16, name)
             nc.vector.tensor_copy(
-                picked[c, b0][:].rearrange("p (u d l e) -> p d u e l", u=2, l=4, e=2),
-                wd[c][:].indirect(offsets[:, 32 * b0 : 32 * b1]),
+                picked[c][:].rearrange("p (u d l e) -> p d u e l", u=2, l=4, e=2),
+                wd[c][:].indirect(offsets[:]),
             )
 
-        def transpose_wd(c, b0, b1, bank):
-            words = picked[c, b0][:].bitcast(F32)
-            turned = banks.tile([P, 4, P], F32, name=f"bank{bank}")
-            for b in range(b0, b1):
+        def turn_wd(c, n, grouped):
+            words = picked[c][:].bitcast(F32)
+            turned = bank(n, [P, 4, P], F32)
+            for b in range(PASSES):
                 for u in range(2):
-                    start = P * ((b1 - b0) * u + b - b0)
+                    start = P * (PASSES * u + b)
                     nc.tensor.transpose(turned[:, 2 * u + b, :], words[:, start : start + P], ident[:])
-            return turned
-
-        def copy_out_wd(c, b0, b1, turned, engine_copy):
-            engine_copy(
-                grouped[c][:].bitcast(F32).rearrange("p (b n u) -> p b n u", b=2, u=2)[:, b0:b1],
-                turned[:].rearrange("p (u b) n -> p b n u", u=2)[:, b0:b1],
-            )
-
-        def turn_wd(c, b0, b1, bank, engine_copy):
-            copy_out_wd(c, b0, b1, transpose_wd(c, b0, b1, bank), engine_copy)
-
-        def quantise_wd(c, b0, b1, codes):
-            plane = keep.tile([P, P * (b1 - b0)], U8, name=f"wd_plane{c}_{b0}", align_bytes=64)
-            nc.vector.quantize_mx(out=codes[:].bitcast(FP8X4), scales=plane[:], in_=grouped[c][:, PASS * b0 : PASS * b1])
-            for b in range(b0, b1):
-                columns = slice(P * (b - b0), P * (b - b0 + 1))
-                wd_operand[c, b] = (codes[:, columns].bitcast(FP8X4), plane[:, columns])
-
-        pair_words = keep.tile([P, 2 * T], BF16, name="pair_words", align_bytes=64)
-        pair_picked = [keep.tile([P, PASS], U32, name=f"pair_picked{b}", align_bytes=64) for b in range(PASSES)]
-        pair_grouped = keep.tile([P, 2, S], BF16, name="pair_grouped", align_bytes=64)
-
-        def round_pair(engine_copy, i):
-            engine_copy(
-                pair_words[:, 2 * CHUNK_EDGES[i] : 2 * CHUNK_EDGES[i + 1]].rearrange("p (col e) -> p col e", e=2),
-                pair_raw[i][:].rearrange("p e col -> p col e"),
-            )
-
-        def pick_pair(b):
-            nc.vector.tensor_copy(
-                pair_picked[b][:].rearrange("p (t d l) -> p d t l", t=4, l=4),
-                pair_words[:].bitcast(U32).indirect(offsets[:, 32 * b : 32 * (b + 1)]),
-            )
-
-        def turn_pair(b, bank):
-            words = pair_picked[b][:].bitcast(F32)
-            turned = banks.tile([P, 4, P], F32, name=f"bank{bank}")
-            for t in range(4):
-                nc.tensor.transpose(turned[:, t, :], words[:, P * t : P * (t + 1)], ident[:])
             nc.scalar.copy(
-                pair_grouped[:, :, PASS * b : PASS * (b + 1)].rearrange("p half (n t) -> p half n t", t=4),
-                turned[:].bitcast(BF16).rearrange("p t (half n) -> p half n t", half=2),
+                grouped.bitcast(F32).rearrange("p (b n u) -> p b n u", b=2, u=2),
+                turned[:].rearrange("p (u b) n -> p b n u", u=2),
             )
 
-        h_plane = [keep.tile([P, M], U8, name=f"h_plane{b}", align_bytes=64) for b in range(PASSES)]
-        h_pairs = [keep.tile([P, 4 * M], BF16, name=f"h_rows{b}", align_bytes=64) for b in range(PASSES)]
-        h_grouped = {0: keep.tile([P, 4 * M], BF16, name="h_grouped0", align_bytes=64)}
-        h_codes = {}
-        sig = [keep.tile([P, 4, M], F32, name=f"sig{b}") for b in range(PASSES)]
+        def quantise_wd(values, codes, plane, keys):
+            nc.vector.quantize_mx(out=codes.bitcast(FP8X4), scales=plane, in_=values)
+            for n, key in enumerate(keys):
+                columns = slice(P * n, P * (n + 1))
+                wd_operand[key] = (codes[:, columns].bitcast(FP8X4), plane[:, columns])
+
+        h_pairs = [sb([P, 4 * M], BF16, f"h_pairs{b}") for b in range(PASSES)]
+        h_grouped = [sb([P, 4 * M], BF16, f"h_grouped{b}") for b in range(PASSES)]
+        h_codes = [sb([P, M], U32, f"h_codes{b}") for b in range(PASSES)]
+        h_plane = {}
+        sig = [sb([P, 4, M], F32, f"sig{b}") for b in range(PASSES)]
 
         def encode(b, t):
             columns = slice(PASSES * P * t + P * b, PASSES * P * t + P * (b + 1))
-            acc = banks.tile([P, M], F32, name=f"bank{(4 * b + t + SUM_BANKS) % 8}")
+            acc = bank((4 * b + t + 6) % 8, [P, M], F32)
             for a in range(PASSES):
                 nc.tensor.matmul_mx(
                     out=acc[:], lhsT=v_codes[a, b][:, t, :].bitcast(FP8X4), lhsT_scale=v_plane[:].bitcast(U8)[4 * a : P, columns],
@@ -232,42 +193,45 @@ def tile_list_listed_rating_autoencoder_kernel(tc, tab_words, tab_scales, offs, 
                 h_pairs[b][:].bitcast(F32).rearrange("p (u m) -> p m u", u=2),
             )
 
-        def quantise_h(b):
-            nc.vector.quantize_mx(out=h_codes[b][:].bitcast(FP8X4), scales=h_plane[b][:], in_=h_grouped[b][:])
+        def on_rows_plane(width, offset, name):
+            return on_rows.tile([P, width], U8, name=name, align_bytes=ALIGN, offset=offset)
+
+        def quantise_h(b, plane):
+            h_plane[b] = plane
+            nc.vector.quantize_mx(out=h_codes[b][:].bitcast(FP8X4), scales=plane[:], in_=h_grouped[b][:])
 
         sums = {}
 
         def add_shortcut(c):
-            sums[c] = banks.tile([P, M], F32, name=f"bank{SUM_BANK[c]}")
+            sums[c] = bank(SUM_BANK[c], [P, M], F32)
             for a in range(PASSES):
                 nc.tensor.matmul_mx(
                     out=sums[c][:],
-                    lhsT=w4[c // 4][:, a, :].bitcast(U8)[:, 2 * P * (c % 4) : 2 * P * (c % 4 + 1)].bitcast(FP4X4),
+                    lhsT=w4[:, a, :].bitcast(U8)[:, 2 * P * c : 2 * P * (c + 1)].bitcast(FP4X4),
                     lhsT_scale=w4_plane[:, a, :].bitcast(U8)[:, P * c : P * (c + 1)],
                     rhs=x_codes[a][:].bitcast(FP8X4), rhs_scale=x_plane[a][:],
                     start=(a == 0), stop=False,
                 )
 
-        def add_decoded(c):
+        def add_decoded(c, b):
+            nc.tensor.matmul_mx(
+                out=sums[c][:], lhsT=wd_operand[c, b][0], lhsT_scale=wd_operand[c, b][1],
+                rhs=h_codes[b][:].bitcast(FP8X4), rhs_scale=h_plane[b][:],
+                start=False, stop=(b == PASSES - 1),
+            )
+
+        def close(c):
             for b in range(PASSES):
-                nc.tensor.matmul_mx(
-                    out=sums[c][:], lhsT=wd_operand[c, b][0], lhsT_scale=wd_operand[c, b][1],
-                    rhs=h_codes[b][:].bitcast(FP8X4), rhs_scale=h_plane[b][:],
-                    start=False, stop=(b == PASSES - 1),
-                )
+                add_decoded(c, b)
 
         def rate(c):
             parts = 2 if c == TILES - 1 else 1
             width = M // parts
             for part in range(parts):
                 users = slice(width * part, width * (part + 1))
-                rated = rated_early[c] if c < EARLY else ring.tile([P, width], F32, name="rated")[:]
-                nc.scalar.activation(rated, sums[c][:, users], ACT.Tanh, bias=bias[:, c : c + 1])
-                nc.sync.dma_start(out[P * c : P * (c + 1), users], rated)
-
-        def turn_whole(c, name):
-            grouped[c] = keep.tile([P, S], BF16, name=name, align_bytes=64)
-            turn_wd(c, 0, PASSES, SUM_BANKS + c % 2, nc.scalar.copy)
+                result = rated[c // 4][:, c % 4, users]
+                nc.scalar.activation(result, sums[c][:, users], ACT.Tanh, bias=bias[:, c : c + 1])
+                nc.sync.dma_start(out[P * c : P * (c + 1), users], result)
 
         pick_table(0, 0, PASSES, "v_codes0")
         for a in range(PASSES):
@@ -277,91 +241,108 @@ def tile_list_listed_rating_autoencoder_kernel(tc, tab_words, tab_scales, offs, 
         pick_table(1, 0, 1, "v_codes1a")
         pick_table(1, 1, 2, "v_codes1b")
 
-        for c in range(EARLY - 1):
-            pick_wd(c, 0, PASSES, f"picked{c}_0")
+        for c in range(4):
+            pick_wd(c, f"picked{c}")
         for b in range(PASSES):
             for t in range(4):
                 encode(b, t)
                 apply_gain(b, t)
 
+        grouped01 = sb([P, 2 * S], BF16, "grouped01")
+        grouped2 = on_words.tile([P, S], BF16, name="grouped2", align_bytes=ALIGN, offset=0)
+        grouped34 = sb([P, 2 * S], BF16, "grouped34")
+        turn_wd(0, 6, grouped01[:, 0:S])
+        group_h(0)
+        turn_wd(1, 7, grouped01[:, S : 2 * S])
+        turn_wd(2, 6, grouped2[:])
+
         bias = keep.tile([P, TILES], F32, name="bias")
-        bias_ps = banks.tile([P, P], F32, name="bank5")
+        bias_ps = bank(5, [P, P], F32)
         nc.tensor.transpose(bias_ps[:], rows[:, PASS : PASS + P], ident[:])
         nc.scalar.copy(bias[:], bias_ps[:, 0:TILES])
-        def quantise_two(c, values, codes):
-            plane = keep.tile([P, 2 * PASSES * P], U8, name=f"plane_two{c}", align_bytes=64)
-            nc.vector.quantize_mx(out=codes[:].bitcast(FP8X4), scales=plane[:], in_=values[:])
-            for n in range(2 * PASSES):
-                columns = slice(P * n, P * (n + 1))
-                wd_operand[c + n // PASSES, n % PASSES] = (codes[:, columns].bitcast(FP8X4), plane[:, columns])
-
-        grouped01 = keep.tile([P, 2 * S], BF16, name="grouped01", align_bytes=64)
-        for c in range(2):
-            grouped[c] = grouped01[:, S * c : S * (c + 1)]
-            turn_wd(c, 0, PASSES, SUM_BANKS + c, nc.scalar.copy)
-            if c == 0:
-                group_h(0)
-        turn_whole(2, "grouped2")
-        h_grouped[1] = keep.tile([P, 4 * M], BF16, name="h_grouped1", align_bytes=64)
         group_h(1)
         for c in range(4):
             add_shortcut(c)
 
-        h_codes[0] = keep.tile([P, M], U32, name="rows", align_bytes=64)
-        quantise_h(0)
-        quantise_two(0, grouped01, on_wd4.tile([P, 2 * PASSES * P], U32, name="codes01", align_bytes=64, offset=4 * PASSES * M))
-        h_codes[1] = on_wd4.tile([P, M], U32, name="h_codes1", align_bytes=64, offset=4 * M)
-        quantise_h(1)
-        quantise_wd(2, 0, PASSES, on_wd4.tile([P, PASSES * P], U32, name="codes2", align_bytes=64, offset=4 * PASSES * (M + 2 * P)))
-        pick_wd(4, 0, PASSES, "h_grouped1")
+        quantise_h(0, on_rows_plane(M, 0, "h_plane0"))
+        quantise_wd(grouped01[:], sb([P, 4 * P], U32, "codes01")[:], on_rows_plane(4 * P, M, "plane01")[:], [(0, 0), (0, 1), (1, 0), (1, 1)])
+        quantise_h(1, on_rows_plane(M, 2 * M, "h_plane1"))
+        quantise_wd(grouped2[:], sb([P, 2 * P], U32, "codes2")[:], on_rows_plane(2 * P, 3 * M, "plane2")[:], [(2, 0), (2, 1)])
+        pick_wd(4, "h_grouped1")
+        pick_wd(5, "picked5")
 
-        round_pair(nc.scalar.copy, 0)
-        round_pair(nc.scalar.copy, 1)
-        nc.gpsimd.tensor_copy(pair_words[:, 2 * CHUNK_EDGES[2] : 2 * CHUNK_EDGES[3]].rearrange("p (col e) -> p e col", e=2), pair_raw[2][:])
-        rated0 = keep.tile([P, M], F32, name="pair_raw1", align_bytes=64)
-        rated_early = {0: rated0[:]}
-        add_decoded(0)
-        rate(0)
+        rated = [sb([P, 4, M], F32, f"x_raw{half}") for half in range(2)]
+        for c in range(2):
+            close(c)
+            rate(c)
+        close(2)
+        turn_wd(3, 0, grouped34[:, 0:S])
+        rate(2)
+        turn_wd(4, 2, grouped34[:, S : 2 * S])
+        for c in range(4, TILES):
+            add_shortcut(c)
+
+        pair_words = on_words.tile([P, 2 * T], BF16, name="pair_words", align_bytes=ALIGN, offset=0)
+
+        def round_pair(engine_copy, i):
+            engine_copy(
+                pair_words[:, 2 * CHUNK_EDGES[i] : 2 * CHUNK_EDGES[i + 1]].rearrange("p (col e) -> p col e", e=2),
+                pair_raw[i][:].rearrange("p e col -> p col e"),
+            )
+
+        round_pair(nc.gpsimd.tensor_copy, 0)
+        round_pair(nc.gpsimd.tensor_copy, 1)
+        round_pair(nc.gpsimd.tensor_copy, 2)
         round_pair(nc.scalar.copy, 3)
         round_pair(nc.scalar.copy, 4)
-        pick_pair(0)
-        pick_pair(1)
 
-        rated_later = on_last_chunk.tile([P, 4, M], F32, name="rated_later", align_bytes=64, offset=4 * S)
-        for c in range(1, EARLY):
-            rated_early[c] = rated_later[:, c - 1, :]
-        grouped34 = on_last_chunk.tile([P, 2 * S], BF16, name="grouped34", align_bytes=64, offset=0)
-        for c in (1, 2):
-            add_decoded(c)
-            rate(c)
+        quantise_wd(grouped34[:], sb([P, 4 * P], U32, "pair_raw2")[:], sb([P, 4 * P], U8, "plane34")[:], [(3, 0), (3, 1), (4, 0), (4, 1)])
+
+        pair_picked = [sb([P, PASS], U32, f"pair_picked{b}") for b in range(PASSES)]
+        for b in range(PASSES):
+            nc.vector.tensor_copy(
+                pair_picked[b][:].rearrange("p (t d l) -> p d t l", t=4, l=4),
+                pair_words[:].bitcast(U32).indirect(offsets[:, 32 * b : 32 * (b + 1)]),
+            )
+
+        grouped5 = sb([P, S], BF16, "pair_raw4")
+        turn_wd(5, 7, grouped5[:])
         for c in (3, 4):
-            grouped[c] = grouped34[:, S * (c - 3) : S * (c - 2)]
-            turn_wd(c, 0, PASSES, (0, 6)[c - 3], nc.scalar.copy)
-        add_shortcut(4)
-        add_shortcut(5)
-        turn_pair(0, 5)
-        turn_pair(1, 7)
-        quantise_two(3, grouped34, keep.tile([P, 2 * PASSES * P], U32, name="codes34", align_bytes=64))
-        add_shortcut(6)
-        add_decoded(3)
-        add_decoded(4)
-        add_shortcut(7)
-
-        pick_wd(7, 0, 1, "picked7_0")
-        pick_wd(7, 1, 2, "picked7_1")
-        for half, c in enumerate(PAIR):
-            grouped[c] = pair_grouped[:, half, :]
-            quantise_wd(c, 0, PASSES, keep.tile([P, PASSES * P], U32, name=f"wd_codes{c}", align_bytes=64))
-        grouped[7] = keep.tile([P, S], BF16, name="grouped7", align_bytes=64)
-        rate(3)
-        turn_wd(7, 0, 1, 5, nc.scalar.copy)
-        last_turned = transpose_wd(7, 1, 2, 2)
-        rate(4)
-        for c in PAIR:
-            add_decoded(c)
+            close(c)
             rate(c)
-        quantise_wd(7, 0, 1, keep.tile([P, P], U32, name="wd_codes7_0", align_bytes=64))
-        copy_out_wd(7, 1, 2, last_turned, nc.vector.tensor_copy)
-        quantise_wd(7, 1, 2, keep.tile([P, P], U32, name="wd_codes7_1", align_bytes=64))
-        add_decoded(7)
+
+        pair_grouped = {(c, b): sb([P, P, 4], BF16, f"pair_grouped{c}_{b}") for c in PAIR for b in range(PASSES)}
+
+        def quantise_pair(c, b):
+            quantise_wd(
+                pair_grouped[c, b][:].rearrange("p n t -> p (n t)"), sb([P, P], U32, f"pair_codes{c}_{b}")[:],
+                sb([P, P], U8, f"pair_plane{c}_{b}")[:], [(c, b)],
+            )
+
+        first = bank(6, [P, 4, P], F32)
+        for t in range(4):
+            nc.tensor.transpose(first[:, t, :], pair_picked[0][:].bitcast(F32)[:, P * t : P * (t + 1)], ident[:])
+        for e, c in enumerate(PAIR):
+            nc.scalar.copy(pair_grouped[c, 0][:], first[:].bitcast(BF16).rearrange("p t (n e) -> p e n t", e=2)[:, e])
+        halves = pair_picked[1][:].bitcast(BF16).rearrange("p (t j e) -> p t j e", t=4, e=2)
+        second = {}
+        for e, c in enumerate(PAIR):
+            second[c] = bank((2, 7)[e], [P, 4, P], BF16)
+            for t in range(4):
+                nc.tensor.transpose(second[c][:, t, :], halves[:, t, :, e], ident_bf[:])
+
+        quantise_pair(6, 0)
+        quantise_wd(grouped5[:], sb([P, 2 * P], U32, "pair_picked0")[:], sb([P, 2 * P], U8, "plane5")[:], [(5, 0), (5, 1)])
+        nc.vector.tensor_copy(pair_grouped[6, 1][:], second[6][:].rearrange("p t n -> p n t"))
+        nc.scalar.copy(pair_grouped[7, 1][:], second[7][:].rearrange("p t n -> p n t"))
+        quantise_pair(7, 0)
+        quantise_pair(6, 1)
+        quantise_pair(7, 1)
+        add_decoded(6, 0)
+        close(5)
+        rate(5)
+        add_decoded(7, 0)
+        add_decoded(6, 1)
+        rate(6)
+        add_decoded(7, 1)
         rate(7)

@@ -50,7 +50,7 @@ def tile_list_listed_rating_autoencoder_kernel(tc, tab_words, tab_scales, offs, 
         tab_plane = sb([P, T // 4], I32, "tab_plane")
         w4_plane = sb([P, PASSES, N // 4], I32, "w4_plane")
         rows = on_rows.tile([P, 5 * P], F32, name="rows", align_bytes=ALIGN, offset=0)
-        g_rows = sb([PASSES, PASS], F32, "g_rows")
+        g_rows = sb([P, PASS], F32, "g_rows")
         for a in range(PASSES):
             nc.sync.dma_start(tab_plane[16 * a : 16 * (a + 1), :], tab_scales[a].bitcast(I32).rearrange("(quad r) w -> r quad w", r=4))
         nc.gpsimd.memset(tab_plane[32:64, :], 0)
@@ -65,7 +65,7 @@ def tile_list_listed_rating_autoencoder_kernel(tc, tab_words, tab_scales, offs, 
         x_raw = [sb([P, 4, M], F32, f"x_raw{a}") for a in range(PASSES)]
         tab = [sb([P, T], I32, f"tab{a}") for a in range(PASSES)]
         wd = [sb([P, T], F32, f"wd{c}") for c in range(SINGLES)]
-        w4 = sb([P, PASSES, N // 2], I32, "w4")
+        w4 = [sb([P, PASSES, N // 4], I32, f"w4_{half}") for half in range(2)]
         widths = [CHUNK_EDGES[i + 1] - CHUNK_EDGES[i] for i in range(CHUNKS)]
         pair_raw = [sb([P, 2, widths[i]], F32, f"pair_raw{i}") for i in range(CHUNKS)]
         pair_rows = wdT[PAIR[0] * P : (PAIR[1] + 1) * P, :].rearrange("(e p) col -> p e col", e=2)
@@ -79,12 +79,15 @@ def tile_list_listed_rating_autoencoder_kernel(tc, tab_words, tab_scales, offs, 
         def load_wd(c):
             nc.sync.dma_start(wd[c][:], wdT[P * c : P * (c + 1), :])
 
+        def load_shortcut(half):
+            nc.sync.dma_start(w4[half][:], w4_words.bitcast(I32).rearrange("a p w -> p a w")[:, :, N // 4 * half : N // 4 * (half + 1)])
+
         def load_pair(i):
             nc.sync.dma_start(pair_raw[i][:], pair_rows[:, :, CHUNK_EDGES[i] : CHUNK_EDGES[i + 1]])
 
         load_table(0)
         load_x(0)
-        nc.sync.dma_start(g_rows[:], g.rearrange("(b j) -> b j", b=PASSES))
+        nc.sync.dma_start(g_rows[64 : 64 + PASSES, :], g.rearrange("(b j) -> b j", b=PASSES))
         load_x(1)
         load_table(1)
 
@@ -106,19 +109,20 @@ def tile_list_listed_rating_autoencoder_kernel(tc, tab_words, tab_scales, offs, 
         rows_of_quads = w4_scales.bitcast(I32).rearrange("a (quad r) w -> r quad a w", r=4)
         for r in range(4):
             nc.sync.dma_start(w4_plane[r:P:32, :, :], rows_of_quads[r])
-        nc.sync.dma_start(w4[:], w4_words.bitcast(I32).rearrange("a p w -> p a w"))
+        load_shortcut(0)
         load_wd(4)
         load_pair(0)
         load_wd(5)
+        load_shortcut(1)
         for i in range(1, CHUNKS):
             load_pair(i)
 
         gains = keep.tile([P, 4, PASSES], F32, name="gains")
         gains_ps = bank(5, [P, 4, P], F32)
-        nc.scalar.copy(rows[0:PASSES, 0:PASS].rearrange("b (t d l) -> b t d l", t=4, l=4), g_rows[:].rearrange("b (d t l) -> b t d l", t=4, l=4))
+        nc.scalar.copy(rows[64 : 64 + PASSES, 0:PASS].rearrange("b (t d l) -> b t d l", t=4, l=4), g_rows[64 : 64 + PASSES, :].rearrange("b (d t l) -> b t d l", t=4, l=4))
         for t in range(4):
             nc.tensor.transpose(gains_ps[:, t, :], rows[:, P * t : P * (t + 1)], ident[:])
-        nc.scalar.copy(gains[:], gains_ps[:, :, 0:PASSES])
+        nc.scalar.copy(gains[:], gains_ps[:, :, 64 : 64 + PASSES])
 
         x_codes = [sb([P, M], U32, f"x_codes{a}") for a in range(PASSES)]
         x_plane = [sb([P, M], U8, f"x_plane{a}") for a in range(PASSES)]
@@ -207,7 +211,7 @@ def tile_list_listed_rating_autoencoder_kernel(tc, tab_words, tab_scales, offs, 
             for a in range(PASSES):
                 nc.tensor.matmul_mx(
                     out=sums[c][:],
-                    lhsT=w4[:, a, :].bitcast(U8)[:, 2 * P * c : 2 * P * (c + 1)].bitcast(FP4X4),
+                    lhsT=w4[c // 4][:, a, :].bitcast(U8)[:, 2 * P * (c % 4) : 2 * P * (c % 4 + 1)].bitcast(FP4X4),
                     lhsT_scale=w4_plane[:, a, :].bitcast(U8)[:, P * c : P * (c + 1)],
                     rhs=x_codes[a][:].bitcast(FP8X4), rhs_scale=x_plane[a][:],
                     start=(a == 0), stop=False,
@@ -231,7 +235,8 @@ def tile_list_listed_rating_autoencoder_kernel(tc, tab_words, tab_scales, offs, 
                 users = slice(width * part, width * (part + 1))
                 result = rated[c // 4][:, c % 4, users]
                 nc.scalar.activation(result, sums[c][:, users], ACT.Tanh, bias=bias[:, c : c + 1])
-                nc.sync.dma_start(out[P * c : P * (c + 1), users], result)
+                queue = nc.scalar if part == 1 else nc.sync
+                queue.dma_start(out[P * c : P * (c + 1), users], result)
 
         pick_table(0, 0, PASSES, "v_codes0")
         for a in range(PASSES):

@@ -45,14 +45,15 @@ def tile_list_listed_rating_autoencoder_kernel(tc, tab_words, tab_scales, offs, 
             return banks.tile(shape, dtype, name=f"bank{n}")
 
         offsets = sb([P, S // 16], U16, "offsets")
-        nc.sync.dma_start(offsets[:], offs)
 
         tab_plane = sb([P, T // 4], I32, "tab_plane")
         w4_plane = sb([P, PASSES, N // 4], I32, "w4_plane")
         rows = on_rows.tile([P, 5 * P], F32, name="rows", align_bytes=ALIGN, offset=0)
         g_rows = sb([P, PASS], F32, "g_rows")
-        for a in range(PASSES):
+        for a in reversed(range(PASSES)):
             nc.sync.dma_start(tab_plane[16 * a : 16 * (a + 1), :], tab_scales[a].bitcast(I32).rearrange("(quad r) w -> r quad w", r=4))
+        nc.sync.dma_start(g_rows[64 : 64 + PASSES, :], g.rearrange("(b j) -> b j", b=PASSES))
+        nc.sync.dma_start(offsets[:], offs)
         nc.gpsimd.memset(tab_plane[32:64, :], 0)
         nc.vector.memset(tab_plane[64:P, :], 0)
         nc.vector.memset(rows[:], 0.0)
@@ -87,7 +88,6 @@ def tile_list_listed_rating_autoencoder_kernel(tc, tab_words, tab_scales, offs, 
 
         load_table(0)
         load_x(0)
-        nc.sync.dma_start(g_rows[64 : 64 + PASSES, :], g.rearrange("(b j) -> b j", b=PASSES))
         load_x(1)
         load_table(1)
 

from contextlib import ExitStack

import concourse.mybir as mybir
from concourse.masks import make_identity

K, T, S, M, N = 1024, 2048, 1024, 512, 1024
FLOPS = 2 * M * (K * S + S * N + K * N)

F32 = mybir.dt.float32
BF16 = mybir.dt.bfloat16
I32 = mybir.dt.int32
U32 = mybir.dt.uint32
U16 = mybir.dt.uint16
U8 = mybir.dt.uint8
FP8X4 = mybir.dt.float8_e4m3fn_x4
FP4X4 = mybir.dt.float4_e2m1fn_x4
ACT = mybir.ActivationFunctionType
ALU = mybir.AluOpType

P = 128
PASS = 4 * P
PASSES = 2
TILES = N // P
SINGLES = 6
PAIR = (6, 7)
SUM_BANK = (0, 1, 2, 3, 4, 5, 0, 1)
CHUNK_EDGES = (0, 768, 1152, 1536, 1792, 2048)
CHUNKS = len(CHUNK_EDGES) - 1
X_ON_SCALAR = (72, 44)
ALIGN = 256


def tile_list_listed_rating_autoencoder_kernel(tc, tab_words, tab_scales, offs, x, w4_words, w4_scales, wdT, g, bo, out):
    nc = tc.nc
    with ExitStack() as ctx:
        keep = ctx.enter_context(tc.tile_pool(name="keep", bufs=1))
        on_rows = ctx.enter_context(tc.tile_pool(name="on_rows", bufs=1))
        on_words = ctx.enter_context(tc.tile_pool(name="on_words", bufs=1))
        banks = ctx.enter_context(tc.psum_pool(name="banks", bufs=1))

        def sb(shape, dtype, name):
            return keep.tile(shape, dtype, name=name, align_bytes=ALIGN)

        def bank(n, shape, dtype):
            return banks.tile(shape, dtype, name=f"bank{n}")

        offsets = sb([P, S // 16], U16, "offsets")

        tab_plane = sb([P, T // 4], I32, "tab_plane")
        w4_plane = sb([P, PASSES, N // 4], I32, "w4_plane")
        rows = on_rows.tile([P, 5 * P], F32, name="rows", align_bytes=ALIGN, offset=0)
        g_rows = sb([P, PASS], F32, "g_rows")
        for a in reversed(range(PASSES)):
            nc.sync.dma_start(tab_plane[16 * a : 16 * (a + 1), :], tab_scales[a].bitcast(I32).rearrange("(quad r) w -> r quad w", r=4))
        nc.sync.dma_start(g_rows[64 : 64 + PASSES, :], g.rearrange("(b j) -> b j", b=PASSES))
        nc.sync.dma_start(offsets[:], offs)
        nc.gpsimd.memset(tab_plane[32:64, :], 0)
        nc.vector.memset(tab_plane[64:P, :], 0)
        nc.vector.memset(rows[:], 0.0)
        nc.vector.memset(w4_plane[:], 0)
        ident = sb([P, P], F32, "ident")
        make_identity(nc, ident[:])
        ident_bf = sb([P, P], BF16, "ident_bf")
        nc.gpsimd.tensor_copy(ident_bf[:], ident[:])

        x_raw = [sb([P, 4, M], F32, f"x_raw{a}") for a in range(PASSES)]
        tab = [sb([P, T], I32, f"tab{a}") for a in range(PASSES)]
        wd = [sb([P, T], F32, f"wd{c}") for c in range(SINGLES)]
        w4 = [sb([P, PASSES, N // 4], I32, f"w4_{half}") for half in range(2)]
        widths = [CHUNK_EDGES[i + 1] - CHUNK_EDGES[i] for i in range(CHUNKS)]
        pair_raw = [sb([P, 2, widths[i]], F32, f"pair_raw{i}") for i in range(CHUNKS)]
        pair_rows = wdT[PAIR[0] * P : (PAIR[1] + 1) * P, :].rearrange("(e p) col -> p e col", e=2)

        def load_table(a):
            nc.sync.dma_start(tab[a][:], tab_words[a].rearrange("p col t -> p (col t)").bitcast(I32))

        def load_x(a):
            nc.sync.dma_start(x_raw[a][:], x[PASS * a : PASS * (a + 1), :].rearrange("(p t) m -> p t m", t=4))

        def load_wd(c):
            nc.sync.dma_start(wd[c][:], wdT[P * c : P * (c + 1), :])

        def load_shortcut(half):
            nc.sync.dma_start(w4[half][:], w4_words.bitcast(I32).rearrange("a p w -> p a w")[:, :, N // 4 * half : N // 4 * (half + 1)])

        def load_pair(i):
            nc.sync.dma_start(pair_raw[i][:], pair_rows[:, :, CHUNK_EDGES[i] : CHUNK_EDGES[i + 1]])

        load_table(0)
        load_x(0)
        load_x(1)
        load_table(1)

        v_plane = sb([P, S // 4], I32, "v_plane")
        listed_plane = sb([P, S], U8, "listed_plane")
        ordered_plane = sb([P, S // 4], I32, "ordered_plane")
        nc.gpsimd.memset(v_plane[:], 0)
        nc.vector.tensor_copy(listed_plane[:], tab_plane[:].bitcast(U8).indirect(offsets[:]))
        nc.vector.tensor_copy(
            ordered_plane[:].rearrange("p (t d) -> p t d", t=4),
            listed_plane[:].bitcast(I32).rearrange("p (d t) -> p t d", t=4),
        )
        for quad in (0, 2, 1, 3):
            nc.sync.dma_start(v_plane[32 * quad : 32 * quad + 8, :], ordered_plane[quad:32:4, :])

        for c in range(4):
            load_wd(c)
        nc.sync.dma_start(rows[0:TILES, PASS : PASS + P], bo.rearrange("(c p) -> c p", p=P))
        rows_of_quads = w4_scales.bitcast(I32).rearrange("a (quad r) w -> r quad a w", r=4)
        for r in range(4):
            nc.sync.dma_start(w4_plane[r:P:32, :, :], rows_of_quads[r])
        load_shortcut(0)
        load_wd(4)
        load_pair(0)
        load_wd(5)
        load_shortcut(1)
        for i in range(1, CHUNKS):
            load_pair(i)

        gains = keep.tile([P, 4, PASSES], F32, name="gains")
        gains_ps = bank(5, [P, 4, P], F32)
        nc.scalar.copy(rows[64 : 64 + PASSES, 0:PASS].rearrange("b (t d l) -> b t d l", t=4, l=4), g_rows[64 : 64 + PASSES, :].rearrange("b (d t l) -> b t d l", t=4, l=4))
        for t in range(4):
            nc.tensor.transpose(gains_ps[:, t, :], rows[:, P * t : P * (t + 1)], ident[:])
        nc.scalar.copy(gains[:], gains_ps[:, :, 64 : 64 + PASSES])

        x_codes = [sb([P, M], U32, f"x_codes{a}") for a in range(PASSES)]
        x_plane = [sb([P, M], U8, f"x_plane{a}") for a in range(PASSES)]
        x_grouped = [sb([P, M, 4], BF16, f"x_grouped{a}") for a in range(PASSES)]
        v_codes = {}

        def round_x(engine_copy, a, lo, hi):
            dst = x_grouped[a][:].rearrange("p (s z) t -> p s t z", z=4)
            src = x_raw[a][:].rearrange("p t (s z) -> p s t z", z=4)
            engine_copy(dst[:, lo:hi], src[:, lo:hi])

        def pick_table(a, b0, b1, name):
            codes = sb([P, 4, P * (b1 - b0)], U32, name)
            nc.vector.tensor_copy(
                codes[:].rearrange("p t (d l) -> p d t l", l=4),
                tab[a][:].bitcast(U32).indirect(offsets[:, 32 * b0 : 32 * b1]),
            )
            for b in range(b0, b1):
                v_codes[a, b] = codes[:, :, P * (b - b0) : P * (b - b0 + 1)]

        wd_operand = {}
        picked = {}

        def pick_wd(c, name):
            picked[c] = sb([P, S], BF16, name)
            nc.vector.tensor_copy(
                picked[c][:].rearrange("p (u d l e) -> p d u e l", u=2, l=4, e=2),
                wd[c][:].indirect(offsets[:]),
            )

        def turn_wd(c, n, grouped):
            words = picked[c][:].bitcast(F32)
            turned = bank(n, [P, 4, P], F32)
            for b in range(PASSES):
                for u in range(2):
                    start = P * (PASSES * u + b)
                    nc.tensor.transpose(turned[:, 2 * u + b, :], words[:, start : start + P], ident[:])
            nc.scalar.copy(
                grouped.bitcast(F32).rearrange("p (b n u) -> p b n u", b=2, u=2),
                turned[:].rearrange("p (u b) n -> p b n u", u=2),
            )

        def quantise_wd(values, codes, plane, keys):
            nc.vector.quantize_mx(out=codes.bitcast(FP8X4), scales=plane, in_=values)
            for n, key in enumerate(keys):
                columns = slice(P * n, P * (n + 1))
                wd_operand[key] = (codes[:, columns].bitcast(FP8X4), plane[:, columns])

        h_pairs = [sb([P, 4 * M], BF16, f"h_pairs{b}") for b in range(PASSES)]
        h_grouped = [sb([P, 4 * M], BF16, f"h_grouped{b}") for b in range(PASSES)]
        h_codes = [sb([P, M], U32, f"h_codes{b}") for b in range(PASSES)]
        h_plane = {}
        sig = [sb([P, 4, M], F32, f"sig{b}") for b in range(PASSES)]

        def encode(b, t):
            columns = slice(PASSES * P * t + P * b, PASSES * P * t + P * (b + 1))
            acc = bank((4 * b + t + 6) % 8, [P, M], F32)
            for a in range(PASSES):
                nc.tensor.matmul_mx(
                    out=acc[:], lhsT=v_codes[a, b][:, t, :].bitcast(FP8X4), lhsT_scale=v_plane[:].bitcast(U8)[4 * a : P, columns],
                    rhs=x_codes[a][:].bitcast(FP8X4), rhs_scale=x_plane[a][:], start=(a == 0), stop=(a == PASSES - 1),
                )
            nc.scalar.activation(sig[b][:, t, :], acc[:], ACT.Sigmoid)

        def apply_gain(b, t):
            pairs = h_pairs[b][:].rearrange("p (u m e) -> p u m e", u=2, e=2)
            nc.gpsimd.tensor_scalar(pairs[:, t // 2, :, t % 2], sig[b][:, t, :], gains[:, t, b : b + 1], 0.0, ALU.mult, ALU.add)

        def group_h(b):
            nc.scalar.copy(
                h_grouped[b][:].bitcast(F32).rearrange("p (m u) -> p m u", u=2),
                h_pairs[b][:].bitcast(F32).rearrange("p (u m) -> p m u", u=2),
            )

        def on_rows_plane(width, offset, name):
            return on_rows.tile([P, width], U8, name=name, align_bytes=ALIGN, offset=offset)

        def quantise_h(b, plane):
            h_plane[b] = plane
            nc.vector.quantize_mx(out=h_codes[b][:].bitcast(FP8X4), scales=plane[:], in_=h_grouped[b][:])

        sums = {}

        def add_shortcut(c):
            sums[c] = bank(SUM_BANK[c], [P, M], F32)
            for a in range(PASSES):
                nc.tensor.matmul_mx(
                    out=sums[c][:],
                    lhsT=w4[c // 4][:, a, :].bitcast(U8)[:, 2 * P * (c % 4) : 2 * P * (c % 4 + 1)].bitcast(FP4X4),
                    lhsT_scale=w4_plane[:, a, :].bitcast(U8)[:, P * c : P * (c + 1)],
                    rhs=x_codes[a][:].bitcast(FP8X4), rhs_scale=x_plane[a][:],
                    start=(a == 0), stop=False,
                )

        def add_decoded(c, b):
            nc.tensor.matmul_mx(
                out=sums[c][:], lhsT=wd_operand[c, b][0], lhsT_scale=wd_operand[c, b][1],
                rhs=h_codes[b][:].bitcast(FP8X4), rhs_scale=h_plane[b][:],
                start=False, stop=(b == PASSES - 1),
            )

        def close(c):
            for b in range(PASSES):
                add_decoded(c, b)

        def rate(c):
            parts = 2 if c == TILES - 1 else 1
            width = M // parts
            for part in range(parts):
                users = slice(width * part, width * (part + 1))
                result = rated[c // 4][:, c % 4, users]
                nc.scalar.activation(result, sums[c][:, users], ACT.Tanh, bias=bias[:, c : c + 1])
                queue = nc.scalar if part == 1 else nc.sync
                queue.dma_start(out[P * c : P * (c + 1), users], result)

        pick_table(0, 0, PASSES, "v_codes0")
        for a in range(PASSES):
            round_x(nc.scalar.copy, a, 0, X_ON_SCALAR[a])
            round_x(nc.vector.tensor_copy, a, X_ON_SCALAR[a], M // 4)
            nc.vector.quantize_mx(out=x_codes[a][:].bitcast(FP8X4), scales=x_plane[a][:], in_=x_grouped[a][:].rearrange("p m t -> p (m t)"))
        pick_table(1, 0, 1, "v_codes1a")
        pick_table(1, 1, 2, "v_codes1b")

        for c in range(4):
            pick_wd(c, f"picked{c}")
        for b in range(PASSES):
            for t in range(4):
                encode(b, t)
                apply_gain(b, t)

        grouped01 = sb([P, 2 * S], BF16, "grouped01")
        grouped2 = on_words.tile([P, S], BF16, name="grouped2", align_bytes=ALIGN, offset=0)
        grouped34 = sb([P, 2 * S], BF16, "grouped34")
        turn_wd(0, 6, grouped01[:, 0:S])
        group_h(0)
        turn_wd(1, 7, grouped01[:, S : 2 * S])
        turn_wd(2, 6, grouped2[:])

        bias = keep.tile([P, TILES], F32, name="bias")
        bias_ps = bank(5, [P, P], F32)
        nc.tensor.transpose(bias_ps[:], rows[:, PASS : PASS + P], ident[:])
        nc.scalar.copy(bias[:], bias_ps[:, 0:TILES])
        group_h(1)
        for c in range(4):
            add_shortcut(c)

        quantise_h(0, on_rows_plane(M, 0, "h_plane0"))
        quantise_wd(grouped01[:], sb([P, 4 * P], U32, "codes01")[:], on_rows_plane(4 * P, M, "plane01")[:], [(0, 0), (0, 1), (1, 0), (1, 1)])
        quantise_h(1, on_rows_plane(M, 2 * M, "h_plane1"))
        quantise_wd(grouped2[:], sb([P, 2 * P], U32, "codes2")[:], on_rows_plane(2 * P, 3 * M, "plane2")[:], [(2, 0), (2, 1)])
        pick_wd(4, "h_grouped1")
        pick_wd(5, "picked5")

        rated = [sb([P, 4, M], F32, f"x_raw{half}") for half in range(2)]
        for c in range(2):
            close(c)
            rate(c)
        close(2)
        turn_wd(3, 0, grouped34[:, 0:S])
        rate(2)
        turn_wd(4, 2, grouped34[:, S : 2 * S])
        for c in range(4, TILES):
            add_shortcut(c)

        pair_words = on_words.tile([P, 2 * T], BF16, name="pair_words", align_bytes=ALIGN, offset=0)

        def round_pair(engine_copy, i):
            engine_copy(
                pair_words[:, 2 * CHUNK_EDGES[i] : 2 * CHUNK_EDGES[i + 1]].rearrange("p (col e) -> p col e", e=2),
                pair_raw[i][:].rearrange("p e col -> p col e"),
            )

        round_pair(nc.gpsimd.tensor_copy, 0)
        round_pair(nc.gpsimd.tensor_copy, 1)
        round_pair(nc.gpsimd.tensor_copy, 2)
        round_pair(nc.scalar.copy, 3)
        round_pair(nc.scalar.copy, 4)

        quantise_wd(grouped34[:], sb([P, 4 * P], U32, "pair_raw2")[:], sb([P, 4 * P], U8, "plane34")[:], [(3, 0), (3, 1), (4, 0), (4, 1)])

        pair_picked = [sb([P, PASS], U32, f"pair_picked{b}") for b in range(PASSES)]
        for b in range(PASSES):
            nc.vector.tensor_copy(
                pair_picked[b][:].rearrange("p (t d l) -> p d t l", t=4, l=4),
                pair_words[:].bitcast(U32).indirect(offsets[:, 32 * b : 32 * (b + 1)]),
            )

        grouped5 = sb([P, S], BF16, "pair_raw4")
        turn_wd(5, 7, grouped5[:])
        for c in (3, 4):
            close(c)
            rate(c)

        pair_grouped = {(c, b): sb([P, P, 4], BF16, f"pair_grouped{c}_{b}") for c in PAIR for b in range(PASSES)}

        def quantise_pair(c, b):
            quantise_wd(
                pair_grouped[c, b][:].rearrange("p n t -> p (n t)"), sb([P, P], U32, f"pair_codes{c}_{b}")[:],
                sb([P, P], U8, f"pair_plane{c}_{b}")[:], [(c, b)],
            )

        first = bank(6, [P, 4, P], F32)
        for t in range(4):
            nc.tensor.transpose(first[:, t, :], pair_picked[0][:].bitcast(F32)[:, P * t : P * (t + 1)], ident[:])
        for e, c in enumerate(PAIR):
            nc.scalar.copy(pair_grouped[c, 0][:], first[:].bitcast(BF16).rearrange("p t (n e) -> p e n t", e=2)[:, e])
        halves = pair_picked[1][:].bitcast(BF16).rearrange("p (t j e) -> p t j e", t=4, e=2)
        second = {}
        for e, c in enumerate(PAIR):
            second[c] = bank((2, 7)[e], [P, 4, P], BF16)
            for t in range(4):
                nc.tensor.transpose(second[c][:, t, :], halves[:, t, :, e], ident_bf[:])

        quantise_pair(6, 0)
        quantise_wd(grouped5[:], sb([P, 2 * P], U32, "pair_picked0")[:], sb([P, 2 * P], U8, "plane5")[:], [(5, 0), (5, 1)])
        nc.vector.tensor_copy(pair_grouped[6, 1][:], second[6][:].rearrange("p t n -> p n t"))
        nc.scalar.copy(pair_grouped[7, 1][:], second[7][:].rearrange("p t n -> p n t"))
        quantise_pair(7, 0)
        quantise_pair(6, 1)
        quantise_pair(7, 1)
        add_decoded(6, 0)
        close(5)
        rate(5)
        add_decoded(7, 0)
        add_decoded(6, 1)
        rate(6)
        add_decoded(7, 1)
        rate(7)
